import numpy as np, ml_dtypes
CORES = [23,119,17,113]
N = 4
BF = ml_dtypes.bfloat16
def gentries(a):
    return np.ascontiguousarray(a.reshape(8, 16, -1).transpose(0, 2, 1)).reshape(8, -1)
def gtable(e):
    e = np.asarray(e); return np.ascontiguousarray(e.reshape(8, -1, 16).transpose(0, 2, 1)).reshape(128, -1).astype(np.int32)
M, L, T, H, A, R = 1792, 256, 3, 4096, 12, 1024
W = M + L * T; NONE = 4095
def hashes(w, a):
    u = np.matmul(w.transpose(0, 2, 1), a) & 4095
    return (((u[:, 0] * u[:, 1]) >> 5) + u[:, 1]) & (H - 1)
def some(rng, n, tops):
    return (rng.random((N, 8, 16, n)) * rng.choice(np.array(tops), (N, 8, 1, n))).astype(np.int64)
def places(rng, sizes):
    v = np.zeros((N, 8, L), np.int64)
    for r in range(N):
        for g in range(8):
            pool = rng.permutation(M)[:int(sizes[r, g])]; v[r, g] = pool[rng.integers(0, len(pool), L)]
    return v
def flat(a):
    return np.ascontiguousarray(a.reshape(N, 128, -1)).astype(np.float32).astype(BF)
def pack(X, B, E, x, v, w):
    return {"nodes": flat(X), "book": flat(B), "kids": np.ascontiguousarray(E.reshape(N, 128, M)).astype(np.int32), "cand": flat(x),
            "spot": np.stack([gtable(a) for a in v]), "wts": flat(w)}
def setup_inputs(rng):
    X = some(rng, M, (48, 96, 160, 256)); B = some(rng, H, (96, 160, 256)); x = some(rng, L, (96, 192, 256))
    k = np.minimum(rng.integers(0, 17, (N, 8, 16, M)), rng.integers(0, 17, (N, 8, 16, M)))
    fill = rng.choice(np.array([0.3, 0.6, 0.9, 1.0]), (N, 8, 1, M))
    E = 4096 * k + np.where(rng.random((N, 8, 16, M)) < fill, rng.integers(0, M, (N, 8, 16, M)), NONE)
    v = places(rng, rng.choice(np.array([8, 32, 128, M]), (N, 8)))
    return pack(X, B, E, x, v, rng.integers(0, 16, (N, 8, 16, 2)))
def setup_inputs_spread(rng):
    X = (np.exp2(8 * rng.random((N, 8, 1, M))) * rng.random((N, 8, 16, M))).astype(np.int64)
    x = (np.exp2(8 * rng.random((N, 8, 1, L))) * rng.random((N, 8, 16, L))).astype(np.int64); B = rng.integers(0, 256, (N, 8, 16, H))
    E = 4096 * rng.integers(0, 17, (N, 8, 16, M)) + np.where(rng.random((N, 8, 16, M)) < rng.random((N, 8, 1, M)), rng.integers(0, M, (N, 8, 16, M)), NONE)
    v = np.minimum((M * rng.random((N, 8, L)) ** 3).astype(np.int64), M - 1); w = np.minimum((16 * rng.random((N, 8, 16, 2)) ** 2).astype(np.int64), 15)
    return pack(X, B, E, x, v, w)
def setup_inputs_ends(rng):
    X = 255 * rng.integers(0, 2, (N, 8, 16, M)); B = 255 * rng.integers(0, 2, (N, 8, 16, H)); x = 255 * rng.integers(0, 2, (N, 8, 16, L))
    a = rng.random((N, 8, 1, L)); x = np.where(a < 0.15, 0, np.where(a < 0.4, 255, x))
    X[..., 0] = 0; X[..., M - 1] = 255
    w = 15 * rng.integers(0, 2, (N, 8, 16, 2)); w[:, ::2, 13] = 15; w[:, ::2, 14] = 1; w[:, ::2, 15] = 15; w[:, 7] = 15
    E = 69631 * rng.integers(0, 2, (N, 8, 16, M)); o = rng.random(E.shape)
    E = np.where(o < 0.35, rng.choice(np.array([65536, M - 1, M - 1 + 65536]), E.shape), E)
    E = np.where(o < 0.1, rng.integers(1, M - 16, E.shape) + 65536 * rng.integers(0, 2, E.shape), E)
    E[..., M - 1] = 69631 * rng.integers(0, 2, (N, 8, 16)); E[:, :, 15, M - 1] = M - 1 + 65536; low = rng.integers(0, 8, (N, 8))
    E[:, :, :15, M - 2] = 0; E[:, :, 15, M - 2] = 69631
    for j in range(1, T): E[:, :, :, M - 2 - j] = 65536 + M - 1 - j
    E[:, :, :15, M - 2 - T] = 69631; E[:, :, 15, M - 2 - T] = 0
    v = np.where(rng.random((N, 8, L)) < 0.68, (M - 1) * rng.integers(0, 2, (N, 8, L)), rng.integers(1, M - 16, (N, 8, L)))
    v[:, :, L - 1] = M - 1 - T; x[..., L - 1] = 255
    v[:, :, L - 17] = M - 1; x[..., L - 17] = 255
    v[:, :, L - 33] = M - 2 - T; x[..., L - 33] = 255
    v[:, :, L - 2] = M - 1; x[:, ::2, :, L - 2] = 0; x[:, ::2, 14:, L - 2] = 255; x[:, ::2, 13, L - 2] = 1
    s = rng.integers(0, 2, (N, 8)); s[:, 7] = 1; s[:, 1] = 0
    for r in range(N):
        h = hashes(w[r], np.full((8, 16, 1), 255))[:, 0]
        for g in range(8):
            B[r, g, :, h[g]] = 255 * s[r, g]; E[r, g, low[r, g], M - 1] = 65536
    return pack(X, B, E, x, v, w)
def setup_inputs_corners(rng):
    X = some(rng, M, (2, 64, 256)); B = some(rng, H, (2, 128, 256))
    kind = rng.integers(0, 9, (N, 8, 1, M)); kind[..., 5:6 + T] = 4
    own = np.arange(M); one = rng.integers(0, 16, (N, 8, 1, M)); line = np.arange(16)[:, None]
    c = rng.integers(0, M, (N, 8, 16, M))
    c = np.where(kind == 3, own, np.where(kind == 4, (own + 1) % M, np.where(kind == 5, 0, np.where(kind == 6, M - 1, c))))
    hide = (kind == 0) | ((kind == 2) & (line != one)) | ((kind == 7) & (line == one)) | ((kind == 8) & (rng.random(c.shape) < 0.5))
    m = rng.integers(0, 4, (N, 8, 1, M)); m = np.where(kind == 4, 1, m)
    k = np.where(m == 0, 0, np.where(m == 1, 16, np.where(m == 2, 15, rng.integers(0, 17, c.shape))))
    E = 4096 * k + np.where(hide, NONE, c)
    v = rng.integers(0, M, (N, 8, L)); w = rng.integers(0, 16, (N, 8, 16, 2))
    for r in range(N):
        o = rng.permutation(8); q = rng.permutation(M)
        v[r, o[0]] = 0; v[r, o[1]] = M - 1; v[r, o[2]] = q[:L]; v[r, o[3]] = rng.permutation(np.repeat(q[:L // 2], 2))
        v[r, o[4]] = rng.choice(np.array([5, 0, M - 1, 6]), L); v[r, o[5], ::2] = 5; v[r, o[5], L - 1] = 5
        b = rng.permutation(8)
        w[r, b[0]] = 0; w[r, b[1]] = 15; w[r, b[2], 1:] = 0; w[r, b[2], 0] = 15; w[r, b[3], :15] = 0; w[r, b[3], 15] = 15; w[r, b[4], :, 0] = 0; w[r, b[5], :, 1] = 0
    d = rng.integers(0, 4, (N, 8, 1, L)); x = some(rng, L, (64, 256))
    x = np.where(d == 0, 0, np.where(d == 1, 255, np.where(d == 2, np.take_along_axis(X, v[:, :, None, :], 3), x)))
    return pack(X, B, E, x, v, w)
def full(rng, X, B, E, x, v, r, late):
    n = T - 1 if late else 0; half = rng.permutation(8)
    for g in range(8):
        u = rng.permutation(M)[:L * T].reshape(T, L); e = E[r, g]; v[r, g] = u[0]
        for j in range(n): e[:, u[j]] = 65536 + u[j + 1][None, :]
        if half[g] < 4:
            e[:, u[n]] = NONE + 4096 * rng.integers(0, 17, (16, L))
        else:
            X[r, g] = rng.integers(0, 8, (16, M)); x[r, g] = rng.integers(8, 24, (16, L)); B[r, g] = rng.integers(24, 256, (16, H))
            e[:, u[n]] = rng.integers(0, M, (16, L)) + 4096 * rng.integers(0, 16, (16, L))
def setup_inputs_crowd(rng):
    X = some(rng, M, (16, 64, 128)); B = some(rng, H, (160, 256)); x = np.minimum(some(rng, L, (128, 256)) + rng.integers(0, 64, (N, 8, 1, L)), 255)
    k = rng.integers(0, 17, (N, 8, 16, M)) * (rng.random((N, 8, 16, M)) < 0.3); fill = rng.choice(np.array([0.5, 1.0]), (N, 8, 1, M))
    E = 4096 * k + np.where(rng.random((N, 8, 16, M)) < fill, rng.integers(0, M, (N, 8, 16, M)), NONE)
    v = places(rng, rng.choice(np.array([1, 2, 3, 16]), (N, 8))); v[:, 0] = 0; v[:, 7] = M - 1
    o = rng.permutation(N); full(rng, X, B, E, x, v, int(o[0]), False); full(rng, X, B, E, x, v, int(o[1]), True)
    return pack(X, B, E, x, v, rng.integers(0, 16, (N, 8, 16, 2)))
def setup_inputs_ties(rng):
    X = 100 + rng.integers(0, 3, (N, 8, 16, M)); x = 100 + rng.integers(0, 3, (N, 8, 16, L)); B = rng.integers(0, 3, (N, 8, 16, H))
    c = rng.integers(0, M, (N, 8, 16, M)); c[:, ::2, 8:] = c[:, ::2, :8]
    E = 4096 * rng.integers(8, 15, c.shape) + np.where(rng.random(c.shape) < 0.8, c, NONE)
    v = places(rng, rng.choice(np.array([4, 16, 64, M]), (N, 8)))
    return pack(X, B, E, x, v, rng.integers(0, 16, (N, 8, 16, 2)))
def check_inputs(d):
    bad = []
    for k, lo, hi in (("nodes", 0, 255), ("book", 0, 255), ("kids", 0, 69631), ("cand", 0, 255), ("spot", 0, M - 1), ("wts", 0, 15)):
        a = np.asarray(d[k]).astype(np.float32)
        if not (np.min(a) >= lo and np.max(a) <= hi and np.all(a == np.floor(a))): bad.append("range of " + k)
    c = np.asarray(d["kids"]).astype(np.int64) & 4095
    if np.any((c >= M) & (c != NONE)): bad.append("children in kids")
    return bad
def reference(nodes, book, kids, cand, spot, wts):
    X = np.zeros((N, 8, 16, W), np.int64); X[..., :M] = nodes.astype(np.float32).astype(np.int64).reshape(N, 8, 16, M)
    E = np.full((N, 8, 16, W), NONE, np.int64); E[..., :M] = kids.astype(np.int64).reshape(N, 8, 16, M)
    B = book.astype(np.float32).astype(np.int64).reshape(N, 8, 16, H); w = wts.astype(np.float32).astype(np.int64).reshape(N, 8, 16, 2)
    xs = cand.astype(np.float32).astype(np.int64).reshape(N, 8, 16, L).copy(); vs = np.stack([gentries(a) for a in spot]).astype(np.int64)
    lane = np.arange(L); p = lane & 15; gr = np.arange(8)[:, None]
    for t in range(T):
        for r in range(N):
            x, v, q = xs[r], vs[r], (r + 1 + t % (N - 1)) % N
            ev = np.take_along_axis(E[r], v[:, None, :], 2)
            c = ev & 4095; thr = ev >> 12; filled = c != NONE
            xc = np.take_along_axis(X[r], np.where(filled, c, 0).reshape(8, 1, 16 * L), 2).reshape(8, 16, 16, L)
            dif = np.abs(x[:, :, None, :] - xc); fd = dif.reshape(8, 16, 16 * L)
            bc = np.take_along_axis(B[r], hashes(w[r], fd)[:, None, :], 2)
            s = np.add.reduce((bc >= fd).astype(np.int64), axis=1).reshape(8, 16, L)
            over = np.add.reduce((x[:, :, None, :] >= xc).astype(np.int64), axis=1)
            cap = filled & (over >= A) & (s > thr); stay = filled & ~cap
            go = stay[:, p, lane]
            best = np.argmax(np.where(stay, s, -1), axis=1)
            down = np.take_along_axis(c, best[:, None, :], 1)[:, 0]
            first = np.full((8, W), L); np.minimum.at(first, (gr, v), np.where(go, L, lane[None, :]))
            win = ~go & (first[gr, v] == lane[None, :]); wb = win[:, None, :]
            z = np.abs(np.take_along_axis(X[r], v[:, None, :], 2) - x)
            y = np.take_along_axis(B[q], hashes(w[q], z)[:, None, :], 2)
            n = M + L * t + lane
            X[r][:, :, M + L * t:M + L * t + L] = np.where(wb, x, 0)
            E[r][:, :, M + L * t:M + L * t + L] = np.where(wb & cap, c + 4096 * s, NONE)
            col = np.where(cap, NONE, ev); col[:, p, lane] = n[None, :] + 4096 * np.max(np.where(cap, s, 0), axis=1)
            gi, li = np.nonzero(win)
            E[r][gi, :, v[gi, li]] = col[gi, :, li]
            x = np.where(wb, np.abs(x - y), x)
            back = np.add.reduce(w[r][:, :, 0:1] * x, axis=1) & (R - 1)
            xs[r] = x; vs[r] = np.where(win, back, np.where(go, down, v))
    return {"ykids": E.reshape(N, 128, W).astype(np.float32), "ynodes": np.ascontiguousarray(X[..., M:]).reshape(N, 128, L * T).astype(np.float32).astype(BF),
            "ycand": xs.reshape(N, 128, L).astype(np.float32).astype(BF), "yspot": np.stack([gtable(a) for a in vs]).astype(np.float32)}

@@ -1,0 +1,592 @@
+from concourse.mybir import dt, AluOpType as A, ActivationFunctionType as F
+
+M, L, STEPS, H = 1792, 256, 3, 4096
+W = M + L * STEPS
+NENG = 8
+BIG = float(2 ** 23)
+
+SB = {
+    "XT": (4096, "bfloat16"), "BK": (4096, "bfloat16"), "ET": (2944, "float32"), "KI": (M, "int32"), "IDX": (2304, "float32"),
+    "ONE": (1024, "bfloat16"), "ZER": (128, "bfloat16"), "IDb": (128, "bfloat16"), "NIDb": (128, "bfloat16"), "IDf": (128, "float32"), "NIDf": (128, "float32"),
+    "N20": (128, "bfloat16"), "N22": (128, "bfloat16"), "I4K": (128, "bfloat16"), "G8t": (8, "bfloat16"), "G8": (8, "bfloat16"), "G8f": (8, "float32"),
+    "GW": (16, "float32"), "W1": (2048, "bfloat16"), "W2": (2048, "bfloat16"), "GS": (24, "bfloat16"), "GO": (8, "bfloat16"), "GO2": (8, "bfloat16"),
+    "PICK": (1024, "bfloat16"), "PK8": (8, "bfloat16"), "TRI": (128, "bfloat16"), "pms": (128, "bfloat16"), "pm": (256, "bfloat16"), "npm": (256, "bfloat16"),
+    "pmn": (256, "float32"), "rmf": (128, "float32"), "rmb": (128, "bfloat16"), "CR": (512, "bfloat16"), "REP": (2048, "bfloat16"), "trash": (16, "float32"),
+    "II": (256, "bfloat16"), "pmI": (256, "bfloat16"), "cI0": (128, "bfloat16"), "cI1": (128, "bfloat16"), "cI2": (128, "bfloat16"),
+    "wt": (2, "bfloat16"), "sp": (16, "int32"), "x0": (256, "bfloat16"), "x1": (256, "bfloat16"), "lv0": (16, "float32"), "lv1": (16, "float32"), "lvu": (16, "uint16"),
+    "Ei": (256, "int32"), "Ci": (256, "int32"), "CL": (256, "uint16"), "Ff": (256, "float32"), "em": (256, "bfloat16"), "Cm": (256, "float16"), "Rm": (256, "float32"),
+    "vA": (256, "float16"), "vcol": (16, "float32"), "xT": (256, "bfloat16"), "d0": (256, "bfloat16"),
+    "XG": (4096, "bfloat16"), "DD": (4096, "bfloat16"), "SG": (4096, "bfloat16"), "CMP": (4096, "bfloat16"), "HL": (256, "uint16"),
+    "hu0": (256, "int32"), "hp0": (128, "int32"), "hu1": (256, "int32"), "hp1": (128, "int32"), "ru": (32, "int32"), "rp": (16, "int32"), "rl": (16, "uint16"), "MQ": (3072, "bfloat16"), "MD": (3072, "bfloat16"),
+    "tA": (256, "float32"), "cap": (256, "bfloat16"), "nc": (256, "bfloat16"), "key": (256, "float32"), "wm": (256, "bfloat16"), "w1s": (256, "bfloat16"), "wb": (256, "bfloat16"),
+    "k1": (256, "float32"), "k2": (256, "float32"), "dpm": (256, "float32"), "NE": (256, "float32"), "n1": (256, "float32"), "n2": (256, "float32"), "Si": (256, "int32"), "pS": (256, "bfloat16"),
+    "r2": (256, "float32"), "winb": (256, "bfloat16"), "winm": (256, "bfloat16"), "newc": (256, "float32"), "NEs": (256, "float32"), "NEw": (256, "float32"),
+    "rr": (256, "bfloat16"), "rx": (256, "bfloat16"), "ws": (32, "float32"), "of": (16, "float32"), "ofu": (16, "uint16"), "vt": (16, "float32"),
+    "dn": (16, "int32"), "bk2": (16, "float32"), "b1": (16, "float32"), "b2": (16, "float32"), "bi": (16, "int32"), "bk": (16, "int32"),
+}
+for _t in range(STEPS):
+    for _n in ("z", "zl", "yr", "yl"):
+        SB[_n + str(_t)] = (256, "bfloat16")
+PS = ["dp0", "dp1", "up", "BH0", "BH1", "ov", "m0", "m1"]
+SCRATCH = {k: ("sbuf", [128, n], d) for k, (n, d) in SB.items()}
+for _n in PS:
+    SCRATCH[_n] = ("psum", [128, 512], "float32")
+NDMA = 10
+SEMAPHORES = ["qv", "qs", "qt", "qg"] + ["D%d" % i for i in range(NDMA)] + [n + str(t) for t in range(STEPS) for n in ("zs", "za", "ys", "ya")]
+
+
+ORDER = {}
+CYC = 0.83e-3
+PECYC = 0.45e-3
+WAKE = 0.18
+CHUNKS = ((0, 2), (2, 4), (4, 6), (6, 8))
+G1V = ()
+SGV = (0,)
+MQV = tuple(range(8))
+
+
+def overlap(a, b):
+    return a[1] < b[2] and b[1] < a[2] and not (a[3] == b[3] and a[3] > 1 and (a[1] - b[1]) % a[3])
+
+
+def schedule(nodes, psum):
+    wake = WAKE
+    n = len(nodes)
+    preds = [[] for _ in range(n)]
+    hist = {}
+    for i in range(n):
+        kind, q, fn, reads, writes, cost, sem = nodes[i]
+        seen = {}
+        for rs, w in ((reads, False), (writes, True)):
+            for r in rs:
+                bank = r[0] in psum
+                for (j, rj, wj) in hist.get(r[0], ()):
+                    ov = overlap(r, rj)
+                    same = nodes[j][1] == q and kind == "c" and nodes[j][0] == "c"
+                    if bank and (q == "t" or not same):
+                        full = not same or (ov and wj and q != "t")
+                    elif ov and (w or wj):
+                        full = not same or wj
+                    else:
+                        continue
+                    seen[j] = seen.get(j, False) or full
+        preds[i] = list(seen.items())
+        for rs, w in ((reads, False), (writes, True)):
+            for r in rs:
+                h = hist.get(r[0], [])
+                if w and abs(r[3]) == 1 and r[4] == 128 and r[0] not in psum:
+                    h = [e for e in h if not (r[1] <= e[1][1] and e[1][2] <= r[2])]
+                if r[0] in psum and len(h) > 40:
+                    h = h[-40:]
+                hist[r[0]] = h + [(i, r, w)]
+    succ = [[] for _ in range(n)]
+    for i in range(n):
+        for j, full in preds[i]:
+            succ[j].append((i, full))
+    prio = [0.0] * n
+    for i in range(n - 1, -1, -1):
+        c = nodes[i][5]
+        prio[i] = max([c] + [prio[k] + (c + wake if full else 0.0) for k, full in succ[i]])
+        if nodes[i][0] == "d":
+            prio[i] += 1e7 - 1e3 * i
+    left = [len(p) for p in preds]
+    ready = {}
+    free = {}
+    est = [0.0] * n
+    for i in range(n):
+        if not left[i]:
+            ready.setdefault(nodes[i][1], []).append(i)
+    order = []
+    while len(order) < n:
+        best = None
+        for q, r in ready.items():
+            if r:
+                t = min(max(est[i], free.get(q, 0.0)) for i in r)
+                if best is None or t < best[0]:
+                    best = (t, q)
+        t, q = best
+        i = max((k for k in ready[q] if max(est[k], free.get(q, 0.0)) <= t + 0.02), key=lambda k: (prio[k], -k))
+        ready[q].remove(i)
+        st = max(est[i], free.get(q, 0.0))
+        end = st + nodes[i][5]
+        free[q] = end if nodes[i][0] == "c" else st + (0.1 if nodes[i][0] == "d" else 1.0)
+        order.append(i)
+        for k, full in succ[i]:
+            est[k] = max(est[k], end + wake if full else st)
+            left[k] -= 1
+            if not left[k]:
+                ready.setdefault(nodes[k][1], []).append(k)
+    return order
+
+
+def rank_program(g, core, T, topo):
+    rank = T.rank_of(core)
+    if rank is None:
+        return
+    queues = {"v": g.vector, "s": g.scalar, "t": g.tensor, "g": g, "y": g.sync}
+    known = {q: {} for q in queues}
+    count = {}
+    clock = {}
+    hist = {}
+
+    def R(name, lo=0, hi=None, step=1, p1=128):
+        return (name, lo, SB[name][0] if hi is None and name in SB else (512 if hi is None else hi), step, p1)
+
+    def P(name, win, off):
+        return ("ind", win, off)
+
+    def ap(r):
+        if r[0] == "ind":
+            return ap(r[1]).indirect(ap(r[2]))
+        name, lo, hi, step, p1 = r
+        if step == -1:
+            return T[name][:, hi - 1:(lo - 1 if lo > 0 else None):-1]
+        if p1 != 128:
+            return T[name][0:p1, lo:hi]
+        return T[name][:, lo:hi] if step == 1 else T[name][:, lo:hi:step]
+
+    def flat(rs):
+        out = []
+        for r in rs:
+            out += [r[1], r[2]] if r[0] == "ind" else [r]
+        return out
+
+    def need(q, ev):
+        sem, val = ev
+        k = known[q]
+        if k.get(sem, 0) >= val:
+            return
+        queues[q].wait_ge(T.sem[sem], val)
+        k[sem] = val
+        for s2, v2 in clock.get(ev, {}).items():
+            if k.get(s2, 0) < v2:
+                k[s2] = v2
+
+    def deps(q, me, reads, writes):
+        evs = {}
+        for rs, w in ((reads, False), (writes, True)):
+            for r in rs:
+                bank = r[0] in PS
+                for (who, ev, lo, hi, wasw, step) in hist.get(r[0], ()):
+                    over = lo < r[2] and r[1] < hi and not (step == r[3] and step > 1 and (lo - r[1]) % step)
+                    if who == me:
+                        if not wasw or not over or (w and me == "t"):
+                            continue
+                    elif not (bank or (over and (w or wasw))):
+                        continue
+                    if evs.get(ev[0], 0) < ev[1]:
+                        evs[ev[0]] = ev[1]
+        for sem in sorted(evs):
+            need(q, (sem, evs[sem]))
+
+    def note(me, ev, reads, writes):
+        for rs, w in ((reads, False), (writes, True)):
+            for r in rs:
+                old = hist.get(r[0], [])
+                if w and abs(r[3]) == 1 and r[4] == 128:
+                    old = [e for e in old if not (r[1] <= e[2] and e[3] <= r[2])]
+                else:
+                    old = [e for e in old if not (e[0] == me and e[2:] == (r[1], r[2], w, abs(r[3])))]
+                hist[r[0]] = old + [(me, ev, r[1], r[2], w, abs(r[3]))]
+
+    nodes = []
+
+    def emit(q, fn, reads, writes, cost):
+        nodes.append(("c", q, fn, flat(reads), flat(writes), cost, None))
+
+    nd = [0]
+
+    def dma(q, out, in_, reads, writes):
+        sem = "D%d" % nd[0]
+        nd[0] += 1
+        size = 128 * (writes or reads)[0][2] * 4
+        nodes.append(("d", q, lambda: queues[q].dma_start(out, in_), reads, writes, 2.0 + size / 2.0e5, sem))
+
+    def send(src, dst, peer, lsem, rsem):
+        to = T.cores[peer]
+        rid, pid = topo.addr(to)[:2]
+        engs = topo.engines(core, to)[:NENG]
+
+        def fn():
+            g.remote_dma(T[dst][:], T[src][:], T.sem[rsem], T.sem[lsem], pid, rid, sum(1 << e for e in engs))
+        nodes.append(("r", "g", fn, [R(src)], [R(dst)], 5.0, (lsem, len(engs))))
+
+    def finish():
+        order = ORDER.get("order")
+        if order is None or len(order) != len(nodes):
+            order = schedule(nodes, PS)
+            ORDER["order"] = order
+        for i in order:
+            kind, q, fn, reads, writes, cost, sem = nodes[i]
+            if kind == "c":
+                deps(q, q, reads, writes)
+                name = "q" + q
+                count[name] = count.get(name, 0) + 1
+                fn().then_inc(T.sem[name], 1)
+                ev, me = (name, count[name]), q
+            elif kind == "d":
+                deps(q, sem, reads, writes)
+                fn().then_inc(T.sem[sem], 16)
+                count[sem] = 16
+                ev, me = (sem, 16), sem
+            else:
+                deps("g", sem[0], reads, [])
+                fn()
+                count[sem[0]] = sem[1]
+                ev, me, writes = sem, sem[0], []
+            clock[ev] = dict(known[q])
+            note(me, ev, reads, writes)
+        for sem in sorted(count):
+            need("g", (sem, count[sem]))
+
+    for t in range(STEPS):
+        for buf, sem in (("zl", "za"), ("yl", "ya")):
+            hist[buf + str(t)] = [("remote", (sem + str(t), NENG), 0, 256, True, 1)]
+            count[sem + str(t)] = NENG
+
+    def width(r):
+        return 16 * width(r[2]) if r[0] == "ind" else -((r[1] - r[2]) // abs(r[3]))
+
+    def dtype_of(r):
+        return "float32" if r[0] in PS else SB[r[0]][1]
+
+    def vcost(out, ins, kind):
+        if out[0] == "ind":
+            return 0.05 + 4.0 * width(out[2]) * 16 * CYC
+        n = width(out)
+        if any(r[0] == "ind" for r in ins):
+            return 0.05 + 1.56 * n * CYC
+        if kind == 2:
+            c = n if any(r[0] in PS for r in ins) else 2 * n
+        else:
+            c = n
+            if kind == 1 and all(dtype_of(r) not in ("float32", "int32") for r in [out] + ins if width(r) > 1):
+                c = n / 2
+        return max(64, c) * CYC
+
+    V, S, TE = g.vector, g.scalar, g.tensor
+
+    def tt(out, a, b, op):
+        emit("v", lambda: V.tensor_tensor(ap(out), ap(a), ap(b), op), [a, b], [out], vcost(out, [a, b], 2))
+
+    def ts(out, a, s1, op0, s2=None, op1=None):
+        rs = [a] + [s for s in (s1, s2) if not isinstance(s, (int, float)) and s is not None]
+        c1 = s1 if isinstance(s1, (int, float)) else ap(s1)
+        if op1 is None:
+            emit("v", lambda: V.tensor_scalar(ap(out), ap(a), c1, None, op0), rs, [out], vcost(out, [a], 1))
+        else:
+            c2 = s2 if isinstance(s2, (int, float)) else ap(s2)
+            emit("v", lambda: V.tensor_scalar(ap(out), ap(a), c1, c2, op0, op1), rs, [out], vcost(out, [a], 1))
+
+    def cp(out, a):
+        emit("v", lambda: V.tensor_copy(ap(out), ap(a)), [a], [out], vcost(out, [a], 1))
+
+    def fill(out, c):
+        emit("v", lambda: V.memset(ap(out), c), [], [out], vcost(out, [], 1))
+
+    def scan(out, d0, d1):
+        emit("v", lambda: V.tensor_tensor_scan(ap(out), ap(d0), ap(d1), 0.0, A.mult, A.max), [d0, d1], [out], vcost(out, [d0, d1], 1))
+
+    def act(out, a, f, bias=0.0, scale=1.0):
+        col = not isinstance(bias, (int, float))
+        emit("s", lambda: S.activation(ap(out), ap(a), f, bias=ap(bias) if col else bias, scale=scale), [a] + ([bias] if col else []), [out], vcost(out, [a], 0))
+
+    def mm(out, lhsT, rhs, start=True, stop=True):
+        cost = max(64, width(rhs)) * (4 if dtype_of(lhsT) == "float32" else 1) * PECYC
+        emit("t", lambda: TE.matmul(ap(out), ap(lhsT), ap(rhs), start, stop), [lhsT, rhs], [out], cost)
+
+    def aff(out, a, pat, op, fl, base, cm):
+        emit("g", lambda: g.affine_select(ap(out), ap(a), pat, op, fl, base, cm), [a], [out], 0.17 + 2 * width(out) * CYC)
+
+    def iota(out, pat, base, cm):
+        emit("g", lambda: g.iota(ap(out), pat, base, cm, allow_small_or_imprecise_dtypes=True), [], [out], 0.13 + 2 * width(out) * CYC)
+
+    dma("y", T.sp[:], T.spot[:], [], [R("sp")])
+    dma("y", T.KI[:], T.kids[:], [], [R("KI")])
+    dma("s", T.wt[:], T.wts[:], [], [R("wt")])
+    dma("s", T.x0[:], T.cand[:], [], [R("x0")])
+    dma("s", T.XT[:, 0:M], T.nodes[:], [], [R("XT", 0, M)])
+    dma("y", T.BK[:], T.book[:], [], [R("BK")])
+
+    fill(R("ONE"), 1.0)
+    fill(R("ZER"), 0.0)
+    aff(R("IDb"), R("ONE", 0, 128), [[-1, 128]], A.is_equal, 0.0, 0, 1)
+    aff(R("G8t"), R("ONE", 0, 8), [[-16, 8]], A.is_ge, 0.0, 0, 1)
+    aff(R("G8"), R("G8t"), [[16, 8]], A.is_ge, 0.0, 15, -1)
+    fill(R("W1"), 0.0)
+    fill(R("W2"), 0.0)
+    fill(R("XT", M, 4096), 0.0)
+    ts(R("NIDb"), R("IDb"), -1.0, A.mult)
+    for m in range(16):
+        cp(R("REP", m, 2048, 16), R("IDb"))
+    cp(R("G8f"), R("G8"))
+    cp(R("lvu"), R("sp"))
+    cp(R("lv0"), R("sp"))
+    for j, w in ((0, "W1"), (1, "W2")):
+        ts(R("GW", 8 * j, 8 * j + 8), R("G8f"), R("wt", j, j + 1), A.mult)
+        for q in range(8):
+            ts(R(w, 16 * q, 16 * q + 129 * 15 + 1, 129), R("ONE", 0, 16), R("GW", 8 * j + q, 8 * j + q + 1), A.mult)
+    aff(R("PK8"), R("ONE", 0, 8), [[-16, 8]], A.is_equal, 0.0, 0, 1)
+    aff(R("TRI"), R("ZER"), [[1, 128]], A.is_gt, -8192.0, 0, -1)
+    iota(R("IDX"), [[1, 2304]], -1280, 0)
+    fill(R("CR"), 0.0)
+    fill(R("CR", 128, 256, 1, 2), 2048.0)
+    fill(R("CR", 256, 384, 1, 2), 1.0)
+    fill(R("CR", 256, 384, 1, 1), -2048.0)
+    iota(R("CR", 128, 256, 1, 1), [[0, 8], [-4096, 16]], 65536, 0)
+    iota(R("II"), [[1, 256]], 1, 0)
+    fill(R("CR", 0, 128, 1, 2), 1.0)
+    fill(R("CR", 0, 128, 1, 1), -4096.0)
+    iota(R("trash"), [[16, 16]], W, 1)
+
+    def more_constants():
+        cp(R("IDf"), R("IDb"))
+        ts(R("NIDf"), R("IDb"), -1.0, A.mult)
+        ts(R("N20"), R("IDb"), -float(2 ** 20), A.mult)
+        ts(R("N22"), R("IDb"), -float(2 ** 22), A.mult)
+        ts(R("I4K"), R("IDb"), 4096.0, A.mult)
+        for z, c in ((0, 4096.0), (8, 65536.0), (16, 4096.0)):
+            ts(R("GS", z, z + 8), R("G8"), c, A.mult)
+        ts(R("GO"), R("G8"), -float(2 ** 19), A.mult)
+        if SGV:
+            ts(R("GO2"), R("G8"), -float(2 ** 20), A.mult)
+        tt(R("pms", 0, 64), R("IDb", 0, 64), R("IDb", 64, 128), A.add)
+        tt(R("pms", 64, 96), R("pms", 0, 32), R("pms", 32, 64), A.add)
+        tt(R("pm", 0, 16), R("pms", 64, 80), R("pms", 80, 96), A.add)
+        for n in (16, 32, 64, 128):
+            cp(R("pm", n, 2 * n), R("pm", 0, n))
+        ts(R("npm"), R("pm"), -1.0, A.mult, 1.0, A.add)
+
+    def even_more():
+        ts(R("pmn"), R("pm"), BIG + 1.0, A.mult, -BIG, A.add)
+        fill(R("rmf"), 1.0)
+        fill(R("rmb"), 1.0)
+        ts(R("rmf", 0, 128, 16), R("ONE", 0, 8), 0.0, A.mult)
+        ts(R("rmb", 0, 128, 16), R("ONE", 0, 8), 0.0, A.mult)
+        tt(R("pmI"), R("pm"), R("II"), A.mult)
+        for u in range(STEPS):
+            ts(R("cI%d" % u), R("IDb"), -2304.0 + 256.0 * u, A.mult)
+        cp(R("ET", 0, M), R("KI"))
+        fill(R("ET", M, W), 4095.0)
+
+    def hash_ops(u, n, ui, p, out):
+        cp(R(ui, 0, 2 * n), u)
+        ts(R(ui, 0, 2 * n), R(ui, 0, 2 * n), 4095, A.bitwise_and)
+        tt(R(p, 0, n), R(ui, 0, n), R(ui, n, 2 * n), A.mult)
+        ts(R(p, 0, n), R(p, 0, n), 5, A.arith_shift_right)
+        tt(R(p, 0, n), R(p, 0, n), R(ui, n, 2 * n), A.add)
+        ts(R(p, 0, n), R(p, 0, n), 4095, A.bitwise_and)
+        cp(out, R(p, 0, n))
+
+    for t in range(STEPS):
+        x, xn = ("x0", "x1") if t % 2 == 0 else ("x1", "x0")
+        lv, lvn = ("lv0", "lv1") if t % 2 == 0 else ("lv1", "lv0")
+        st = str(t)
+        last = t == STEPS - 1
+        tab = ("KI", M) if t == 0 else ("ET", M + 256 * (t - 1))
+
+        def G1(b0, b1):
+            if b0 in G1V:
+                cp(R("XG", 512 * b0, 512 * b1), P("ind", R("XT"), R("CL", 32 * b0, 32 * b1)))
+            else:
+                act(R("XG", 512 * b0, 512 * b1), P("ind", R("XT"), R("CL", 32 * b0, 32 * b1)), F.Copy)
+
+        def sub(j):
+            h, b = j // 4, "dp%d" % (j % 2)
+            mm(R(b), R("NIDb"), R("XG", 512 * j, 512 * j + 512), True, False)
+            mm(R(b), R("xT", 128 * h, 128 * h + 128), R("REP", 512 * (j % 4), 512 * (j % 4) + 512), False, True)
+            act(R("DD", 512 * j, 512 * j + 512), R(b), F.Abs)
+            if h in SGV:
+                ts(R("SG", 512 * j, 512 * j + 512), R(b), 0.0, A.is_ge)
+            else:
+                act(R("SG", 512 * j, 512 * j + 512), R(b), F.Sign, 0.5)
+
+        def hashes(b0, b1, c):
+            n = 32 * (b1 - b0)
+            for u, w in ((0, "W1"), (n, "W2")):
+                for k in range(16):
+                    mm(R("up", u, u + n), R(w, 128 * k, 128 * k + 128), R("DD", 512 * b0 + k, 512 * b1, 16), k == 0, k == 15)
+            hash_ops(R("up", 0, 2 * n), n, "hu%d" % (c % 2), "hp%d" % (c % 2), R("HL", 32 * b0, 32 * b1))
+            tt(R("CMP", 512 * b0, 512 * b1), P("ind", R("BK"), R("HL", 32 * b0, 32 * b1)), R("DD", 512 * b0, 512 * b1), A.is_ge)
+
+        def over(h):
+            for k in range(16):
+                mm(R("ov", 128 * h + k, 128 * h + 128, 16), R("SG", 2048 * h + k, 2048 * h + 2048, 16), R("GO2" if h in SGV else "GO"))
+            act(R("tA", 128 * h, 128 * h + 128), R("ov", 128 * h, 128 * h + 128), F.Relu, 11.5 * 2 ** 20 - (0.0 if h in SGV else BIG) - 4095.0)
+
+        def scount(h):
+            for k in range(16):
+                mm(R("BH%d" % h, k, 384, 16), R("CMP", 2048 * h + k, 2048 * h + 2048, 16), R("GS"), False, k == 15)
+
+        def bh_open(h):
+            b = "BH%d" % h
+            hs = (128 * h, 128 * h + 128)
+            mm(R(b), R("ONE", 0, 128), R("CR"), True, False)
+            mm(R(b, 0, 128), R("Ff", *hs), R("NIDf"), False, False)
+            mm(R(b, 0, 128), R("em", *hs), R("N20"), False, False)
+            mm(R(b, 128, 256), R("Cm", *hs), R("IDb"), False, False)
+            mm(R(b, 128, 256), R("em", *hs), R("N22"), False, False)
+            mm(R(b, 256, 384), R("Cm", *hs), R("IDb"), False, False)
+            mm(R(b, 384, 512), R("Rm", *hs), R("IDf"), False, False)
+
+        def same(q):
+            b = "m%d" % (q % 2)
+            pk = R("PICK", 128 * q, 128 * q + 128)
+            mm(R(b, 0, 128), R("IDb"), R("TRI"), True, False)
+            mm(R(b, 0, 128), pk, R("vA", 0, 128), False, True)
+            mm(R(b, 128, 256), pk, R("vA", 128, 256))
+            mm(R(b, 256, 384), R("IDb"), R("TRI"), True, False)
+            mm(R(b, 256, 384), pk, R("vA", 128, 256), False, True)
+            o = 384 * q
+            if q in MQV:
+                ts(R("MQ", o, o + 256), R(b, 0, 256), R("vcol", q, q + 1), A.add, 0.0, A.is_equal)
+                ts(R("MQ", o + 256, o + 384), R(b, 256, 384), R("vcol", 8 + q, 9 + q), A.add, 0.0, A.is_equal)
+                return
+            act(R("MD", o, o + 256), R(b, 0, 256), F.Abs, R("vcol", q, q + 1))
+            act(R("MD", o + 256, o + 384), R(b, 256, 384), F.Abs, R("vcol", 8 + q, 9 + q))
+            if q % 2:
+                ts(R("MQ", o - 384, o + 384), R("MD", o - 384, o + 384), 0.0, A.is_equal)
+
+        def decide(h):
+            b = "BH%d" % h
+            lo, hi = 128 * h, 128 * h + 128
+
+            def r(n, step=1):
+                return R(n, lo, hi, step)
+            tt(r("cap"), R(b, 0, 128), r("tA"), A.is_gt)
+            tt(r("nc"), R(b, 0, 128), r("tA"), A.is_le)
+            tt(R(b, 128, 256), r("nc"), R(b, 128, 256), A.mult)
+            tt(r("wm"), r("pmn"), R(b, 128, 256), A.is_gt)
+            scan(r("w1s"), R("rmb"), r("wm"))
+            scan(r("wb", -1), R("rmb"), r("w1s", -1))
+
+        def decide2(h):
+            b = "BH%d" % h
+            lo, hi = 128 * h, 128 * h + 128
+
+            def r(n, step=1):
+                return R(n, lo, hi, step)
+            tt(r("r2"), r("nc"), R(b, 384, 512), A.mult)
+            tt(r("NE"), r("cap"), R(b, 256, 384), A.mult)
+            scan(r("n1"), R("rmf"), r("NE"))
+            scan(r("n2", -1), R("rmf"), r("n1", -1))
+            ts(r("Si"), r("n2"), 2.0 ** -12, A.mult, 0.5 - 2.0 ** -13, A.add)
+            tt(r("pS"), r("Si"), r("pm"), A.mult)
+            scan(r("k1"), R("rmf"), R(b, 128, 256))
+            scan(R(b, 128, 256, -1), R("rmf"), r("k1", -1))
+            tt(r("dpm"), r("pm"), R(b, 128, 256), A.mult)
+
+        for a, b in ((0, 64), (64, 256)):
+            cp(R("Ei", a, b), P("ind", R(tab[0], 0, tab[1]), R("lvu", a // 16, b // 16)))
+            ts(R("Ci", a, b), R("Ei", a, b), 4095, A.bitwise_and)
+            cp(R("CL", a, b), R("Ci", a, b))
+        tt(R("d0"), P("ind", R("XT"), R("lvu")), R(x), A.subtract)
+        for h in range(2):
+            mm(R("m0", 128 * h, 128 * h + 128), R(x, 128 * h, 128 * h + 128), R("IDb"))
+        act(R("xT"), R("m0", 0, 256), F.Copy)
+        act(R("z" + st), R("d0"), F.Abs)
+        send("z" + st, "zl" + st, (rank + 1 + t) % 4, "zs" + st, "za" + st)
+        for b0, b1 in CHUNKS:
+            G1(b0, b1)
+        if t == 0:
+            aff(R("PICK"), R("ONE"), [[-16, 8], [0, 128]], A.is_equal, 0.0, 0, 1)
+            more_constants()
+        ts(R("Ff"), R("Ei"), -4095.0, A.add)
+        ts(R("em"), R("Ci"), 4095.0, A.is_equal)
+        ts(R("Cm"), R("Ci"), -2048.0, A.add)
+        tt(R("Rm"), R("Ff"), R("npm"), A.mult)
+        cp(R("vA"), P("ind", R("IDX"), R("lvu")))
+        for h in range(2):
+            mm(R("m1", 8 * h, 8 * h + 8), R("vA", 128 * h, 128 * h + 128), R("PK8"))
+        ts(R("vcol"), R("m1", 0, 16), -1.0, A.mult)
+        bh_open(0)
+        bh_open(1)
+        if t == 0:
+            even_more()
+        for c, (b0, b1) in enumerate(CHUNKS):
+            for j in range(b0, b1):
+                sub(j)
+                if j in (3, 7):
+                    over(j // 4)
+                if j == 3:
+                    for u, w in ((256, "W1"), (272, "W2")):
+                        for m in range(16):
+                            mm(R("ov", u, u + 16), R(w, 128 * m, 128 * m + 128), R("zl" + st, m, 256, 16), m == 0, m == 15)
+                    hash_ops(R("ov", 256, 288), 16, "ru", "rp", R("rl"))
+                    act(R("yr" + st), P("ind", R("BK"), R("rl")), F.Copy)
+                    send("yr" + st, "yl" + st, (rank - 1 - t) % 4, "ys" + st, "ya" + st)
+            hashes(b0, b1, c)
+            if b1 in (4, 8):
+                scount(b1 // 4 - 1)
+        for q in range(8):
+            same(q)
+        decide(0)
+        decide2(0)
+        mm(R("dp0", 0, 256), R("IDb"), R("yl" + st), True, False)
+        mm(R("dp0", 0, 256), R("NIDb"), R(x), False, True)
+        act(R("rr"), R("dp0", 0, 256), F.Abs)
+        for m in range(16):
+            mm(R("up", 384, 400), R("W1", 128 * m, 128 * m + 128), R("rr", m, 256, 16), m == 0, m == 15)
+        cp(R("bi"), R("up", 384, 400))
+        ts(R("bk"), R("bi"), 1023, A.bitwise_and)
+        tt(R("bk2"), R("bk"), R(lv), A.subtract)
+        mm(R("dp0", 256, 512), R("IDb"), R("rr"), True, False)
+        mm(R("dp0", 256, 512), R("NIDb"), R(x), False, True)
+        act(R("rx"), R("dp0", 256, 512), F.Copy)
+        decide(1)
+        for hi in range(2):
+            for q in range(8):
+                o = 256 + 128 * hi + 16 * q
+                mm(R("ov", o, o + 16), R("MQ", 384 * q + 128 * hi, 384 * q + 128 * hi + 128), R("wb", 16 * q, 16 * q + 16), True, hi == 0)
+                if hi == 1:
+                    mm(R("ov", o, o + 16), R("MQ", 384 * q + 256, 384 * q + 384), R("wb", 128 + 16 * q, 144 + 16 * q), False, True)
+        decide2(1)
+        tt(R("winb"), R("ov", 256, 512), R("wb"), A.is_lt)
+        tt(R("winm"), R("ov", 256, 512), R("wm"), A.is_lt)
+        for h in range(2):
+            hs = (128 * h, 128 * h + 128)
+            mm(R("up", 320 + 8 * h, 328 + 8 * h), R("wm", *hs), R("G8"))
+            mm(R("up", 336 + 8 * h, 344 + 8 * h), R("dpm", *hs), R("G8f"))
+        for h in range(2):
+            mm(R("up", 352 + 8 * h, 360 + 8 * h), R("winm", 128 * h, 128 * h + 128), R("G8"))
+        for h in range(2):
+            hs = (128 * h, 128 * h + 128)
+            mm(R("dp1", *hs), R("winb", *hs), R("IDb"))
+        mm(R("m0", 0, 256), R("cI" + st), R("pm"), True, False)
+        mm(R("m0", 0, 256), R("IDb"), R("pmI"), False, False)
+        for h in range(2):
+            hs = (128 * h, 128 * h + 128)
+            mm(R("m0", *hs), R("r2", *hs), R("IDf"), False, False)
+            mm(R("m0", *hs), R("pS", *hs), R("I4K"), False, h == 1)
+        for h in range(2):
+            hs = (128 * h, 128 * h + 128)
+            mm(R("m1", *hs), R("NE", *hs), R("IDf"))
+        act(R("NEs"), R("m1", 0, 256), F.Copy)
+        tt(R("dp0", 0, 256), R("rx"), R("dp1", 0, 256), A.mult)
+        tt(R(xn), R("dp0", 0, 256), R(x), A.add)
+        act(R("newc"), R("m0", 0, 256), F.Identity, 4095.0)
+        tt(R("vt"), R(lv), R("trash"), A.subtract)
+        tt(R("of"), R("vt"), R("up", 352, 368), A.mult)
+        tt(R("of"), R("of"), R("trash"), A.add)
+        cp(R("ofu"), R("of"))
+        cp(P("ind", R("ET", 0, 2944), R("ofu")), R("newc"))
+        n0 = M + 256 * t
+        tt(R("XT", n0, n0 + 256), R(x), R("dp1", 0, 256), A.mult)
+        tt(R("NEw"), R("NEs"), R("dp1", 0, 256), A.mult)
+        act(R("ET", n0, n0 + 256), R("NEw"), F.Identity, 4095.0)
+        cp(R("dn"), R("up", 336, 352))
+        ts(R("dn"), R("dn"), 4095, A.bitwise_and)
+        tt(R("b1"), R(lv), R("dn"), A.subtract)
+        tt(R("b1"), R("b1"), R("up", 320, 336), A.mult)
+        tt(R("b1"), R("b1"), R("dn"), A.add)
+        tt(R("b2"), R("bk2"), R("up", 352, 368), A.mult)
+        tt(R(lvn), R("b1"), R("b2"), A.add)
+        if not last:
+            cp(R("lvu"), R(lvn))
+        else:
+            dma("y", T.ykids[:], T.ET[:, 0:W], [R("ET", 0, W)], [])
+            dma("s", T.ycand[:], T[xn][:], [R(xn)], [])
+            dma("s", T.ynodes[:], T.XT[:, M:W], [R("XT", M, W)], [])
+            dma("s", T.yspot[:], T[lvn][:], [R(lvn)], [])
+
+    finish()

@@ -1,56 +1,74 @@
+import math
 from concourse.mybir import dt, AluOpType as A, ActivationFunctionType as F
 
 M, L, STEPS, H = 1792, 256, 3, 4096
 W = M + L * STEPS
+UNITS = 2 * STEPS
 NENG = 8
-BIG = float(2 ** 23)
+MK = 786432.0
+B5 = float(2 ** 22)
+VO = 1280.0
 
 SB = {
-    "XT": (4096, "bfloat16"), "BK": (4096, "bfloat16"), "ET": (2944, "float32"), "KI": (M, "int32"), "IDX": (2304, "float32"),
-    "ONE": (1024, "bfloat16"), "ZER": (128, "bfloat16"), "IDb": (128, "bfloat16"), "NIDb": (128, "bfloat16"), "IDf": (128, "float32"), "NIDf": (128, "float32"),
-    "N20": (128, "bfloat16"), "N22": (128, "bfloat16"), "I4K": (128, "bfloat16"), "G8t": (8, "bfloat16"), "G8": (8, "bfloat16"), "G8f": (8, "float32"),
-    "GW": (16, "float32"), "W1": (2048, "bfloat16"), "W2": (2048, "bfloat16"), "GS": (24, "bfloat16"), "GO": (8, "bfloat16"), "GO2": (8, "bfloat16"),
-    "PICK": (1024, "bfloat16"), "PK8": (8, "bfloat16"), "TRI": (128, "bfloat16"), "pms": (128, "bfloat16"), "pm": (256, "bfloat16"), "npm": (256, "bfloat16"),
-    "pmn": (256, "float32"), "rmf": (128, "float32"), "rmb": (128, "bfloat16"), "CR": (512, "bfloat16"), "REP": (2048, "bfloat16"), "trash": (16, "float32"),
-    "II": (256, "bfloat16"), "pmI": (256, "bfloat16"), "cI0": (128, "bfloat16"), "cI1": (128, "bfloat16"), "cI2": (128, "bfloat16"),
-    "wt": (2, "bfloat16"), "sp": (16, "int32"), "x0": (256, "bfloat16"), "x1": (256, "bfloat16"), "lv0": (16, "float32"), "lv1": (16, "float32"), "lvu": (16, "uint16"),
-    "Ei": (256, "int32"), "Ci": (256, "int32"), "CL": (256, "uint16"), "Ff": (256, "float32"), "em": (256, "bfloat16"), "Cm": (256, "float16"), "Rm": (256, "float32"),
-    "vA": (256, "float16"), "vcol": (16, "float32"), "xT": (256, "bfloat16"), "d0": (256, "bfloat16"),
-    "XG": (4096, "bfloat16"), "DD": (4096, "bfloat16"), "SG": (4096, "bfloat16"), "CMP": (4096, "bfloat16"), "HL": (256, "uint16"),
-    "hu0": (256, "int32"), "hp0": (128, "int32"), "hu1": (256, "int32"), "hp1": (128, "int32"), "ru": (32, "int32"), "rp": (16, "int32"), "rl": (16, "uint16"), "MQ": (3072, "bfloat16"), "MD": (3072, "bfloat16"),
-    "tA": (256, "float32"), "cap": (256, "bfloat16"), "nc": (256, "bfloat16"), "key": (256, "float32"), "wm": (256, "bfloat16"), "w1s": (256, "bfloat16"), "wb": (256, "bfloat16"),
-    "k1": (256, "float32"), "k2": (256, "float32"), "dpm": (256, "float32"), "NE": (256, "float32"), "n1": (256, "float32"), "n2": (256, "float32"), "Si": (256, "int32"), "pS": (256, "bfloat16"),
-    "r2": (256, "float32"), "winb": (256, "bfloat16"), "winm": (256, "bfloat16"), "newc": (256, "float32"), "NEs": (256, "float32"), "NEw": (256, "float32"),
-    "rr": (256, "bfloat16"), "rx": (256, "bfloat16"), "ws": (32, "float32"), "of": (16, "float32"), "ofu": (16, "uint16"), "vt": (16, "float32"),
-    "dn": (16, "int32"), "bk2": (16, "float32"), "b1": (16, "float32"), "b2": (16, "float32"), "bi": (16, "int32"), "bk": (16, "int32"),
+    "XT": (W + 16, "bfloat16"), "BK": (2 * H + 16, "bfloat16"), "fA": (128, "bfloat16"), "ET": (W + 384, "float32"), "EN": (2 * L, "float32"), "KI": (M, "int32"), "IDX": (2304, "float32"), "XW": (W + 384, "bfloat16"),
+    "ONE": (1024, "bfloat16"), "IDb": (128, "bfloat16"), "NIDb": (128, "bfloat16"), "IDf": (128, "float32"),
+    "G8t": (8, "bfloat16"), "G8": (8, "bfloat16"), "G8f": (8, "float32"), "G8x": (16, "bfloat16"), "GW": (16, "float32"), "GWb": (16, "bfloat16"),
+    "W1": (2048, "bfloat16"), "W2": (2048, "bfloat16"), "BW": (256, "bfloat16"), "NM": (256, "bfloat16"), "ruw": (256, "int32"), "fuw": (256, "int32"), "bw": (256, "int32"), "GS": (32, "bfloat16"), "GO": (8, "bfloat16"), "tb": (UNITS, "float32"),
+    "REP": (2048, "bfloat16"), "TRI": (2048, "bfloat16"), "BDt": (128, "bfloat16"), "BD": (128, "bfloat16"), "NBD": (128, "bfloat16"), "BD2": (128, "bfloat16"),
+    "BDQ": (512, "bfloat16"), "BDW": (640, "bfloat16"), "Ck": (32, "float32"), "pms": (128, "bfloat16"), "pm": (128, "bfloat16"),
+    "CT": (512, "bfloat16"), "CRK": (128, "bfloat16"), "CH": (256, "bfloat16"), "C8": (128, "bfloat16"), "DK": (256, "bfloat16"), "DE": (512, "bfloat16"),
+    "DB5": (128, "bfloat16"), "D256": (128, "bfloat16"), "I4K": (128, "bfloat16"), "N4K": (128, "bfloat16"), "P64K": (128, "bfloat16"),
+    "II": (256, "bfloat16"), "PN": (128 * STEPS, "bfloat16"), "N4": (128, "float32"), "rm": (256, "bfloat16"), "trash": (16, "float32"), "RT": (256, "float32"),
+    "wt": (2, "bfloat16"), "sp": (16, "int32"), "x0": (256, "bfloat16"), "x1": (256, "bfloat16"), "lv0": (16, "float32"), "lv1": (16, "float32"),
+    "lvu": (16, "uint16"), "lvw": (16, "float32"),
+    "Ef": (256, "float32"), "Kb": (256, "bfloat16"), "CL": (256, "uint16"), "CF": (128, "uint16"), "em": (256, "bfloat16"), "Cm": (256, "float16"),
+    "vA": (256, "float16"), "xT": (256, "bfloat16"), "d0": (256, "bfloat16"),
+    "XG": (4096, "bfloat16"), "DD": (4096, "bfloat16"), "SG": (4096, "bfloat16"), "CMP": (4096, "bfloat16"), "EQ": (4352, "bfloat16"), "HL": (256, "uint16"),
+    "hr": (512, "bfloat16"), "u1": (256, "float32"), "hp": (256, "int32"), "hf": (256, "float32"), "hg": (256, "bfloat16"),
+    "ru": (16, "int32"), "rp": (8, "int32"), "rl": (8, "uint16"), "fu": (16, "int32"), "fp": (8, "int32"), "fl": (8, "uint16"),
+    "fd": (128, "bfloat16"), "fD": (128, "bfloat16"), "fS": (128, "bfloat16"), "fC": (128, "bfloat16"), "fr": (128, "bfloat16"), "fo": (128, "bfloat16"), "fs": (128, "bfloat16"),
+    "tA": (256, "bfloat16"), "ncn": (256, "bfloat16"), "wm": (256, "bfloat16"), "sc": (256, "bfloat16"), "s1": (256, "bfloat16"), "s2": (256, "bfloat16"),
+    "k1": (256, "float32"), "k2": (256, "float32"), "k3": (256, "int32"), "tw": (256, "float32"), "win": (256, "bfloat16"),
+    "A1": (256, "float32"), "A2": (256, "float32"), "rr": (256, "bfloat16"), "rw": (256, "bfloat16"),
+    "of": (16, "float32"), "ofu": (16, "uint16"), "dn": (16, "int32"), "b1": (16, "float32"), "b2": (16, "float32"), "bi": (16, "int32"),
+    "zo": (128 * UNITS, "bfloat16"), "zl": (128 * UNITS, "bfloat16"), "yo": (128 * UNITS, "bfloat16"), "yl": (128 * UNITS, "bfloat16"),
 }
-for _t in range(STEPS):
-    for _n in ("z", "zl", "yr", "yl"):
-        SB[_n + str(_t)] = (256, "bfloat16")
-PS = ["dp0", "dp1", "up", "BH0", "BH1", "ov", "m0", "m1"]
-SCRATCH = {k: ("sbuf", [128, n], d) for k, (n, d) in SB.items()}
+PS = ["dp0", "dp1", "HB", "m0", "BH0", "BH1", "m1", "m2"]
+INORDER = ("BH0", "BH1", "m1", "m2")
+SCRATCH = {k: ("sbuf", [128, n], d) for k, (n, d) in SB.items() if k not in ("hf", "hg")}
 for _n in PS:
     SCRATCH[_n] = ("psum", [128, 512], "float32")
-NDMA = 10
-SEMAPHORES = ["qv", "qs", "qt", "qg"] + ["D%d" % i for i in range(NDMA)] + [n + str(t) for t in range(STEPS) for n in ("zs", "za", "ys", "ya")]
+NDMA = 15
+SEMAPHORES = ["qv", "qs", "qt", "qg"] + ["D%d" % i for i in range(NDMA)] + [n + str(u) for u in range(UNITS) for n in ("zs", "za", "ys", "ya")]
 
+TWICE = 1
+SGN = (4, 0, 2, 0, 2, 0)
+XGV = ((2, 3), (), (), (), (), ())
+AGAIN = ((), (2, 3), (), (2, 3), (), (2, 3))
+EARLY = (2, 4)
+HASHA = (0, 1, 2, 3, 4, 5)
+GP = 512
+CP = 512
+CONV = "v"
 
 ORDER = {}
 CYC = 0.83e-3
-PECYC = 0.45e-3
-WAKE = 0.18
-CHUNKS = ((0, 2), (2, 4), (4, 6), (6, 8))
-G1V = ()
-SGV = (0,)
-MQV = tuple(range(8))
+PECYC = 0.42e-3
+WAKE = 0.22
+ACT0 = 0.06
+FLIGHT = 4.0
+FIRST = 2.0
+DMA0 = 2.0
+DMARATE = 2.5e5
+ROUNDS = 1000
+SWAPS = 12000
 
 
 def overlap(a, b):
     return a[1] < b[2] and b[1] < a[2] and not (a[3] == b[3] and a[3] > 1 and (a[1] - b[1]) % a[3])
 
 
-def schedule(nodes, psum):
-    wake = WAKE
+def schedule(nodes):
     n = len(nodes)
     preds = [[] for _ in range(n)]
     hist = {}
@@ -59,14 +77,16 @@ def schedule(nodes, psum):
         seen = {}
         for rs, w in ((reads, False), (writes, True)):
             for r in rs:
-                bank = r[0] in psum
+                bank = r[0] in INORDER
                 for (j, rj, wj) in hist.get(r[0], ()):
                     ov = overlap(r, rj)
                     same = nodes[j][1] == q and kind == "c" and nodes[j][0] == "c"
                     if bank and (q == "t" or not same):
-                        full = not same or (ov and wj and q != "t")
+                        full = not same
+                    elif same and q == "t" and r[0] not in PS:
+                        continue
                     elif ov and (w or wj):
-                        full = not same or wj
+                        full = not same or q != "t"
                     else:
                         continue
                     seen[j] = seen.get(j, False) or full
@@ -74,49 +94,159 @@ def schedule(nodes, psum):
         for rs, w in ((reads, False), (writes, True)):
             for r in rs:
                 h = hist.get(r[0], [])
-                if w and abs(r[3]) == 1 and r[4] == 128 and r[0] not in psum:
+                if w and abs(r[3]) == 1 and r[4] == 128 and r[0] not in INORDER:
                     h = [e for e in h if not (r[1] <= e[1][1] and e[1][2] <= r[2])]
-                if r[0] in psum and len(h) > 40:
+                if r[0] in INORDER and len(h) > 40:
                     h = h[-40:]
                 hist[r[0]] = h + [(i, r, w)]
+    loads = [i for i in range(n) if nodes[i][0] == "d"]
+    for a, b in zip(loads, loads[1:]):
+        preds[b].append((a, None))
     succ = [[] for _ in range(n)]
     for i in range(n):
         for j, full in preds[i]:
             succ[j].append((i, full))
-    prio = [0.0] * n
+    banks = [[b for b in PS if any(r[0] == b for r in nodes[i][3] + nodes[i][4])] for i in range(n)]
+    first = min(i for i in range(n) if nodes[i][0] == "r")
+    hold = [nodes[i][5] if nodes[i][0] == "c" else (0.1 if nodes[i][0] == "d" else 0.8) for i in range(n)]
+    last = [nodes[i][5] + (FIRST if i == first else 0.0) for i in range(n)]
+    moved = DMA0
+    for i in loads:
+        if nodes[i][4]:
+            moved += last[i] - DMA0
+            last[i] = moved
+
+    def gap(i, full):
+        return 0.0 if full is None else (last[i] + WAKE if full else hold[i])
+
+    def find(uses, t):
+        lo, hi = 0, len(uses)
+        while lo < hi:
+            mid = (lo + hi) // 2
+            if uses[mid][0] < t:
+                lo = mid + 1
+            else:
+                hi = mid
+        return lo
+
+    def place(rank, back):
+        before, after = (succ, preds) if back else (preds, succ)
+        left = [len(p) for p in before]
+        est = [last[i] - hold[i] if back else 0.0 for i in range(n)]
+        at = [0.0] * n
+        ready = [(rank[i], i) for i in range(n) if not left[i]]
+        busy = {}
+        while ready:
+            e = min(ready)
+            ready.remove(e)
+            i = e[1]
+            q, t, h = nodes[i][1], est[i], hold[i]
+            own = busy.setdefault(q, [])
+            shared = [busy.setdefault(b, []) for b in banks[i]]
+            t0 = -1.0
+            while t != t0:
+                t0 = t
+                k = max(find(own, t) - 1, 0)
+                while k < len(own) and own[k][0] < t + h:
+                    t = max(t, own[k][1])
+                    k += 1
+                for uses in shared:
+                    k = find(uses, t - 2.0)
+                    while k < len(uses) and uses[k][0] - WAKE < t + h:
+                        if uses[k][2] != q:
+                            t = max(t, uses[k][1] + WAKE)
+                        k += 1
+            for uses in [own] + shared:
+                uses.insert(find(uses, t), (t, t + h, q))
+            at[i] = t + h if back else t
+            for k, f in after[i]:
+                est[k] = max(est[k], at[i] + gap(k, f) - hold[k] if back else t + gap(i, f))
+                left[k] -= 1
+                if not left[k]:
+                    ready.append((rank[k], k))
+        return at
+
+    def settle(rank):
+        at = place(rank, False)
+        rank = [-a for a in place([-(at[i] + last[i]) for i in range(n)], True)]
+        at = place(rank, False)
+        return max(at[i] + last[i] for i in range(n)), rank, at
+    seed = [1]
+
+    def draw():
+        seed[0] = (seed[0] * 1103515245 + 12345) % 2 ** 31
+        return seed[0] / 2.0 ** 31
+    rank = [0.0] * n
     for i in range(n - 1, -1, -1):
-        c = nodes[i][5]
-        prio[i] = max([c] + [prio[k] + (c + wake if full else 0.0) for k, full in succ[i]])
-        if nodes[i][0] == "d":
-            prio[i] += 1e7 - 1e3 * i
-    left = [len(p) for p in preds]
-    ready = {}
-    free = {}
-    est = [0.0] * n
-    for i in range(n):
-        if not left[i]:
-            ready.setdefault(nodes[i][1], []).append(i)
-    order = []
-    while len(order) < n:
-        best = None
-        for q, r in ready.items():
-            if r:
-                t = min(max(est[i], free.get(q, 0.0)) for i in r)
-                if best is None or t < best[0]:
-                    best = (t, q)
-        t, q = best
-        i = max((k for k in ready[q] if max(est[k], free.get(q, 0.0)) <= t + 0.02), key=lambda k: (prio[k], -k))
-        ready[q].remove(i)
-        st = max(est[i], free.get(q, 0.0))
-        end = st + nodes[i][5]
-        free[q] = end if nodes[i][0] == "c" else st + (0.1 if nodes[i][0] == "d" else 1.0)
-        order.append(i)
-        for k, full in succ[i]:
-            est[k] = max(est[k], end + wake if full else st)
-            left[k] -= 1
-            if not left[k]:
-                ready.setdefault(nodes[k][1], []).append(k)
-    return order
+        rank[i] = min([-last[i]] + [rank[k] - gap(i, f) for k, f in succ[i]])
+    span, rank, at = settle(rank)
+    best = (span, at)
+    for _ in range(ROUNDS):
+        lo, wide, far, part = -span * draw(), 3 + 17 * draw(), 0.5 * 8 ** draw(), 0.1 * 10 ** draw()
+        s2, r2, at = settle([a + far * (draw() + draw() - 1) * 2 if lo - wide <= a < lo and draw() < part else a for a in rank])
+        if s2 <= span + 0.15:
+            span, rank = s2, r2
+        if s2 < best[0]:
+            best = (s2, at)
+
+
+    def run(order):
+        at, why, free, held = [0.0] * n, [None] * n, {}, {}
+        for i in order:
+            t, w, q = 0.0, None, nodes[i][1]
+            for k, d in after[i]:
+                if at[k] + d > t:
+                    t, w = at[k] + d, (k, False)
+            if q in free and free[q][0] > t:
+                t, w = free[q][0], (free[q][1], True)
+            for b in banks[i]:
+                for other, (e, k) in held.setdefault(b, {}).items():
+                    if other != q and e + WAKE > t:
+                        t, w = e + WAKE, (k, True)
+            at[i], why[i] = t, w
+            free[q] = (t + hold[i], i)
+            for b in banks[i]:
+                held[b][q] = free[q]
+        j = max(range(n), key=lambda k: at[k] + last[k])
+        return at[j] + last[j], at, why, j
+    after = [[(k, gap(k, f)) for k, f in preds[i]] for i in range(n)]
+    needs = [set(k for k, f in preds[i]) for i in range(n)]
+    order = sorted(range(n), key=lambda i: (best[1][i], i))
+    span, at, why, j = run(order)
+    for step in range(SWAPS):
+        pairs, k = [], j
+        while why[k] is not None:
+            if why[k][1]:
+                pairs.append((why[k][0], k))
+            k = why[k][0]
+        a, b = pairs[int(draw() * len(pairs))]
+        more = (0, 0, 0, 3, 10)[int(draw() * 5)]
+        pa, pb = order.index(a), order.index(b)
+        if draw() < 0.5:
+            pa = max(0, pa - more)
+            part, first = order[pa:pb + 1], {b}
+            for k in reversed(part):
+                if k in first:
+                    first |= needs[k]
+            if a in first:
+                continue
+        else:
+            pb = min(n - 1, pb + more)
+            part, late = order[pa:pb + 1], {a}
+            for k in part:
+                if needs[k] & late:
+                    late.add(k)
+            if b in late:
+                continue
+            first = set(part) - late
+        other = order[:pa] + [k for k in part if k in first] + [k for k in part if k not in first] + order[pb + 1:]
+        s2, at, w2, j2 = run(other)
+        if s2 <= span - (0.1 * (1 - step / SWAPS) + 0.01) * math.log(draw() + 1e-9):
+            order, span, why, j = other, s2, w2, j2
+            if s2 < best[0]:
+                best = (s2, at)
+    ORDER["plan"] = (best, preds, hold, last, banks)
+    return sorted(range(n), key=lambda i: (best[1][i], i))
 
 
 def rank_program(g, core, T, topo):
@@ -132,7 +262,7 @@ def rank_program(g, core, T, topo):
     def R(name, lo=0, hi=None, step=1, p1=128):
         return (name, lo, SB[name][0] if hi is None and name in SB else (512 if hi is None else hi), step, p1)
 
-    def P(name, win, off):
+    def P(win, off):
         return ("ind", win, off)
 
     def ap(r):
@@ -170,7 +300,7 @@ def rank_program(g, core, T, topo):
                 for (who, ev, lo, hi, wasw, step) in hist.get(r[0], ()):
                     over = lo < r[2] and r[1] < hi and not (step == r[3] and step > 1 and (lo - r[1]) % step)
                     if who == me:
-                        if not wasw or not over or (w and me == "t"):
+                        if not (w or wasw) or not over or me == "t":
                             continue
                     elif not (bank or (over and (w or wasw))):
                         continue
@@ -192,15 +322,17 @@ def rank_program(g, core, T, topo):
     nodes = []
 
     def emit(q, fn, reads, writes, cost):
-        nodes.append(("c", q, fn, flat(reads), flat(writes), cost, None))
+        offs = [r[2] for r in writes if r[0] == "ind"]
+        nodes.append(("c", q, [fn], flat(reads) + offs, [r[1] if r[0] == "ind" else r for r in writes], cost, None))
 
     nd = [0]
 
     def dma(q, out, in_, reads, writes):
         sem = "D%d" % nd[0]
         nd[0] += 1
-        size = 128 * (writes or reads)[0][2] * 4
-        nodes.append(("d", q, lambda: queues[q].dma_start(out, in_), reads, writes, 2.0 + size / 2.0e5, sem))
+        r = (writes or reads)[0]
+        size = 128 * (r[2] - r[1]) * (4 if SB[r[0]][1] in ("float32", "int32") else 2)
+        nodes.append(("d", q, lambda: queues[q].dma_start(out, in_), reads, writes, DMA0 + size / DMARATE, sem))
 
     def send(src, dst, peer, lsem, rsem):
         to = T.cores[peer]
@@ -208,21 +340,23 @@ def rank_program(g, core, T, topo):
         engs = topo.engines(core, to)[:NENG]
 
         def fn():
-            g.remote_dma(T[dst][:], T[src][:], T.sem[rsem], T.sem[lsem], pid, rid, sum(1 << e for e in engs))
-        nodes.append(("r", "g", fn, [R(src)], [R(dst)], 5.0, (lsem, len(engs))))
+            g.remote_dma(ap(dst), ap(src), T.sem[rsem], T.sem[lsem], pid, rid, sum(1 << e for e in engs))
+        nodes.append(("r", "g", fn, [src], [dst], FLIGHT, (lsem, len(engs))))
 
     def finish():
         order = ORDER.get("order")
         if order is None or len(order) != len(nodes):
-            order = schedule(nodes, PS)
+            order = schedule(nodes)
             ORDER["order"] = order
+            ORDER["nodes"] = nodes
         for i in order:
             kind, q, fn, reads, writes, cost, sem = nodes[i]
             if kind == "c":
                 deps(q, q, reads, writes)
                 name = "q" + q
-                count[name] = count.get(name, 0) + 1
-                fn().then_inc(T.sem[name], 1)
+                for f in fn:
+                    count[name] = count.get(name, 0) + 1
+                    f().then_inc(T.sem[name], 1)
                 ev, me = (name, count[name]), q
             elif kind == "d":
                 deps(q, sem, reads, writes)
@@ -239,10 +373,10 @@ def rank_program(g, core, T, topo):
         for sem in sorted(count):
             need("g", (sem, count[sem]))
 
-    for t in range(STEPS):
-        for buf, sem in (("zl", "za"), ("yl", "ya")):
-            hist[buf + str(t)] = [("remote", (sem + str(t), NENG), 0, 256, True, 1)]
-            count[sem + str(t)] = NENG
+    for buf, sem in (("zl", "za"), ("yl", "ya")):
+        hist[buf] = [("remote", (sem + str(u), NENG), 128 * u, 128 * u + 128, True, 1) for u in range(UNITS)]
+        for u in range(UNITS):
+            count[sem + str(u)] = NENG
 
     def width(r):
         return 16 * width(r[2]) if r[0] == "ind" else -((r[1] - r[2]) // abs(r[3]))
@@ -252,15 +386,17 @@ def rank_program(g, core, T, topo):
 
     def vcost(out, ins, kind):
         if out[0] == "ind":
-            return 0.05 + 4.0 * width(out[2]) * 16 * CYC
+            return 0.05 + 3.8 * width(out[2]) * 16 * CYC
         n = width(out)
         if any(r[0] == "ind" for r in ins):
             return 0.05 + 1.56 * n * CYC
+        if kind == 0:
+            return ACT0 + n * CYC
         if kind == 2:
             c = n if any(r[0] in PS for r in ins) else 2 * n
         else:
             c = n
-            if kind == 1 and all(dtype_of(r) not in ("float32", "int32") for r in [out] + ins if width(r) > 1):
+            if all(dtype_of(r) not in ("float32", "int32") for r in [out] + ins):
                 c = n / 2
         return max(64, c) * CYC
 
@@ -284,16 +420,27 @@ def rank_program(g, core, T, topo):
     def fill(out, c):
         emit("v", lambda: V.memset(ap(out), c), [], [out], vcost(out, [], 1))
 
-    def scan(out, d0, d1):
-        emit("v", lambda: V.tensor_tensor_scan(ap(out), ap(d0), ap(d1), 0.0, A.mult, A.max), [d0, d1], [out], vcost(out, [d0, d1], 1))
+    def scan(out, d0, d1, op0=A.mult, op1=A.max):
+        emit("v", lambda: V.tensor_tensor_scan(ap(out), ap(d0), ap(d1), 0.0, op0, op1), [d0, d1], [out], vcost(out, [d0, d1], 1))
 
     def act(out, a, f, bias=0.0, scale=1.0):
-        col = not isinstance(bias, (int, float))
-        emit("s", lambda: S.activation(ap(out), ap(a), f, bias=ap(bias) if col else bias, scale=scale), [a] + ([bias] if col else []), [out], vcost(out, [a], 0))
+        cols = [c for c in (bias, scale) if not isinstance(c, (int, float))]
+        b = bias if isinstance(bias, (int, float)) else ap(bias)
+        s = scale if isinstance(scale, (int, float)) else ap(scale)
+        emit("s", lambda: S.activation(ap(out), ap(a), f, bias=b, scale=s), [a] + cols, [out], vcost(out, [a], 0))
 
-    def mm(out, lhsT, rhs, start=True, stop=True):
-        cost = max(64, width(rhs)) * (4 if dtype_of(lhsT) == "float32" else 1) * PECYC
-        emit("t", lambda: TE.matmul(ap(out), ap(lhsT), ap(rhs), start, stop), [lhsT, rhs], [out], cost)
+    def mms(calls):
+        fns, cost = [], 0.0
+        for c in calls:
+            fns.append(lambda c=c: TE.matmul(ap(c[0]), ap(c[1]), ap(c[2]), c[3], c[4]))
+            cost += max(64, width(c[2])) * (4 if dtype_of(c[1]) == "float32" else 1) * PECYC
+        nodes.append(("c", "t", fns, [c[1] for c in calls] + [c[2] for c in calls], [c[0] for c in calls], cost, None))
+
+    def msum(terms, new=True, done=True):
+        mms([(o, a, b, new and i == 0, done and i == len(terms) - 1) for i, (o, a, b) in enumerate(terms)])
+
+    def mm(out, lhsT, rhs):
+        msum([(out, lhsT, rhs)])
 
     def aff(out, a, pat, op, fl, base, cm):
         emit("g", lambda: g.affine_select(ap(out), ap(a), pat, op, fl, base, cm), [a], [out], 0.17 + 2 * width(out) * CYC)
@@ -301,292 +448,371 @@ def rank_program(g, core, T, topo):
     def iota(out, pat, base, cm):
         emit("g", lambda: g.iota(ap(out), pat, base, cm, allow_small_or_imprecise_dtypes=True), [], [out], 0.13 + 2 * width(out) * CYC)
 
-    dma("y", T.sp[:], T.spot[:], [], [R("sp")])
-    dma("y", T.KI[:], T.kids[:], [], [R("KI")])
-    dma("s", T.wt[:], T.wts[:], [], [R("wt")])
-    dma("s", T.x0[:], T.cand[:], [], [R("x0")])
-    dma("s", T.XT[:, 0:M], T.nodes[:], [], [R("XT", 0, M)])
-    dma("y", T.BK[:], T.book[:], [], [R("BK")])
+    def sfill(name, lo, hi, c):
+        for a in range(lo, hi, 1024):
+            b = min(hi, a + 1024)
+            act(R(name, a, b), R("ONE", 0, b - a), F.Copy, 0.0, c)
 
+    def gfill(name, lo, hi, c, step=0):
+        for a in range(lo, hi, 384):
+            b = min(hi, a + 384)
+            iota(R(name, a, b), [[step, b - a]], c + step * (a - lo), 0)
+
+    dma("y", T.sp[:], T.spot[:], [], [R("sp")])
+    dma("s", T.wt[:], T.wts[:], [], [R("wt")])
+    dma("y", T.KI[:], T.kids[:], [], [R("KI")])
+    dma("y", T.XT[:, 0:M], T.nodes[:], [], [R("XT", 0, M)])
+    dma("y", T.x0[:], T.cand[:], [], [R("x0")])
+    dma("y", T.BK[:, 0:H], T.book[:], [], [R("BK", 0, H)])
+    dma("y", T.BK[:, H:2 * H], T.book[:], [], [R("BK", H, 2 * H)])
+
+    ID, NID, RM = R("IDb"), R("NIDb"), R("rm", 0, 128)
+    N256, P256, NB5 = R("DE", 0, 128), R("D256"), R("DE", 256, 384)
     fill(R("ONE"), 1.0)
-    fill(R("ZER"), 0.0)
-    aff(R("IDb"), R("ONE", 0, 128), [[-1, 128]], A.is_equal, 0.0, 0, 1)
+    aff(ID, R("ONE", 0, 128), [[-1, 128]], A.is_equal, 0.0, 0, 1)
     aff(R("G8t"), R("ONE", 0, 8), [[-16, 8]], A.is_ge, 0.0, 0, 1)
     aff(R("G8"), R("G8t"), [[16, 8]], A.is_ge, 0.0, 15, -1)
-    fill(R("W1"), 0.0)
-    fill(R("W2"), 0.0)
-    fill(R("XT", M, 4096), 0.0)
-    ts(R("NIDb"), R("IDb"), -1.0, A.mult)
+    aff(R("BDt"), R("ONE", 0, 128), [[-16, 8], [0, 16]], A.is_ge, 0.0, 0, 1)
+    aff(R("BD"), R("BDt"), [[16, 8], [0, 16]], A.is_ge, 0.0, 15, -1)
+    iota(R("CRK"), [[0, 8], [-32, 16]], 528, 0)
+    iota(R("II"), [[1, 256]], 0, 0)
+    iota(R("trash"), [[16, 16]], W, 1)
+    gfill("IDX", 0, 2304, -int(VO), 1)
+    gfill("XW", 0, M + L, 0)
+    fill(R("XT", M, W + 16), 0.0)
+    fill(R("CH"), MK / 128)
+    fill(R("BK", 2 * H, 2 * H + 16), -1.0)
+    ts(NID, ID, -1.0, A.mult)
+    cp(R("IDf"), ID)
     for m in range(16):
-        cp(R("REP", m, 2048, 16), R("IDb"))
+        cp(R("REP", m, 2048, 16), ID)
     cp(R("G8f"), R("G8"))
     cp(R("lvu"), R("sp"))
     cp(R("lv0"), R("sp"))
     for j, w in ((0, "W1"), (1, "W2")):
-        ts(R("GW", 8 * j, 8 * j + 8), R("G8f"), R("wt", j, j + 1), A.mult)
-        for q in range(8):
-            ts(R(w, 16 * q, 16 * q + 129 * 15 + 1, 129), R("ONE", 0, 16), R("GW", 8 * j + q, 8 * j + q + 1), A.mult)
-    aff(R("PK8"), R("ONE", 0, 8), [[-16, 8]], A.is_equal, 0.0, 0, 1)
-    aff(R("TRI"), R("ZER"), [[1, 128]], A.is_gt, -8192.0, 0, -1)
-    iota(R("IDX"), [[1, 2304]], -1280, 0)
-    fill(R("CR"), 0.0)
-    fill(R("CR", 128, 256, 1, 2), 2048.0)
-    fill(R("CR", 256, 384, 1, 2), 1.0)
-    fill(R("CR", 256, 384, 1, 1), -2048.0)
-    iota(R("CR", 128, 256, 1, 1), [[0, 8], [-4096, 16]], 65536, 0)
-    iota(R("II"), [[1, 256]], 1, 0)
-    fill(R("CR", 0, 128, 1, 2), 1.0)
-    fill(R("CR", 0, 128, 1, 1), -4096.0)
-    iota(R("trash"), [[16, 16]], W, 1)
+        if HASHA:
+            sfill(w, 0, 2048, 0.0)
+            ts(R("GW", 8 * j, 8 * j + 8), R("G8f"), R("wt", j, j + 1), A.mult)
+            for q in range(8):
+                ts(R(w, 16 * q, 16 * q + 129 * 15 + 1, 129), R("ONE", 0, 16), R("GW", 8 * j + q, 8 * j + q + 1), A.mult)
+        ts(R("GWb", 8 * j, 8 * j + 8), R("G8"), R("wt", j, j + 1), A.mult)
+        ts(R("BW", 128 * j, 128 * j + 128), R("BD"), R("wt", j, j + 1), A.mult)
+    for name, lo, c in (("DK", 0, -2.0 ** -12), ("DK", 128, -2.0 ** -12), ("DE", 0, -256.0), ("DE", 128, 1024.0), ("DE", 256, -B5), ("DE", 384, -256.0),
+                        ("D256", 0, 256.0), ("DB5", 0, B5), ("I4K", 0, 4096.0), ("N4K", 0, -4096.0), ("P64K", 0, 65536.0)):
+        ts(R(name, lo, lo + 128), ID, c, A.mult)
+    for name, lo, c in (("GS", 0, 1.0), ("GS", 8, 1.0), ("GS", 16, 65536.0), ("GS", 24, 1.0), ("GO", 0, -32.0), ("G8x", 0, 8192.0), ("G8x", 8, 1.0)):
+        ts(R(name, lo, lo + 8), R("G8"), c, A.mult)
+    fill(R("tb"), 224.0)
+    for u in range(UNITS):
+        if SGN[u]:
+            fill(R("tb", u, u + 1, 1, 32 * SGN[u]), 736.0)
+    tt(R("pms", 0, 64), R("IDb", 0, 64), R("IDb", 64, 128), A.add)
+    tt(R("pms", 64, 96), R("pms", 0, 32), R("pms", 32, 64), A.add)
+    tt(R("pm", 0, 16), R("pms", 64, 80), R("pms", 80, 96), A.add)
+    for n in (16, 32, 64):
+        cp(R("pm", n, 2 * n), R("pm", 0, n))
+    for name, lo, a, b in (("CT", 0, 2048.0, 192.0), ("CT", 128, 2048.0, -1856.0), ("CT", 256, B5, -B5), ("CT", 384, -256.0, 0.0),
+                           ("N4", 0, -4095.0, 4095.0), ("NM", 0, B5, -B5), ("NM", 128, B5, -B5), ("C8", 0, -8192.0, 16384.0)) + tuple(("PN", 128 * t, M + 256.0 * t + 2 ** 17, -2.0 ** 17) for t in range(STEPS)):
+        ts(R(name, lo, lo + 128), R("pm"), a, A.mult, b, A.add)
+    fill(R("rm"), 1.0)
+    ts(R("rm", 0, 256, 16), R("ONE", 0, 16), 0.0, A.mult)
+    fill(R("RT"), -1.0)
+    cp(R("RT", 0, 256, 16), R("trash"))
+    for name, lo, c in (("BD2", 0, 16384.0), ("NBD", 0, -1.0), ("BDQ", 0, 1.0), ("BDQ", 128, 1.0), ("BDQ", 256, 65536.0), ("BDQ", 384, 1.0),
+                        ("BDW", 0, 256.0), ("BDW", 128, -256.0), ("BDW", 256, B5), ("BDW", 384, 32.0), ("BDW", 512, -32.0)):
+        ts(R(name, lo, lo + 128), R("BD"), c, A.mult)
+    scan(R("Ck", 0, 16), R("ONE", 0, 16), R("pm", 0, 16))
+    ts(R("Ck", 16, 32), R("pm", 0, 16), -1.5, A.mult)
+    tt(R("Ck", 0, 16), R("Ck", 0, 16), R("Ck", 16, 32), A.add)
+    for k in range(16):
+        ts(R("TRI", 128 * k, 128 * k + 128), R("BD2"), R("Ck", k, k + 1), A.mult)
 
-    def more_constants():
-        cp(R("IDf"), R("IDb"))
-        ts(R("NIDf"), R("IDb"), -1.0, A.mult)
-        ts(R("N20"), R("IDb"), -float(2 ** 20), A.mult)
-        ts(R("N22"), R("IDb"), -float(2 ** 22), A.mult)
-        ts(R("I4K"), R("IDb"), 4096.0, A.mult)
-        for z, c in ((0, 4096.0), (8, 65536.0), (16, 4096.0)):
-            ts(R("GS", z, z + 8), R("G8"), c, A.mult)
-        ts(R("GO"), R("G8"), -float(2 ** 19), A.mult)
-        if SGV:
-            ts(R("GO2"), R("G8"), -float(2 ** 20), A.mult)
-        tt(R("pms", 0, 64), R("IDb", 0, 64), R("IDb", 64, 128), A.add)
-        tt(R("pms", 64, 96), R("pms", 0, 32), R("pms", 32, 64), A.add)
-        tt(R("pm", 0, 16), R("pms", 64, 80), R("pms", 80, 96), A.add)
-        for n in (16, 32, 64, 128):
-            cp(R("pm", n, 2 * n), R("pm", 0, n))
-        ts(R("npm"), R("pm"), -1.0, A.mult, 1.0, A.add)
+    def r(n, h, step=1):
+        return R(n, 128 * h, 128 * h + 128, step)
 
-    def even_more():
-        ts(R("pmn"), R("pm"), BIG + 1.0, A.mult, -BIG, A.add)
-        fill(R("rmf"), 1.0)
-        fill(R("rmb"), 1.0)
-        ts(R("rmf", 0, 128, 16), R("ONE", 0, 8), 0.0, A.mult)
-        ts(R("rmb", 0, 128, 16), R("ONE", 0, 8), 0.0, A.mult)
-        tt(R("pmI"), R("pm"), R("II"), A.mult)
-        for u in range(STEPS):
-            ts(R("cI%d" % u), R("IDb"), -2304.0 + 256.0 * u, A.mult)
-        cp(R("ET", 0, M), R("KI"))
-        fill(R("ET", M, W), 4095.0)
+    def l(n, h):
+        return R(n, 8 * h, 8 * h + 8)
 
-    def hash_ops(u, n, ui, p, out):
-        cp(R(ui, 0, 2 * n), u)
-        ts(R(ui, 0, 2 * n), R(ui, 0, 2 * n), 4095, A.bitwise_and)
-        tt(R(p, 0, n), R(ui, 0, n), R(ui, n, 2 * n), A.mult)
-        ts(R(p, 0, n), R(p, 0, n), 5, A.arith_shift_right)
-        tt(R(p, 0, n), R(p, 0, n), R(ui, n, 2 * n), A.add)
-        ts(R(p, 0, n), R(p, 0, n), 4095, A.bitwise_and)
-        cp(out, R(p, 0, n))
+    def ends(n, h):
+        return R(n, 128 * h + 15, 128 * h + 128, 16)
 
-    for t in range(STEPS):
-        x, xn = ("x0", "x1") if t % 2 == 0 else ("x1", "x0")
-        lv, lvn = ("lv0", "lv1") if t % 2 == 0 else ("lv1", "lv0")
-        st = str(t)
-        last = t == STEPS - 1
-        tab = ("KI", M) if t == 0 else ("ET", M + 256 * (t - 1))
+    def names(u):
+        t, h = u // 2, u % 2
+        return t, h, "x%d" % (t % 2), "x%d" % (1 - t % 2), "lv%d" % (t % 2), "lv%d" % (1 - t % 2)
 
-        def G1(b0, b1):
-            if b0 in G1V:
-                cp(R("XG", 512 * b0, 512 * b1), P("ind", R("XT"), R("CL", 32 * b0, 32 * b1)))
+    def book(u):
+        return R("BK", 0, 2 * H + 16 if u >= TWICE else H)
+
+    def list_hash(u, src, b, at, ui, p, out):
+        msum([(R(b, at, at + 256), ID, R("NM")), (R(b, at, at + 128), R("BW", 0, 128), src), (R(b, at + 128, at + 256), R("BW", 128, 256), src)])
+        scan(R(ui + "w"), R("rm"), R(b, at, at + 256))
+        ts(R(ui), R(ui + "w", 15, 256, 16), 4095, A.bitwise_and)
+        tt(R(p), R(ui, 0, 8), R(ui, 8, 16), A.mult)
+        ts(R(p), R(p), 5, A.arith_shift_right, 4095, A.bitwise_and)
+        tt(R(p), R(p), R(ui, 8, 16), A.add)
+        if u < TWICE:
+            ts(R(p), R(p), 4095, A.bitwise_and)
+        cp(R(out), R(p))
+
+    def slots(u, out):
+        t, h = u // 2, u % 2
+        if t == 0:
+            ts(r("Ef", h), P(R("KI"), l("lvu", h)), -4095.0, A.add)
+        else:
+            act(r("Ef", h), P(R("ET", 0, M + 256 * (t - 1)), l("lvu", h)), F.Identity, -4095.0)
+        act(r("Kb", h), r("Ef", h), F.Identity, MK + 2047.5)
+        msum([(R("m0", 0, 128), R("IDf"), r("Ef", h)), (R("m0", 0, 128), NID, r("Kb", h))])
+        ts(out, R("m0", 0, 128), MK + 4095.0, A.add, float(W), A.min)
+
+    def marks(u, cl):
+        h = u % 2
+        ts(r("em", h), cl, float(W), A.is_equal)
+        ts(r("Cm", h), cl, -2048.0, A.add)
+
+    def early(u):
+        return u in EARLY
+
+    def head(u):
+        t, h, x, xn, lv, lvn = names(u)
+        slots(u, r("CL", h))
+        mm(R("m0", 128, 256), r(x, h), ID)
+        act(r("xT", h), R("m0", 128, 256), F.Copy)
+        tt(r("d0", h), P(R("XT"), l("lvu", h)), r(x, h), A.subtract)
+        act(r("zo", u), r("d0", h), F.Abs)
+        send(r("zo", u), r("zl", u), (rank + 1 + t) % 4, "zs%d" % u, "za%d" % u)
+        if not early(u):
+            marks(u, r("CL", h))
+        cp(r("vA", h), P(R("IDX"), l("lvu", h)))
+
+    def over(u):
+        h = u % 2
+        b, o = ("m2", 256) if h == 0 else ("HB", 384)
+        ov = R(b, o, o + 128)
+        sums = [(R(b, o + k, o + 128, 16), R("SG", 2048 * h + k, 2048 * h + 2048, 16), R("GO")) for k in range(16)]
+        if early(u):
+            msum([(ov, R("fS"), R("BDW", 384, 512))] + sums)
+            tt(R("fo"), R("fr"), ov, A.mult)
+            msum([(ov, R("fS"), R("BDW", 512, 640)), (ov, ID, R("fo"))])
+        else:
+            mms([c + (True, True) for c in sums])
+        act(r("tA", h), ov, F.Relu, R("tb", u, u + 1))
+
+    def bulk(u):
+        h = u % 2
+        for a in range(2048 * h, 2048 * h + 2048, GP):
+            children = P(R("XT"), R("CL", a // 16, (a + GP) // 16))
+            if (a // 512) % 4 in XGV[u]:
+                cp(R("XG", a, a + GP), children)
             else:
-                act(R("XG", 512 * b0, 512 * b1), P("ind", R("XT"), R("CL", 32 * b0, 32 * b1)), F.Copy)
+                act(R("XG", a, a + GP), children, F.Copy)
 
         def sub(j):
-            h, b = j // 4, "dp%d" % (j % 2)
-            mm(R(b), R("NIDb"), R("XG", 512 * j, 512 * j + 512), True, False)
-            mm(R(b), R("xT", 128 * h, 128 * h + 128), R("REP", 512 * (j % 4), 512 * (j % 4) + 512), False, True)
-            act(R("DD", 512 * j, 512 * j + 512), R(b), F.Abs)
-            if h in SGV:
-                ts(R("SG", 512 * j, 512 * j + 512), R(b), 0.0, A.is_ge)
+            b = R("dp%d" % (j % 2))
+            msum([(b, NID, R("XG", 512 * j, 512 * j + 512)), (b, r("xT", h), R("REP", 512 * (j % 4), 512 * (j % 4) + 512))])
+            return b
+
+        def sign(j, b):
+            if j % 4 < SGN[u]:
+                ts(R("SG", 512 * j, 512 * j + 512), b, 0.0, A.is_ge, 2.0, A.mult)
             else:
-                act(R("SG", 512 * j, 512 * j + 512), R(b), F.Sign, 0.5)
+                act(R("SG", 512 * j, 512 * j + 512), b, F.Sign, 0.5, 1.0)
+        for j in range(4 * h, 4 * h + 4):
+            b = sub(j)
+            act(R("DD", 512 * j, 512 * j + 512), b, F.Abs)
+            if j % 4 not in AGAIN[u]:
+                sign(j, b)
+        for j in AGAIN[u]:
+            sign(4 * h + j, sub(4 * h + j))
 
-        def hashes(b0, b1, c):
-            n = 32 * (b1 - b0)
-            for u, w in ((0, "W1"), (n, "W2")):
-                for k in range(16):
-                    mm(R("up", u, u + n), R(w, 128 * k, 128 * k + 128), R("DD", 512 * b0 + k, 512 * b1, 16), k == 0, k == 15)
-            hash_ops(R("up", 0, 2 * n), n, "hu%d" % (c % 2), "hp%d" % (c % 2), R("HL", 32 * b0, 32 * b1))
-            tt(R("CMP", 512 * b0, 512 * b1), P("ind", R("BK"), R("HL", 32 * b0, 32 * b1)), R("DD", 512 * b0, 512 * b1), A.is_ge)
-
-        def over(h):
-            for k in range(16):
-                mm(R("ov", 128 * h + k, 128 * h + 128, 16), R("SG", 2048 * h + k, 2048 * h + 2048, 16), R("GO2" if h in SGV else "GO"))
-            act(R("tA", 128 * h, 128 * h + 128), R("ov", 128 * h, 128 * h + 128), F.Relu, 11.5 * 2 ** 20 - (0.0 if h in SGV else BIG) - 4095.0)
-
-        def scount(h):
-            for k in range(16):
-                mm(R("BH%d" % h, k, 384, 16), R("CMP", 2048 * h + k, 2048 * h + 2048, 16), R("GS"), False, k == 15)
-
-        def bh_open(h):
-            b = "BH%d" % h
-            hs = (128 * h, 128 * h + 128)
-            mm(R(b), R("ONE", 0, 128), R("CR"), True, False)
-            mm(R(b, 0, 128), R("Ff", *hs), R("NIDf"), False, False)
-            mm(R(b, 0, 128), R("em", *hs), R("N20"), False, False)
-            mm(R(b, 128, 256), R("Cm", *hs), R("IDb"), False, False)
-            mm(R(b, 128, 256), R("em", *hs), R("N22"), False, False)
-            mm(R(b, 256, 384), R("Cm", *hs), R("IDb"), False, False)
-            mm(R(b, 384, 512), R("Rm", *hs), R("IDf"), False, False)
-
-        def same(q):
-            b = "m%d" % (q % 2)
-            pk = R("PICK", 128 * q, 128 * q + 128)
-            mm(R(b, 0, 128), R("IDb"), R("TRI"), True, False)
-            mm(R(b, 0, 128), pk, R("vA", 0, 128), False, True)
-            mm(R(b, 128, 256), pk, R("vA", 128, 256))
-            mm(R(b, 256, 384), R("IDb"), R("TRI"), True, False)
-            mm(R(b, 256, 384), pk, R("vA", 128, 256), False, True)
-            o = 384 * q
-            if q in MQV:
-                ts(R("MQ", o, o + 256), R(b, 0, 256), R("vcol", q, q + 1), A.add, 0.0, A.is_equal)
-                ts(R("MQ", o + 256, o + 384), R(b, 256, 384), R("vcol", 8 + q, 9 + q), A.add, 0.0, A.is_equal)
-                return
-            act(R("MD", o, o + 256), R(b, 0, 256), F.Abs, R("vcol", q, q + 1))
-            act(R("MD", o + 256, o + 384), R(b, 256, 384), F.Abs, R("vcol", 8 + q, 9 + q))
-            if q % 2:
-                ts(R("MQ", o - 384, o + 384), R("MD", o - 384, o + 384), 0.0, A.is_equal)
-
-        def decide(h):
-            b = "BH%d" % h
-            lo, hi = 128 * h, 128 * h + 128
-
-            def r(n, step=1):
-                return R(n, lo, hi, step)
-            tt(r("cap"), R(b, 0, 128), r("tA"), A.is_gt)
-            tt(r("nc"), R(b, 0, 128), r("tA"), A.is_le)
-            tt(R(b, 128, 256), r("nc"), R(b, 128, 256), A.mult)
-            tt(r("wm"), r("pmn"), R(b, 128, 256), A.is_gt)
-            scan(r("w1s"), R("rmb"), r("wm"))
-            scan(r("wb", -1), R("rmb"), r("w1s", -1))
-
-        def decide2(h):
-            b = "BH%d" % h
-            lo, hi = 128 * h, 128 * h + 128
-
-            def r(n, step=1):
-                return R(n, lo, hi, step)
-            tt(r("r2"), r("nc"), R(b, 384, 512), A.mult)
-            tt(r("NE"), r("cap"), R(b, 256, 384), A.mult)
-            scan(r("n1"), R("rmf"), r("NE"))
-            scan(r("n2", -1), R("rmf"), r("n1", -1))
-            ts(r("Si"), r("n2"), 2.0 ** -12, A.mult, 0.5 - 2.0 ** -13, A.add)
-            tt(r("pS"), r("Si"), r("pm"), A.mult)
-            scan(r("k1"), R("rmf"), R(b, 128, 256))
-            scan(R(b, 128, 256, -1), R("rmf"), r("k1", -1))
-            tt(r("dpm"), r("pm"), R(b, 128, 256), A.mult)
-
-        for a, b in ((0, 64), (64, 256)):
-            cp(R("Ei", a, b), P("ind", R(tab[0], 0, tab[1]), R("lvu", a // 16, b // 16)))
-            ts(R("Ci", a, b), R("Ei", a, b), 4095, A.bitwise_and)
-            cp(R("CL", a, b), R("Ci", a, b))
-        tt(R("d0"), P("ind", R("XT"), R("lvu")), R(x), A.subtract)
-        for h in range(2):
-            mm(R("m0", 128 * h, 128 * h + 128), R(x, 128 * h, 128 * h + 128), R("IDb"))
-        act(R("xT"), R("m0", 0, 256), F.Copy)
-        act(R("z" + st), R("d0"), F.Abs)
-        send("z" + st, "zl" + st, (rank + 1 + t) % 4, "zs" + st, "za" + st)
-        for b0, b1 in CHUNKS:
-            G1(b0, b1)
-        if t == 0:
-            aff(R("PICK"), R("ONE"), [[-16, 8], [0, 128]], A.is_equal, 0.0, 0, 1)
-            more_constants()
-        ts(R("Ff"), R("Ei"), -4095.0, A.add)
-        ts(R("em"), R("Ci"), 4095.0, A.is_equal)
-        ts(R("Cm"), R("Ci"), -2048.0, A.add)
-        tt(R("Rm"), R("Ff"), R("npm"), A.mult)
-        cp(R("vA"), P("ind", R("IDX"), R("lvu")))
-        for h in range(2):
-            mm(R("m1", 8 * h, 8 * h + 8), R("vA", 128 * h, 128 * h + 128), R("PK8"))
-        ts(R("vcol"), R("m1", 0, 16), -1.0, A.mult)
-        bh_open(0)
-        bh_open(1)
-        if t == 0:
-            even_more()
-        for c, (b0, b1) in enumerate(CHUNKS):
-            for j in range(b0, b1):
-                sub(j)
-                if j in (3, 7):
-                    over(j // 4)
-                if j == 3:
-                    for u, w in ((256, "W1"), (272, "W2")):
-                        for m in range(16):
-                            mm(R("ov", u, u + 16), R(w, 128 * m, 128 * m + 128), R("zl" + st, m, 256, 16), m == 0, m == 15)
-                    hash_ops(R("ov", 256, 288), 16, "ru", "rp", R("rl"))
-                    act(R("yr" + st), P("ind", R("BK"), R("rl")), F.Copy)
-                    send("yr" + st, "yl" + st, (rank - 1 - t) % 4, "ys" + st, "ya" + st)
-            hashes(b0, b1, c)
-            if b1 in (4, 8):
-                scount(b1 // 4 - 1)
-        for q in range(8):
-            same(q)
-        decide(0)
-        decide2(0)
-        mm(R("dp0", 0, 256), R("IDb"), R("yl" + st), True, False)
-        mm(R("dp0", 0, 256), R("NIDb"), R(x), False, True)
-        act(R("rr"), R("dp0", 0, 256), F.Abs)
-        for m in range(16):
-            mm(R("up", 384, 400), R("W1", 128 * m, 128 * m + 128), R("rr", m, 256, 16), m == 0, m == 15)
-        cp(R("bi"), R("up", 384, 400))
-        ts(R("bk"), R("bi"), 1023, A.bitwise_and)
-        tt(R("bk2"), R("bk"), R(lv), A.subtract)
-        mm(R("dp0", 256, 512), R("IDb"), R("rr"), True, False)
-        mm(R("dp0", 256, 512), R("NIDb"), R(x), False, True)
-        act(R("rx"), R("dp0", 256, 512), F.Copy)
-        decide(1)
-        for hi in range(2):
-            for q in range(8):
-                o = 256 + 128 * hi + 16 * q
-                mm(R("ov", o, o + 16), R("MQ", 384 * q + 128 * hi, 384 * q + 128 * hi + 128), R("wb", 16 * q, 16 * q + 16), True, hi == 0)
-                if hi == 1:
-                    mm(R("ov", o, o + 16), R("MQ", 384 * q + 256, 384 * q + 384), R("wb", 128 + 16 * q, 144 + 16 * q), False, True)
-        decide2(1)
-        tt(R("winb"), R("ov", 256, 512), R("wb"), A.is_lt)
-        tt(R("winm"), R("ov", 256, 512), R("wm"), A.is_lt)
-        for h in range(2):
-            hs = (128 * h, 128 * h + 128)
-            mm(R("up", 320 + 8 * h, 328 + 8 * h), R("wm", *hs), R("G8"))
-            mm(R("up", 336 + 8 * h, 344 + 8 * h), R("dpm", *hs), R("G8f"))
-        for h in range(2):
-            mm(R("up", 352 + 8 * h, 360 + 8 * h), R("winm", 128 * h, 128 * h + 128), R("G8"))
-        for h in range(2):
-            hs = (128 * h, 128 * h + 128)
-            mm(R("dp1", *hs), R("winb", *hs), R("IDb"))
-        mm(R("m0", 0, 256), R("cI" + st), R("pm"), True, False)
-        mm(R("m0", 0, 256), R("IDb"), R("pmI"), False, False)
-        for h in range(2):
-            hs = (128 * h, 128 * h + 128)
-            mm(R("m0", *hs), R("r2", *hs), R("IDf"), False, False)
-            mm(R("m0", *hs), R("pS", *hs), R("I4K"), False, h == 1)
-        for h in range(2):
-            hs = (128 * h, 128 * h + 128)
-            mm(R("m1", *hs), R("NE", *hs), R("IDf"))
-        act(R("NEs"), R("m1", 0, 256), F.Copy)
-        tt(R("dp0", 0, 256), R("rx"), R("dp1", 0, 256), A.mult)
-        tt(R(xn), R("dp0", 0, 256), R(x), A.add)
-        act(R("newc"), R("m0", 0, 256), F.Identity, 4095.0)
-        tt(R("vt"), R(lv), R("trash"), A.subtract)
-        tt(R("of"), R("vt"), R("up", 352, 368), A.mult)
-        tt(R("of"), R("of"), R("trash"), A.add)
-        cp(R("ofu"), R("of"))
-        cp(P("ind", R("ET", 0, 2944), R("ofu")), R("newc"))
-        n0 = M + 256 * t
-        tt(R("XT", n0, n0 + 256), R(x), R("dp1", 0, 256), A.mult)
-        tt(R("NEw"), R("NEs"), R("dp1", 0, 256), A.mult)
-        act(R("ET", n0, n0 + 256), R("NEw"), F.Identity, 4095.0)
-        cp(R("dn"), R("up", 336, 352))
-        ts(R("dn"), R("dn"), 4095, A.bitwise_and)
-        tt(R("b1"), R(lv), R("dn"), A.subtract)
-        tt(R("b1"), R("b1"), R("up", 320, 336), A.mult)
-        tt(R("b1"), R("b1"), R("dn"), A.add)
-        tt(R("b2"), R("bk2"), R("up", 352, 368), A.mult)
-        tt(R(lvn), R("b1"), R("b2"), A.add)
-        if not last:
-            cp(R("lvu"), R(lvn))
+    def verdicts(u):
+        h = u % 2
+        if u in HASHA:
+            for e in range(2):
+                a, c, o = 2048 * h + 1024 * e, 128 * h + 64 * e, 128 * e
+                msum([(R("HB", o, o + 128), R("ONE", 0, 128), R("CH", 0, 128))] +
+                     [(R("HB", o + z, o + z + 64), R(w, 128 * k, 128 * k + 128), R("DD", a + k, a + 1024, 16)) for z, w in ((0, "W1"), (64, "W2")) for k in range(16)])
+                act(R("hr", 2 * c, 2 * c + 128), R("HB", o, o + 128), F.Identity, -2047.5)
+                u2 = R("HB", 256 + 64 * e, 320 + 64 * e)
+                tt(R("u1", c, c + 64), R("HB", o, o + 64), R("hr", 2 * c, 2 * c + 64), A.subtract)
+                tt(u2, R("HB", o + 64, o + 128), R("hr", 2 * c + 64, 2 * c + 128), A.subtract)
+                hp = R("hp", c, c + 64)
+                tt(hp, R("u1", c, c + 64), u2, A.mult)
+                if early(u):
+                    tt(R("HB", o, o + 64), R("fA", c, c + 64), u2, A.add)
+                    u2 = R("HB", o, o + 64)
+                ts(hp, hp, 5, A.arith_shift_right, 4095, A.bitwise_and)
+                tt(hp, hp, u2, A.add)
+                if u < TWICE:
+                    ts(hp, hp, 4095, A.bitwise_and)
+                ts(R("HL", c, c + 64), hp, 2.0 * H, A.min)
+                for z in range(a, a + 1024, CP):
+                    tt(R("CMP", z, z + CP), P(book(u), R("HL", z // 16, (z + CP) // 16)), R("DD", z, z + CP), A.is_ge)
+            if h == 1:
+                over(u)
+            return
+        msum([(R("HB", 0, 256), R("ONE", 0, 128), R("CH"))] +
+             [(R("HB", k, 256, 16), R("DD", 2048 * h + k, 2048 * h + 2048, 16), R("GWb")) for k in range(16)])
+        act(R("hr", 256 * h, 256 * h + 256), R("HB", 0, 256), F.Identity, -2047.5)
+        tt(r("u1", h), R("HB", 0, 128), R("hr", 256 * h, 256 * h + 128), A.subtract)
+        tt(R("HB", 256, 384), R("HB", 128, 256), R("hr", 256 * h + 128, 256 * h + 256), A.subtract)
+        tt(r("hp", h), r("u1", h), R("HB", 256, 384), A.mult)
+        ts(r("hp", h), r("hp", h), 5, A.arith_shift_right, 4095, A.bitwise_and)
+        tt(r("hf", h), r("hp", h), R("HB", 256, 384), A.add)
+        if u < TWICE:
+            ts(r("hg", h), r("hf", h), 4096.0, A.is_ge)
+            msum([(R("HB", 0, 128), r("hf", h), R("IDf")), (R("HB", 0, 128), r("hg", h), R("N4K"))])
         else:
-            dma("y", T.ykids[:], T.ET[:, 0:W], [R("ET", 0, W)], [])
-            dma("s", T.ycand[:], T[xn][:], [R(xn)], [])
-            dma("s", T.ynodes[:], T.XT[:, M:W], [R("XT", M, W)], [])
-            dma("s", T.yspot[:], T[lvn][:], [R(lvn)], [])
+            msum([(R("HB", 0, 128), r("hf", h), R("IDf"))] + ([(R("HB", 0, 128), ID, R("fA"))] if early(u) else []))
+        ts(r("HL", h), R("HB", 0, 128), 2.0 * H, A.min)
+        for a in range(2048 * h, 2048 * h + 2048, CP):
+            tt(R("CMP", a, a + CP), P(book(u), R("HL", a // 16, (a + CP) // 16)), R("DD", a, a + CP), A.is_ge)
+        if h == 1:
+            over(u)
+
+    def serve(u):
+        list_hash(u, r("zl", u), "m0", 256, "ru", "rp", "rl")
+        act(r("yo", u), P(book(u), R("rl")), F.Copy)
+        send(r("yo", u), r("yl", u), (rank - 1 - u // 2) % 4, "ys%d" % u, "ya%d" % u)
+
+    def answer(u):
+        t, h, x, xn, lv, lvn = names(u)
+        a = R("m0", 128, 256)
+        msum([(a, ID, r("yl", u)), (a, NID, r(x, h))])
+        act(r("rr", h), a, F.Abs)
+        msum([(a, ID, R("NM", 0, 128)), (a, R("BW", 0, 128), r("rr", h))])
+        scan(r("bw", h), RM, a)
+        ts(l("bi", h), ends("bw", h), 1023, A.bitwise_and)
+
+    def mend(u):
+        t, h, x, xn, lv, lvn = names(u)
+        tt(R("fd"), P(R("XW", 0, M + L), l("lvu", 0)), r(x, 0), A.subtract)
+        act(R("fD"), R("fd"), F.Abs)
+        n = 32 * SGN[u]
+        if n > 0:
+            ts(R("fS", 0, n), R("fd", 0, n), 0.0, A.is_le, 2.0, A.mult)
+        if n < 128:
+            act(R("fS", n, 128), R("fd", n, 128), F.Sign, 0.5, -1.0)
+        list_hash(u, R("fD"), "m2", 256, "fu", "fp", "fl")
+        tt(R("fC"), P(book(u), R("fl")), R("fD"), A.is_ge)
+        slots(u, R("CF"))
+        ts(R("fA"), R("CF"), M + 128.0 * (u - 1), A.is_ge, 2.0 * H, A.mult)
+        marks(u, R("CF"))
+        mm(R("m0", 0, 128), R("fA"), ID)
+        act(R("fr"), R("m0", 0, 128), F.Relu, 1.0, -1.0)
+
+    def counts(u):
+        h = u % 2
+        b = "BH%d" % h
+        q, ky = R("m2", 0, 256), R(b, 0, 256)
+
+        def sums(bank, lo, hi, c):
+            return [(R(bank, lo + k, hi, 16), R("CMP", 2048 * h + k, 2048 * h + 2048, 16), R("GS", c, c + (hi - lo) // 16)) for k in range(16)]
+        fq = [(q, ID, R("CT", 0, 256)), (q, r("Kb", h), R("DK")), (q, r("em", h), R("DE", 0, 256))]
+        fk = [(ky, ID, R("CT", 256, 512)), (R(b, 0, 128), R("ONE", 0, 128), R("CRK")), (ky, r("em", h), R("DE", 256, 512)), (R(b, 0, 128), r("Cm", h), ID)]
+        if early(u):
+            mm(R(b, 256, 384), R("fC"), R("NBD"))
+            tt(R("fs"), R("fr"), R(b, 256, 384), A.mult)
+            fq += [(q, R("fC"), R("BDQ", 0, 256)), (R("m2", 0, 128), ID, R("fs")), (R("m2", 128, 256), ID, R("fs"))]
+            fk += [(ky, R("fC"), R("BDQ", 256, 512)), (R(b, 0, 128), R("P64K"), R("fs")), (R(b, 128, 256), ID, R("fs"))]
+        msum(fq, True, False)
+        msum(fk, True, False)
+        msum(sums("m2", 0, 256, 0), False)
+        msum(sums(b, 0, 256, 16), False, False)
+
+    def decide(u):
+        t, h, x, xn, lv, lvn = names(u)
+        b = "BH%d" % h
+        n0 = M + 128 * u
+        tt(r("wm", h), R("m2", 128, 256), r("tA", h), A.is_gt)
+        tt(r("ncn", h), R("m2", 0, 128), r("tA", h), A.is_le)
+        mm(R("m2", 384, 400), r("wm", h), R("G8x"))
+        tt(l("lvw", h), l(lv, h), R("m2", 384, 392), A.subtract)
+        tt(l("b1", h), l(lv, h), R("m2", 392, 400), A.mult)
+        msum([(R(b, 0, 128), R("DB5"), r("ncn", h)), (R(b, 128, 256), N256, r("ncn", h)), (R(b, 128, 256), P256, r("wm", h))], False)
+        for c in range(8 * h, 8 * h + 8):
+            ts(R("EQ", 272 * c, 256 * c + 256), R("vA", 16 * c, 256), R("lvw", c, c + 1), A.subtract, 8192.0 - VO, A.is_equal)
+        scan(r("k1", h), RM, R(b, 0, 128))
+        act(r("sc", h), R(b, 128, 256), F.Relu)
+        scan(r("k2", h, -1), RM, r("k1", h, -1))
+        scan(r("s1", h), RM, r("sc", h))
+        scan(r("s2", h, -1), RM, r("s1", h, -1))
+        ta = R("m1", 0, 128)
+
+        def lower(c):
+            lo = max(128 * h, 16 * c + 16)
+            return (R("m1", lo - 128 * h, 128), R("BD2"), R("EQ", 256 * c + lo, 256 * c + 128 * h + 128))
+        msum([(ta, ID, R("C8"))] + [lower(c) for c in range(8 * h)], True, False)
+        msum([lower(c) for c in range(8 * h, 8 * h + 7)] +
+             [(R("m1", k, 128, 16), R("TRI", 128 * k, 128 * k + 128), R("EQ", 272 * 8 * h + k, 272 * 8 * (h + 1), 272)) for k in range(16)], False)
+        scan(r("tw", h), r("RT", h), ta, A.max, A.min)
+        act(r("win", h), ta, F.Relu, 1.0, -2.0 ** -13)
+        tw = ends("tw", h)
+        tt(l("of", h), l(lv, h), tw, A.max)
+        cp(l("ofu", h), l("of", h))
+        if early(u + 1):
+            cp(P(R("XW"), l("ofu", h)), r(x, h))
+        mm(R(b, 384, 512), r("ncn", h), ID)
+        kd = R(b, 256, 384)
+        msum([(kd, ID, R("NM", 0, 128)), (kd, r("wm", h), NB5), (kd, r("k2", h), R("IDf"))])
+        tt(r("A2", h), r("Ef", h), R(b, 384, 512), A.mult)
+        scan(r("k3", h), RM, kd)
+        ra = R(b, 128, 256)
+        msum([(ra, ID, r("II", h)), (ra, ID, r("PN", t)), (ra, r("s2", h), R("I4K"))])
+        tt(r("A1", h), R("N4"), ra, A.max)
+        tt(P(R("ET"), l("ofu", h)), r("A1", h), r("A2", h), A.add)
+        ts(l("dn", h), ends("k3", h), 4095, A.bitwise_and)
+        tt(l("b1", h), l("b1", h), l("dn", h), A.add)
+        tt(l("b2", h), l("bi", h), tw, A.subtract)
+        tt(l("b1", h), l("b1", h), tw, A.min)
+        tt(l(lvn, h), l("b1", h), l("b2", h), A.max)
+        if t < STEPS - 1:
+            cp(l("lvu", h), l(lvn, h))
+        na, y1, y2, y3 = R("m1", 128, 256), R("m1", 256, 384), R("m1", 384, 512), R(b, 0, 128)
+        msum([(y2, ID, r("rr", h)), (y2, R("BDW", 0, 128), r("win", h))])
+        msum([(y1, ID, r(x, h)), (y1, R("BDW", 0, 128), r("win", h))])
+        msum([(na, ID, r("Cm", h)), (na, r("sc", h), R("I4K")), (na, R("BDW", 256, 384), r("win", h))])
+        act(r("rw", h), y2, F.Relu, -256.0)
+        act(R("XT", n0, n0 + 128), y1, F.Relu, -256.0)
+        ts(R("ET", n0, n0 + 128) if t == 0 else r("EN", u - 2), na, 2048.0 - B5, A.add, 4095.0, A.max)
+        msum([(y3, ID, r(x, h)), (y3, R("BDW", 128, 256), r("win", h))])
+        tt(r(xn, h), r("rw", h), y3, A.max)
+
+    head(0)
+    head(1)
+    bulk(0)
+    for a in range(0, M, 448):
+        if CONV == "v":
+            cp(R("ET", a, a + 448), R("KI", a, a + 448))
+        else:
+            aff(R("ET", a, a + 448), R("KI", a, a + 448), [[0, 448]], A.is_ge, 0.0, 0, 0)
+    for u in range(UNITS):
+        serve(u)
+        if u + 1 < UNITS and (u % 2 == 0 or early(u + 1)):
+            bulk(u + 1)
+        if early(u):
+            mend(u)
+        if u % 2 == 0:
+            verdicts(u)
+            verdicts(u + 1)
+        if u % 2 == 0:
+            over(u)
+        counts(u)
+        answer(u)
+        decide(u)
+        if u + 2 < UNITS and early(u + 2):
+            head(u + 2)
+        if u + 2 < UNITS and u % 2 == 1:
+            if not early(u + 1):
+                head(u + 1)
+                bulk(u + 1)
+            head(u + 2)
+    xn, lvn = "x%d" % (STEPS % 2), "lv%d" % (STEPS % 2)
+    dma("y", T.ykids[:, M + L:W - 128], T.EN[:, 0:384], [R("EN", 0, 384)], [])
+    dma("y", T.ynodes[:, 0:640], T.XT[:, M:W - 128], [R("XT", M, W - 128)], [])
+    dma("y", T.ykids[:, 0:M + L], T.ET[:, 0:M + L], [R("ET", 0, M + L)], [])
+    dma("s", T.ykids[:, W - 128:W], T.EN[:, 384:512], [R("EN", 384, 512)], [])
+    dma("s", T.ynodes[:, 640:768], T.XT[:, W - 128:W], [R("XT", W - 128, W)], [])
+    dma("s", T.yspot[:], T[lvn][:], [R(lvn)], [])
+    dma("s", T.ycand[:], T[xn][:], [R(xn)], [])
 
     finish()

@@ -13,18 +13,18 @@ SB = {
     "XT": (W + 16, "bfloat16"), "BK": (2 * H + 16, "bfloat16"), "fA": (128, "bfloat16"), "ET": (W + 384, "float32"), "EN": (2 * L, "float32"), "KI": (M, "int32"), "IDX": (2304, "float32"), "XW": (W + 384, "bfloat16"),
     "ONE": (1024, "bfloat16"), "IDb": (128, "bfloat16"), "NIDb": (128, "bfloat16"), "IDf": (128, "float32"),
     "G8t": (8, "bfloat16"), "G8": (8, "bfloat16"), "G8f": (8, "float32"), "G8x": (16, "bfloat16"), "GW": (16, "float32"), "GWb": (16, "bfloat16"),
-    "W1": (2048, "bfloat16"), "W2": (2048, "bfloat16"), "BW": (256, "bfloat16"), "NM": (256, "bfloat16"), "ruw": (256, "int32"), "fuw": (256, "int32"), "bw": (256, "int32"), "GS": (32, "bfloat16"), "GO": (8, "bfloat16"), "tb": (UNITS, "float32"),
+    "W1": (2048, "bfloat16"), "W2": (2048, "bfloat16"), "BW": (256, "bfloat16"), "NM": (256, "bfloat16"), "ruw": (256, "int32"), "fuw": (256, "int32"), "bw": (256, "int32"), "GS": (32, "bfloat16"), "GO": (8, "bfloat16"), "BG": (1024, "bfloat16"),
     "REP": (2048, "bfloat16"), "TRI": (2048, "bfloat16"), "BDt": (128, "bfloat16"), "BD": (128, "bfloat16"), "NBD": (128, "bfloat16"), "BD2": (128, "bfloat16"),
     "BDQ": (512, "bfloat16"), "BDW": (640, "bfloat16"), "Ck": (32, "float32"), "pms": (128, "bfloat16"), "pm": (128, "bfloat16"),
-    "CT": (512, "bfloat16"), "CRK": (128, "bfloat16"), "CH": (256, "bfloat16"), "C8": (128, "bfloat16"), "DK": (256, "bfloat16"), "DE": (512, "bfloat16"),
-    "DB5": (128, "bfloat16"), "D256": (128, "bfloat16"), "I4K": (128, "bfloat16"), "N4K": (128, "bfloat16"), "P64K": (128, "bfloat16"),
+    "CT": (512, "bfloat16"), "CRK": (128, "bfloat16"), "CH": (128, "bfloat16"), "C8": (128, "bfloat16"), "DK": (256, "bfloat16"), "DE": (512, "bfloat16"),
+    "DB5": (128, "bfloat16"), "D256": (128, "bfloat16"), "I4K": (128, "bfloat16"), "P64K": (128, "bfloat16"),
     "II": (256, "bfloat16"), "PN": (128 * STEPS, "bfloat16"), "N4": (128, "float32"), "rm": (256, "bfloat16"), "trash": (16, "float32"), "RT": (256, "float32"),
     "wt": (2, "bfloat16"), "sp": (16, "int32"), "x0": (256, "bfloat16"), "x1": (256, "bfloat16"), "lv0": (16, "float32"), "lv1": (16, "float32"),
     "lvu": (16, "uint16"), "lvw": (16, "float32"),
     "Ef": (256, "float32"), "Kb": (256, "bfloat16"), "CL": (256, "uint16"), "CF": (128, "uint16"), "em": (256, "bfloat16"), "Cm": (256, "float16"),
     "vA": (256, "float16"), "xT": (256, "bfloat16"), "d0": (256, "bfloat16"),
     "XG": (4096, "bfloat16"), "DD": (4096, "bfloat16"), "SG": (4096, "bfloat16"), "CMP": (4096, "bfloat16"), "EQ": (4352, "bfloat16"), "HL": (256, "uint16"),
-    "hr": (512, "bfloat16"), "u1": (256, "float32"), "hp": (256, "int32"), "hf": (256, "float32"), "hg": (256, "bfloat16"),
+    "hr": (512, "bfloat16"), "u1": (256, "float32"), "hp": (256, "int32"), "hq": (68, "float32"),
     "ru": (16, "int32"), "rp": (8, "int32"), "rl": (8, "uint16"), "fu": (16, "int32"), "fp": (8, "int32"), "fl": (8, "uint16"),
     "fd": (128, "bfloat16"), "fD": (128, "bfloat16"), "fS": (128, "bfloat16"), "fC": (128, "bfloat16"), "fr": (128, "bfloat16"), "fo": (128, "bfloat16"), "fs": (128, "bfloat16"),
     "tA": (256, "bfloat16"), "ncn": (256, "bfloat16"), "wm": (256, "bfloat16"), "sc": (256, "bfloat16"), "s1": (256, "bfloat16"), "s2": (256, "bfloat16"),
@@ -35,7 +35,7 @@ SB = {
 }
 PS = ["dp0", "dp1", "HB", "m0", "BH0", "BH1", "m1", "m2"]
 INORDER = ("BH0", "BH1", "m1", "m2")
-SCRATCH = {k: ("sbuf", [128, n], d) for k, (n, d) in SB.items() if k not in ("hf", "hg")}
+SCRATCH = {k: ("sbuf", [128, n, 8] if k == "hq" else [128, n], d) for k, (n, d) in SB.items()}
 for _n in PS:
     SCRATCH[_n] = ("psum", [128, 512], "float32")
 NDMA = 15
@@ -43,13 +43,13 @@ SEMAPHORES = ["qv", "qs", "qt", "qg"] + ["D%d" % i for i in range(NDMA)] + [n + 
 
 TWICE = 1
 SGN = (4, 0, 2, 0, 2, 0)
-XGV = ((2, 3), (), (), (), (), ())
-AGAIN = ((), (2, 3), (), (2, 3), (), (2, 3))
+XGV = ((1, 3), (), (1,), (), (1,), ())
+AGAIN = ((), (1, 3), (), (1, 3), (), ())
+BKS = ((), (1, 3), (), (1, 3), (), (1, 3))
 EARLY = (2, 4)
-HASHA = (0, 1, 2, 3, 4, 5)
+HASHA = ()
 GP = 512
 CP = 512
-CONV = "v"
 
 ORDER = {}
 CYC = 0.83e-3
@@ -60,7 +60,8 @@ FLIGHT = 4.0
 FIRST = 2.0
 DMA0 = 2.0
 DMARATE = 2.5e5
-ROUNDS = 1000
+TURN = 0.05
+ROUNDS = 1200
 SWAPS = 12000
 
 
@@ -80,7 +81,7 @@ def schedule(nodes):
                 bank = r[0] in INORDER
                 for (j, rj, wj) in hist.get(r[0], ()):
                     ov = overlap(r, rj)
-                    same = nodes[j][1] == q and kind == "c" and nodes[j][0] == "c"
+                    same = nodes[j][1] == q and kind == "c" and nodes[j][0] == "c" and not sem and not nodes[j][6]
                     if bank and (q == "t" or not same):
                         full = not same
                     elif same and q == "t" and r[0] not in PS:
@@ -110,6 +111,12 @@ def schedule(nodes):
     first = min(i for i in range(n) if nodes[i][0] == "r")
     hold = [nodes[i][5] if nodes[i][0] == "c" else (0.1 if nodes[i][0] == "d" else 0.8) for i in range(n)]
     last = [nodes[i][5] + (FIRST if i == first else 0.0) for i in range(n)]
+    que = [nodes[i][1] for i in range(n)]
+    free_ones = [i for i in range(n) if nodes[i][0] == "c" and nodes[i][6]]
+
+    def flip(i):
+        q, c = (nodes[i][6][0], nodes[i][6][2]) if que[i] == nodes[i][1] else (nodes[i][1], nodes[i][5])
+        que[i], hold[i], last[i] = q, c, c
     moved = DMA0
     for i in loads:
         if nodes[i][4]:
@@ -140,7 +147,7 @@ def schedule(nodes):
             e = min(ready)
             ready.remove(e)
             i = e[1]
-            q, t, h = nodes[i][1], est[i], hold[i]
+            q, t, h = que[i], est[i], hold[i]
             own = busy.setdefault(q, [])
             shared = [busy.setdefault(b, []) for b in banks[i]]
             t0 = -1.0
@@ -180,23 +187,32 @@ def schedule(nodes):
     for i in range(n - 1, -1, -1):
         rank[i] = min([-last[i]] + [rank[k] - gap(i, f) for k, f in succ[i]])
     span, rank, at = settle(rank)
-    best = (span, at)
+    best = (span, at, list(que))
     for _ in range(ROUNDS):
         lo, wide, far, part = -span * draw(), 3 + 17 * draw(), 0.5 * 8 ** draw(), 0.1 * 10 ** draw()
+        turned = [i for i in free_ones if lo - wide <= rank[i] < lo and draw() < TURN]
+        for i in turned:
+            flip(i)
         s2, r2, at = settle([a + far * (draw() + draw() - 1) * 2 if lo - wide <= a < lo and draw() < part else a for a in rank])
+        if s2 < best[0]:
+            best = (s2, at, list(que))
         if s2 <= span + 0.15:
             span, rank = s2, r2
-        if s2 < best[0]:
-            best = (s2, at)
-
+        else:
+            for i in turned:
+                flip(i)
+    for i in free_ones:
+        if que[i] != best[2][i]:
+            flip(i)
 
     def run(order):
         at, why, free, held = [0.0] * n, [None] * n, {}, {}
         for i in order:
-            t, w, q = 0.0, None, nodes[i][1]
-            for k, d in after[i]:
-                if at[k] + d > t:
-                    t, w = at[k] + d, (k, False)
+            t, w, q = 0.0, None, que[i]
+            for k, f in preds[i]:
+                e = at[k] + last[k] + WAKE if f else at[k] + gap(k, f)
+                if e > t:
+                    t, w = e, (k, False)
             if q in free and free[q][0] > t:
                 t, w = free[q][0], (free[q][1], True)
             for b in banks[i]:
@@ -209,7 +225,6 @@ def schedule(nodes):
                 held[b][q] = free[q]
         j = max(range(n), key=lambda k: at[k] + last[k])
         return at[j] + last[j], at, why, j
-    after = [[(k, gap(k, f)) for k, f in preds[i]] for i in range(n)]
     needs = [set(k for k, f in preds[i]) for i in range(n)]
     order = sorted(range(n), key=lambda i: (best[1][i], i))
     span, at, why, j = run(order)
@@ -220,6 +235,17 @@ def schedule(nodes):
                 pairs.append((why[k][0], k))
             k = why[k][0]
         a, b = pairs[int(draw() * len(pairs))]
+        bound = span - (0.1 * (1 - step / SWAPS) + 0.01) * math.log(draw() + 1e-9)
+        if nodes[a][0] == "c" and nodes[a][6] and draw() < 0.3:
+            flip(a)
+            s2, at, w2, j2 = run(order)
+            if s2 < best[0]:
+                best = (s2, at, list(que))
+            if s2 <= bound:
+                span, why, j = s2, w2, j2
+            else:
+                flip(a)
+            continue
         more = (0, 0, 0, 3, 10)[int(draw() * 5)]
         pa, pb = order.index(a), order.index(b)
         if draw() < 0.5:
@@ -241,11 +267,15 @@ def schedule(nodes):
             first = set(part) - late
         other = order[:pa] + [k for k in part if k in first] + [k for k in part if k not in first] + order[pb + 1:]
         s2, at, w2, j2 = run(other)
-        if s2 <= span - (0.1 * (1 - step / SWAPS) + 0.01) * math.log(draw() + 1e-9):
+        if s2 <= bound:
             order, span, why, j = other, s2, w2, j2
             if s2 < best[0]:
-                best = (s2, at)
-    ORDER["plan"] = (best, preds, hold, last, banks)
+                best = (s2, at, list(que))
+    for i in free_ones:
+        if que[i] != best[2][i]:
+            flip(i)
+    ORDER["plan"] = (best[:2], preds, hold, last, banks)
+    ORDER["queues"] = que
     return sorted(range(n), key=lambda i: (best[1][i], i))
 
 
@@ -269,6 +299,8 @@ def rank_program(g, core, T, topo):
         if r[0] == "ind":
             return ap(r[1]).indirect(ap(r[2]))
         name, lo, hi, step, p1 = r
+        if name == "hq":
+            return T.hq[:, lo:hi:step, :]
         if step == -1:
             return T[name][:, hi - 1:(lo - 1 if lo > 0 else None):-1]
         if p1 != 128:
@@ -352,6 +384,8 @@ def rank_program(g, core, T, topo):
         for i in order:
             kind, q, fn, reads, writes, cost, sem = nodes[i]
             if kind == "c":
+                if ORDER["queues"][i] != q:
+                    q, fn = sem[:2]
                 deps(q, q, reads, writes)
                 name = "q" + q
                 for f in fn:
@@ -379,7 +413,7 @@ def rank_program(g, core, T, topo):
             count[sem + str(u)] = NENG
 
     def width(r):
-        return 16 * width(r[2]) if r[0] == "ind" else -((r[1] - r[2]) // abs(r[3]))
+        return 16 * width(r[2]) if r[0] == "ind" else -((r[1] - r[2]) // abs(r[3])) * (8 if r[0] == "hq" else 1)
 
     def dtype_of(r):
         return "float32" if r[0] in PS else SB[r[0]][1]
@@ -428,6 +462,25 @@ def rank_program(g, core, T, topo):
         b = bias if isinstance(bias, (int, float)) else ap(bias)
         s = scale if isinstance(scale, (int, float)) else ap(scale)
         emit("s", lambda: S.activation(ap(out), ap(a), f, bias=b, scale=s), [a] + cols, [out], vcost(out, [a], 0))
+
+    def reached(out, a):
+        act(out, a, F.Sigmoid, 500.0, 1000.0)
+
+    def either(second=False):
+        b, a = nodes.pop(), nodes.pop()
+        if second:
+            a, b = b, a
+        nodes.append(a[:6] + ((b[1], b[2], b[5]),))
+
+    def move(out, a, bias=0.0, relu=False, v=False):
+        act(out, a, F.Relu if relu else (F.Identity if bias else F.Copy), bias)
+        if relu:
+            ts(out, a, bias, A.add, 0.0, A.max)
+        elif bias:
+            ts(out, a, bias, A.add)
+        else:
+            cp(out, a)
+        either(v)
 
     def mms(calls):
         fns, cost = [], 0.0
@@ -481,6 +534,7 @@ def rank_program(g, core, T, topo):
     gfill("XW", 0, M + L, 0)
     fill(R("XT", M, W + 16), 0.0)
     fill(R("CH"), MK / 128)
+    fill(R("hq"), 0.0)
     fill(R("BK", 2 * H, 2 * H + 16), -1.0)
     ts(NID, ID, -1.0, A.mult)
     cp(R("IDf"), ID)
@@ -498,14 +552,10 @@ def rank_program(g, core, T, topo):
         ts(R("GWb", 8 * j, 8 * j + 8), R("G8"), R("wt", j, j + 1), A.mult)
         ts(R("BW", 128 * j, 128 * j + 128), R("BD"), R("wt", j, j + 1), A.mult)
     for name, lo, c in (("DK", 0, -2.0 ** -12), ("DK", 128, -2.0 ** -12), ("DE", 0, -256.0), ("DE", 128, 1024.0), ("DE", 256, -B5), ("DE", 384, -256.0),
-                        ("D256", 0, 256.0), ("DB5", 0, B5), ("I4K", 0, 4096.0), ("N4K", 0, -4096.0), ("P64K", 0, 65536.0)):
+                        ("D256", 0, 256.0), ("DB5", 0, B5), ("I4K", 0, 4096.0), ("P64K", 0, 65536.0)):
         ts(R(name, lo, lo + 128), ID, c, A.mult)
-    for name, lo, c in (("GS", 0, 1.0), ("GS", 8, 1.0), ("GS", 16, 65536.0), ("GS", 24, 1.0), ("GO", 0, -32.0), ("G8x", 0, 8192.0), ("G8x", 8, 1.0)):
+    for name, lo, c in (("GS", 0, 1.0), ("GS", 8, 1.0), ("GS", 16, 65536.0), ("GS", 24, 1.0), ("GO", 0, -64.0), ("G8x", 0, 8192.0), ("G8x", 8, 1.0)):
         ts(R(name, lo, lo + 8), R("G8"), c, A.mult)
-    fill(R("tb"), 224.0)
-    for u in range(UNITS):
-        if SGN[u]:
-            fill(R("tb", u, u + 1, 1, 32 * SGN[u]), 736.0)
     tt(R("pms", 0, 64), R("IDb", 0, 64), R("IDb", 64, 128), A.add)
     tt(R("pms", 64, 96), R("pms", 0, 32), R("pms", 32, 64), A.add)
     tt(R("pm", 0, 16), R("pms", 64, 80), R("pms", 80, 96), A.add)
@@ -514,12 +564,13 @@ def rank_program(g, core, T, topo):
     for name, lo, a, b in (("CT", 0, 2048.0, 192.0), ("CT", 128, 2048.0, -1856.0), ("CT", 256, B5, -B5), ("CT", 384, -256.0, 0.0),
                            ("N4", 0, -4095.0, 4095.0), ("NM", 0, B5, -B5), ("NM", 128, B5, -B5), ("C8", 0, -8192.0, 16384.0)) + tuple(("PN", 128 * t, M + 256.0 * t + 2 ** 17, -2.0 ** 17) for t in range(STEPS)):
         ts(R(name, lo, lo + 128), R("pm"), a, A.mult, b, A.add)
-    fill(R("rm"), 1.0)
-    ts(R("rm", 0, 256, 16), R("ONE", 0, 16), 0.0, A.mult)
+    iota(R("rm"), [[0, 16], [1, 16]], -1, 0)
+    reached(R("rm"), R("rm"))
+    nodes[-1] = nodes[-1][:5] + (nodes[-1][5] + 1.3, None)
     fill(R("RT"), -1.0)
     cp(R("RT", 0, 256, 16), R("trash"))
     for name, lo, c in (("BD2", 0, 16384.0), ("NBD", 0, -1.0), ("BDQ", 0, 1.0), ("BDQ", 128, 1.0), ("BDQ", 256, 65536.0), ("BDQ", 384, 1.0),
-                        ("BDW", 0, 256.0), ("BDW", 128, -256.0), ("BDW", 256, B5), ("BDW", 384, 32.0), ("BDW", 512, -32.0)):
+                        ("BDW", 0, 256.0), ("BDW", 128, -256.0), ("BDW", 256, B5), ("BDW", 384, 64.0), ("BDW", 512, -64.0)):
         ts(R(name, lo, lo + 128), R("BD"), c, A.mult)
     scan(R("Ck", 0, 16), R("ONE", 0, 16), R("pm", 0, 16))
     ts(R("Ck", 16, 32), R("pm", 0, 16), -1.5, A.mult)
@@ -556,11 +607,8 @@ def rank_program(g, core, T, topo):
 
     def slots(u, out):
         t, h = u // 2, u % 2
-        if t == 0:
-            ts(r("Ef", h), P(R("KI"), l("lvu", h)), -4095.0, A.add)
-        else:
-            act(r("Ef", h), P(R("ET", 0, M + 256 * (t - 1)), l("lvu", h)), F.Identity, -4095.0)
-        act(r("Kb", h), r("Ef", h), F.Identity, MK + 2047.5)
+        move(r("Ef", h), P(R("KI") if t == 0 else R("ET", 0, M + 256 * (t - 1)), l("lvu", h)), -4095.0)
+        move(r("Kb", h), r("Ef", h), MK + 2047.5, v=True)
         msum([(R("m0", 0, 128), R("IDf"), r("Ef", h)), (R("m0", 0, 128), NID, r("Kb", h))])
         ts(out, R("m0", 0, 128), MK + 4095.0, A.add, float(W), A.min)
 
@@ -576,13 +624,13 @@ def rank_program(g, core, T, topo):
         t, h, x, xn, lv, lvn = names(u)
         slots(u, r("CL", h))
         mm(R("m0", 128, 256), r(x, h), ID)
-        act(r("xT", h), R("m0", 128, 256), F.Copy)
+        move(r("xT", h), R("m0", 128, 256), v=h == 1)
         tt(r("d0", h), P(R("XT"), l("lvu", h)), r(x, h), A.subtract)
         act(r("zo", u), r("d0", h), F.Abs)
         send(r("zo", u), r("zl", u), (rank + 1 + t) % 4, "zs%d" % u, "za%d" % u)
         if not early(u):
             marks(u, r("CL", h))
-        cp(r("vA", h), P(R("IDX"), l("lvu", h)))
+        move(r("vA", h), P(R("IDX"), l("lvu", h)))
 
     def over(u):
         h = u % 2
@@ -595,16 +643,13 @@ def rank_program(g, core, T, topo):
             msum([(ov, R("fS"), R("BDW", 512, 640)), (ov, ID, R("fo"))])
         else:
             mms([c + (True, True) for c in sums])
-        act(r("tA", h), ov, F.Relu, R("tb", u, u + 1))
+        move(r("tA", h), ov, 736.0, True)
 
     def bulk(u):
         h = u % 2
         for a in range(2048 * h, 2048 * h + 2048, GP):
             children = P(R("XT"), R("CL", a // 16, (a + GP) // 16))
-            if (a // 512) % 4 in XGV[u]:
-                cp(R("XG", a, a + GP), children)
-            else:
-                act(R("XG", a, a + GP), children, F.Copy)
+            move(R("XG", a, a + GP), children, v=(a // 512) % 4 in XGV[u])
 
         def sub(j):
             b = R("dp%d" % (j % 2))
@@ -612,10 +657,9 @@ def rank_program(g, core, T, topo):
             return b
 
         def sign(j, b):
-            if j % 4 < SGN[u]:
-                ts(R("SG", 512 * j, 512 * j + 512), b, 0.0, A.is_ge, 2.0, A.mult)
-            else:
-                act(R("SG", 512 * j, 512 * j + 512), b, F.Sign, 0.5, 1.0)
+            reached(R("SG", 512 * j, 512 * j + 512), b)
+            ts(R("SG", 512 * j, 512 * j + 512), b, 0.0, A.is_ge)
+            either(j % 4 < SGN[u])
         for j in range(4 * h, 4 * h + 4):
             b = sub(j)
             act(R("DD", 512 * j, 512 * j + 512), b, F.Abs)
@@ -626,52 +670,57 @@ def rank_program(g, core, T, topo):
 
     def verdicts(u):
         h = u % 2
-        if u in HASHA:
-            for e in range(2):
-                a, c, o = 2048 * h + 1024 * e, 128 * h + 64 * e, 128 * e
-                msum([(R("HB", o, o + 128), R("ONE", 0, 128), R("CH", 0, 128))] +
-                     [(R("HB", o + z, o + z + 64), R(w, 128 * k, 128 * k + 128), R("DD", a + k, a + 1024, 16)) for z, w in ((0, "W1"), (64, "W2")) for k in range(16)])
-                act(R("hr", 2 * c, 2 * c + 128), R("HB", o, o + 128), F.Identity, -2047.5)
-                u2 = R("HB", 256 + 64 * e, 320 + 64 * e)
-                tt(R("u1", c, c + 64), R("HB", o, o + 64), R("hr", 2 * c, 2 * c + 64), A.subtract)
-                tt(u2, R("HB", o + 64, o + 128), R("hr", 2 * c + 64, 2 * c + 128), A.subtract)
-                hp = R("hp", c, c + 64)
-                tt(hp, R("u1", c, c + 64), u2, A.mult)
+        for e in range(2):
+            a, c, o = 2048 * h + 1024 * e, 128 * h + 64 * e, 128 * e
+            if u in HASHA:
+                sums = [(R("HB", o + z, o + z + 64), R(w, 128 * k, 128 * k + 128), R("DD", a + k, a + 1024, 16)) for z, w in ((0, "W1"), (64, "W2")) for k in range(16)]
+            else:
+                sums = [(R("HB", o + k, o + 128, 8), R("DD", a + k, a + 1024, 8), R("GWb")) for k in range(8)]
+            msum([(R("HB", o, o + 128), R("ONE", 0, 128), R("CH"))] + sums)
+            move(R("hr", 2 * c, 2 * c + 128), R("HB", o, o + 128), -2047.5, v=h == 0)
+            u2 = R("HB", 256 + 64 * e, 320 + 64 * e)
+            tt(R("u1", c, c + 64), R("HB", o, o + 64), R("hr", 2 * c, 2 * c + 64), A.subtract)
+            tt(u2, R("HB", o + 64, o + 128), R("hr", 2 * c + 64, 2 * c + 128), A.subtract)
+            hp = R("hp", c, c + 64)
+            tt(hp, R("u1", c, c + 64), u2, A.mult)
+            ts(hp, hp, 5, A.arith_shift_right, 4095, A.bitwise_and)
+            if u in HASHA:
                 if early(u):
                     tt(R("HB", o, o + 64), R("fA", c, c + 64), u2, A.add)
                     u2 = R("HB", o, o + 64)
-                ts(hp, hp, 5, A.arith_shift_right, 4095, A.bitwise_and)
                 tt(hp, hp, u2, A.add)
                 if u < TWICE:
                     ts(hp, hp, 4095, A.bitwise_and)
                 ts(R("HL", c, c + 64), hp, 2.0 * H, A.min)
-                for z in range(a, a + 1024, CP):
-                    tt(R("CMP", z, z + CP), P(book(u), R("HL", z // 16, (z + CP) // 16)), R("DD", z, z + CP), A.is_ge)
-            if h == 1:
-                over(u)
-            return
-        msum([(R("HB", 0, 256), R("ONE", 0, 128), R("CH"))] +
-             [(R("HB", k, 256, 16), R("DD", 2048 * h + k, 2048 * h + 2048, 16), R("GWb")) for k in range(16)])
-        act(R("hr", 256 * h, 256 * h + 256), R("HB", 0, 256), F.Identity, -2047.5)
-        tt(r("u1", h), R("HB", 0, 128), R("hr", 256 * h, 256 * h + 128), A.subtract)
-        tt(R("HB", 256, 384), R("HB", 128, 256), R("hr", 256 * h + 128, 256 * h + 256), A.subtract)
-        tt(r("hp", h), r("u1", h), R("HB", 256, 384), A.mult)
-        ts(r("hp", h), r("hp", h), 5, A.arith_shift_right, 4095, A.bitwise_and)
-        tt(r("hf", h), r("hp", h), R("HB", 256, 384), A.add)
-        if u < TWICE:
-            ts(r("hg", h), r("hf", h), 4096.0, A.is_ge)
-            msum([(R("HB", 0, 128), r("hf", h), R("IDf")), (R("HB", 0, 128), r("hg", h), R("N4K"))])
-        else:
-            msum([(R("HB", 0, 128), r("hf", h), R("IDf"))] + ([(R("HB", 0, 128), ID, R("fA"))] if early(u) else []))
-        ts(r("HL", h), R("HB", 0, 128), 2.0 * H, A.min)
-        for a in range(2048 * h, 2048 * h + 2048, CP):
-            tt(R("CMP", a, a + CP), P(book(u), R("HL", a // 16, (a + CP) // 16)), R("DD", a, a + CP), A.is_ge)
+            else:
+                z = 17 * (2 * h + e)
+                if u < TWICE:
+                    tt(hp, hp, u2, A.add)
+                    ts(hp, hp, 4095, A.bitwise_and)
+                    cp(R("hq", z + 1, z + 17, 2), hp)
+                else:
+                    tt(R("hq", z + 1, z + 17, 2), hp, u2, A.add)
+                ht = R("HB", o, o + 64)
+                msum(([(ht, ID, R("fA", c, c + 64))] if early(u) else []) +
+                     [(ht, R("hq", z + 1, z + 17), R("IDf", 0, 128, 2)), (ht, R("hq", z, z + 16), R("IDf", 1, 128, 2))])
+                ts(R("HL", c, c + 64), ht, 2.0 * H, A.min)
+            for z in range(a, a + 1024, 512):
+                column, j = P(book(u), R("HL", z // 16, z // 16 + 32)), z // 512
+                if j % 4 in BKS[u]:
+                    bg, b = R("BG", 512 * (j % 2), 512 * (j % 2) + 512), R("dp%d" % (j % 2))
+                    act(bg, column, F.Copy)
+                    msum([(b, NID, R("DD", z, z + 512)), (b, ID, bg)])
+                    reached(R("CMP", z, z + 512), b)
+                    ts(R("CMP", z, z + 512), b, 0.0, A.is_ge)
+                    either()
+                else:
+                    tt(R("CMP", z, z + 512), column, R("DD", z, z + 512), A.is_ge)
         if h == 1:
             over(u)
 
     def serve(u):
         list_hash(u, r("zl", u), "m0", 256, "ru", "rp", "rl")
-        act(r("yo", u), P(book(u), R("rl")), F.Copy)
+        move(r("yo", u), P(book(u), R("rl")))
         send(r("yo", u), r("yl", u), (rank - 1 - u // 2) % 4, "ys%d" % u, "ya%d" % u)
 
     def answer(u):
@@ -687,11 +736,7 @@ def rank_program(g, core, T, topo):
         t, h, x, xn, lv, lvn = names(u)
         tt(R("fd"), P(R("XW", 0, M + L), l("lvu", 0)), r(x, 0), A.subtract)
         act(R("fD"), R("fd"), F.Abs)
-        n = 32 * SGN[u]
-        if n > 0:
-            ts(R("fS", 0, n), R("fd", 0, n), 0.0, A.is_le, 2.0, A.mult)
-        if n < 128:
-            act(R("fS", n, 128), R("fd", n, 128), F.Sign, 0.5, -1.0)
+        ts(R("fS"), R("fd"), 0.0, A.is_le)
         list_hash(u, R("fD"), "m2", 256, "fu", "fp", "fl")
         tt(R("fC"), P(book(u), R("fl")), R("fD"), A.is_ge)
         slots(u, R("CF"))
@@ -699,6 +744,8 @@ def rank_program(g, core, T, topo):
         marks(u, R("CF"))
         mm(R("m0", 0, 128), R("fA"), ID)
         act(R("fr"), R("m0", 0, 128), F.Relu, 1.0, -1.0)
+        ts(R("fr"), R("m0", 0, 128), 1.0, A.is_lt)
+        either()
 
     def counts(u):
         h = u % 2
@@ -732,7 +779,7 @@ def rank_program(g, core, T, topo):
         for c in range(8 * h, 8 * h + 8):
             ts(R("EQ", 272 * c, 256 * c + 256), R("vA", 16 * c, 256), R("lvw", c, c + 1), A.subtract, 8192.0 - VO, A.is_equal)
         scan(r("k1", h), RM, R(b, 0, 128))
-        act(r("sc", h), R(b, 128, 256), F.Relu)
+        move(r("sc", h), R(b, 128, 256), 0.0, True)
         scan(r("k2", h, -1), RM, r("k1", h, -1))
         scan(r("s1", h), RM, r("sc", h))
         scan(r("s2", h, -1), RM, r("s1", h, -1))
@@ -742,10 +789,13 @@ def rank_program(g, core, T, topo):
             lo = max(128 * h, 16 * c + 16)
             return (R("m1", lo - 128 * h, 128), R("BD2"), R("EQ", 256 * c + lo, 256 * c + 128 * h + 128))
         msum([(ta, ID, R("C8"))] + [lower(c) for c in range(8 * h)], True, False)
-        msum([lower(c) for c in range(8 * h, 8 * h + 7)] +
-             [(R("m1", k, 128, 16), R("TRI", 128 * k, 128 * k + 128), R("EQ", 272 * 8 * h + k, 272 * 8 * (h + 1), 272)) for k in range(16)], False)
+        msum([lower(c) for c in range(8 * h, 8 * h + 4)], False, False)
+        msum([lower(c) for c in range(8 * h + 4, 8 * h + 7)], False, False)
+        msum([(R("m1", k, 128, 16), R("TRI", 128 * k, 128 * k + 128), R("EQ", 272 * 8 * h + k, 272 * 8 * (h + 1), 272)) for k in range(16)], False)
         scan(r("tw", h), r("RT", h), ta, A.max, A.min)
         act(r("win", h), ta, F.Relu, 1.0, -2.0 ** -13)
+        ts(r("win", h), ta, 1.0, A.is_lt)
+        either()
         tw = ends("tw", h)
         tt(l("of", h), l(lv, h), tw, A.max)
         cp(l("ofu", h), l("of", h))
@@ -771,8 +821,8 @@ def rank_program(g, core, T, topo):
         msum([(y2, ID, r("rr", h)), (y2, R("BDW", 0, 128), r("win", h))])
         msum([(y1, ID, r(x, h)), (y1, R("BDW", 0, 128), r("win", h))])
         msum([(na, ID, r("Cm", h)), (na, r("sc", h), R("I4K")), (na, R("BDW", 256, 384), r("win", h))])
-        act(r("rw", h), y2, F.Relu, -256.0)
-        act(R("XT", n0, n0 + 128), y1, F.Relu, -256.0)
+        move(r("rw", h), y2, -256.0, True, v=h == 1)
+        move(R("XT", n0, n0 + 128), y1, -256.0, True, v=h == 1)
         ts(R("ET", n0, n0 + 128) if t == 0 else r("EN", u - 2), na, 2048.0 - B5, A.add, 4095.0, A.max)
         msum([(y3, ID, r(x, h)), (y3, R("BDW", 128, 256), r("win", h))])
         tt(r(xn, h), r("rw", h), y3, A.max)
@@ -781,10 +831,7 @@ def rank_program(g, core, T, topo):
     head(1)
     bulk(0)
     for a in range(0, M, 448):
-        if CONV == "v":
-            cp(R("ET", a, a + 448), R("KI", a, a + 448))
-        else:
-            aff(R("ET", a, a + 448), R("KI", a, a + 448), [[0, 448]], A.is_ge, 0.0, 0, 0)
+        move(R("ET", a, a + 448), R("KI", a, a + 448))
     for u in range(UNITS):
         serve(u)
         if u + 1 < UNITS and (u % 2 == 0 or early(u + 1)):

@@ -10,12 +10,13 @@ B5 = float(2 ** 22)
 VO = 1280.0
 
 SB = {
-    "XT": (W + 16, "bfloat16"), "BK": (2 * H + 16, "bfloat16"), "fA": (128, "bfloat16"), "ET": (W + 384, "float32"), "EN": (2 * L, "float32"), "KI": (M, "int32"), "IDX": (2304, "float32"), "XW": (W + 384, "bfloat16"),
-    "ONE": (1024, "bfloat16"), "IDb": (128, "bfloat16"), "NIDb": (128, "bfloat16"), "IDf": (128, "float32"),
-    "G8t": (8, "bfloat16"), "G8": (8, "bfloat16"), "G8f": (8, "float32"), "G8x": (16, "bfloat16"), "GW": (16, "float32"), "GWb": (16, "bfloat16"),
-    "W1": (2048, "bfloat16"), "W2": (2048, "bfloat16"), "BW": (256, "bfloat16"), "NM": (256, "bfloat16"), "ruw": (256, "int32"), "fuw": (256, "int32"), "bw": (256, "int32"), "GS": (32, "bfloat16"), "GO": (8, "bfloat16"), "BG": (1024, "bfloat16"),
-    "REP": (2048, "bfloat16"), "TRI": (2048, "bfloat16"), "BDt": (128, "bfloat16"), "BD": (128, "bfloat16"), "NBD": (128, "bfloat16"), "BD2": (128, "bfloat16"),
-    "BDQ": (512, "bfloat16"), "BDW": (640, "bfloat16"), "Ck": (32, "float32"), "pms": (128, "bfloat16"), "pm": (128, "bfloat16"),
+    "XT": (W + 128, "bfloat16"), "BK": (2 * H + 16, "bfloat16"), "ET": (W + 384, "float32"), "EN": (2 * L, "float32"), "KI": (M, "int32"),
+    "IDX": (2304, "float32"), "XW": (W + 384, "bfloat16"),
+    "ONE": (128, "bfloat16"), "IDb": (128, "bfloat16"), "NIDb": (128, "bfloat16"), "IDf": (128, "float32"),
+    "G8t": (8, "bfloat16"), "G8": (8, "bfloat16"), "G8x": (16, "bfloat16"), "GWb": (16, "bfloat16"), "GS": (32, "bfloat16"), "GO": (8, "bfloat16"),
+    "BW": (256 * (STEPS + 1), "bfloat16"), "NM": (256, "bfloat16"), "REP": (2048, "bfloat16"), "TRI": (2048, "bfloat16"),
+    "BDt": (128, "bfloat16"), "BD": (128, "bfloat16"), "NBD": (128, "bfloat16"), "BD2": (128, "bfloat16"), "BDQ": (512, "bfloat16"), "BDW": (640, "bfloat16"),
+    "Ck": (32, "float32"), "pms": (128, "bfloat16"), "pm": (128, "bfloat16"),
     "CT": (512, "bfloat16"), "CRK": (128, "bfloat16"), "CH": (128, "bfloat16"), "C8": (128, "bfloat16"), "DK": (256, "bfloat16"), "DE": (512, "bfloat16"),
     "DB5": (128, "bfloat16"), "D256": (128, "bfloat16"), "I4K": (128, "bfloat16"), "P64K": (128, "bfloat16"),
     "II": (256, "bfloat16"), "PN": (128 * STEPS, "bfloat16"), "N4": (128, "float32"), "rm": (256, "bfloat16"), "trash": (16, "float32"), "RT": (256, "float32"),
@@ -23,33 +24,31 @@ SB = {
     "lvu": (16, "uint16"), "lvw": (16, "float32"),
     "Ef": (256, "float32"), "Kb": (256, "bfloat16"), "CL": (256, "uint16"), "CF": (128, "uint16"), "em": (256, "bfloat16"), "Cm": (256, "float16"),
     "vA": (256, "float16"), "xT": (256, "bfloat16"), "d0": (256, "bfloat16"),
-    "XG": (4096, "bfloat16"), "DD": (4096, "bfloat16"), "SG": (4096, "bfloat16"), "CMP": (4096, "bfloat16"), "EQ": (4352, "bfloat16"), "HL": (256, "uint16"),
-    "hr": (512, "bfloat16"), "u1": (256, "float32"), "hp": (256, "int32"), "hq": (68, "float32"),
-    "ru": (16, "int32"), "rp": (8, "int32"), "rl": (8, "uint16"), "fu": (16, "int32"), "fp": (8, "int32"), "fl": (8, "uint16"),
-    "fd": (128, "bfloat16"), "fD": (128, "bfloat16"), "fS": (128, "bfloat16"), "fC": (128, "bfloat16"), "fr": (128, "bfloat16"), "fo": (128, "bfloat16"), "fs": (128, "bfloat16"),
+    "XG": (4096, "bfloat16"), "DD": (4096, "bfloat16"), "SG": (4096, "bfloat16"), "CMP": (4096, "bfloat16"), "BG": (1024, "bfloat16"),
+    "EQ": (4352, "bfloat16"), "HL": (256, "uint16"), "hr": (512, "bfloat16"), "u1": (256, "float32"), "hp": (256, "int32"), "hq": (68, "float32"),
+    "ruw": (256, "int32"), "ru": (16, "int32"), "rp": (8, "int32"),
+    "fuw": (256, "int32"), "fu": (16, "int32"), "fp": (8, "int32"), "fl": (8, "uint16"),
+    "fd": (128, "bfloat16"), "fD": (128, "bfloat16"), "fS": (128, "bfloat16"), "fC": (128, "bfloat16"),
+    "fA": (128, "bfloat16"), "fr": (128, "bfloat16"), "fo": (128, "bfloat16"), "fs": (128, "bfloat16"),
     "tA": (256, "bfloat16"), "ncn": (256, "bfloat16"), "wm": (256, "bfloat16"), "sc": (256, "bfloat16"), "s1": (256, "bfloat16"), "s2": (256, "bfloat16"),
     "k1": (256, "float32"), "k2": (256, "float32"), "k3": (256, "int32"), "tw": (256, "float32"), "win": (256, "bfloat16"),
-    "A1": (256, "float32"), "A2": (256, "float32"), "rr": (256, "bfloat16"), "rw": (256, "bfloat16"),
+    "A1": (256, "float32"), "A2": (256, "float32"), "rr": (256, "bfloat16"), "bw": (256, "int32"),
     "of": (16, "float32"), "ofu": (16, "uint16"), "dn": (16, "int32"), "b1": (16, "float32"), "b2": (16, "float32"), "bi": (16, "int32"),
-    "zo": (128 * UNITS, "bfloat16"), "zl": (128 * UNITS, "bfloat16"), "yo": (128 * UNITS, "bfloat16"), "yl": (128 * UNITS, "bfloat16"),
+    "wl": (8 * STEPS, "bfloat16"), "zz": (256, "bfloat16"), "zo": (8 * UNITS, "uint16"), "zl": (8 * UNITS, "uint16"), "yo": (128 * UNITS, "bfloat16"), "yl": (128 * UNITS, "bfloat16"),
 }
 PS = ["dp0", "dp1", "HB", "m0", "BH0", "BH1", "m1", "m2"]
-INORDER = ("BH0", "BH1", "m1", "m2")
 SCRATCH = {k: ("sbuf", [128, n, 8] if k == "hq" else [128, n], d) for k, (n, d) in SB.items()}
 for _n in PS:
     SCRATCH[_n] = ("psum", [128, 512], "float32")
-NDMA = 15
-SEMAPHORES = ["qv", "qs", "qt", "qg"] + ["D%d" % i for i in range(NDMA)] + [n + str(u) for u in range(UNITS) for n in ("zs", "za", "ys", "ya")]
+NDMA = 14
+SEMAPHORES = ["qv", "qs", "qt", "qg"] + ["D%d" % i for i in range(NDMA)] + [n + str(u) for u in range(UNITS) for n in ("zs", "za", "ys", "ya")] + [
+    n + str(t) for t in range(STEPS) for n in ("ws", "wa")]
 
-TWICE = 1
 SGN = (4, 0, 2, 0, 2, 0)
 XGV = ((1, 3), (), (1,), (), (1,), ())
-AGAIN = ((), (1, 3), (), (1, 3), (), ())
 BKS = ((), (1, 3), (), (1, 3), (), (1, 3))
-EARLY = (2, 4)
-HASHA = ()
-GP = 512
-CP = 512
+SUB = (1, 2)
+TWICE = 1
 
 ORDER = {}
 CYC = 0.83e-3
@@ -61,44 +60,42 @@ FIRST = 2.0
 DMA0 = 2.0
 DMARATE = 2.5e5
 TURN = 0.05
-ROUNDS = 1200
-SWAPS = 12000
+HEAT = 0.1
+ROUNDS = 1300
+SWAPS = 4000
+SEED = 2
+SWAPS2 = 30000
+HEAT2 = 0.07
+CASES = ((1.0, 0.22, 4.0, 0.55), (1.35, 0.22, 4.5, 0.45))
 
 
 def overlap(a, b):
     return a[1] < b[2] and b[1] < a[2] and not (a[3] == b[3] and a[3] > 1 and (a[1] - b[1]) % a[3])
 
 
-def schedule(nodes):
+def schedule(nodes, spans):
     n = len(nodes)
     preds = [[] for _ in range(n)]
-    hist = {}
+    hist, users = {}, {}
     for i in range(n):
         kind, q, fn, reads, writes, cost, sem = nodes[i]
         seen = {}
         for rs, w in ((reads, False), (writes, True)):
             for r in rs:
-                bank = r[0] in INORDER
                 for (j, rj, wj) in hist.get(r[0], ()):
-                    ov = overlap(r, rj)
-                    same = nodes[j][1] == q and kind == "c" and nodes[j][0] == "c" and not sem and not nodes[j][6]
-                    if bank and (q == "t" or not same):
-                        full = not same
-                    elif same and q == "t" and r[0] not in PS:
-                        continue
-                    elif ov and (w or wj):
-                        full = not same or q != "t"
-                    else:
-                        continue
-                    seen[j] = seen.get(j, False) or full
+                    if overlap(r, rj) and (w or wj):
+                        seen[j] = seen.get(j, False) or q != "t" or nodes[j][1] != "t"
+        for b in sorted(set(r[0] for r in reads + writes if r[0] in PS)):
+            since = users.setdefault(b, [])
+            for j in (since if spans.get(i) == "opens" else since[:1]):
+                seen[j] = seen.get(j, False) or q != "t" or nodes[j][1] != "t"
+            users[b] = [i] if i in spans else since + [i]
         preds[i] = list(seen.items())
         for rs, w in ((reads, False), (writes, True)):
             for r in rs:
                 h = hist.get(r[0], [])
-                if w and abs(r[3]) == 1 and r[4] == 128 and r[0] not in INORDER:
+                if w and abs(r[3]) == 1:
                     h = [e for e in h if not (r[1] <= e[1][1] and e[1][2] <= r[2])]
-                if r[0] in INORDER and len(h) > 40:
-                    h = h[-40:]
                 hist[r[0]] = h + [(i, r, w)]
     loads = [i for i in range(n) if nodes[i][0] == "d"]
     for a, b in zip(loads, loads[1:]):
@@ -108,66 +105,91 @@ def schedule(nodes):
         for j, full in preds[i]:
             succ[j].append((i, full))
     banks = [[b for b in PS if any(r[0] == b for r in nodes[i][3] + nodes[i][4])] for i in range(n)]
-    first = min(i for i in range(n) if nodes[i][0] == "r")
+    opener = min(i for i in range(n) if nodes[i][0] == "r")
     hold = [nodes[i][5] if nodes[i][0] == "c" else (0.1 if nodes[i][0] == "d" else 0.8) for i in range(n)]
-    last = [nodes[i][5] + (FIRST if i == first else 0.0) for i in range(n)]
-    que = [nodes[i][1] for i in range(n)]
-    free_ones = [i for i in range(n) if nodes[i][0] == "c" and nodes[i][6]]
-
-    def flip(i):
-        q, c = (nodes[i][6][0], nodes[i][6][2]) if que[i] == nodes[i][1] else (nodes[i][1], nodes[i][5])
-        que[i], hold[i], last[i] = q, c, c
+    last = [nodes[i][5] + (FIRST if i == opener else 0.0) for i in range(n)]
     moved = DMA0
     for i in loads:
         if nodes[i][4]:
             moved += last[i] - DMA0
             last[i] = moved
+    times = {CASES[0]: (hold, last)}
+    for case in CASES[1:]:
+        times[case] = ([h * case[0] if nodes[i][0] == "c" else h for i, h in enumerate(hold)],
+                       [a * case[0] if nodes[i][0] == "c" else (a + case[2] - FLIGHT if nodes[i][0] == "r" else a) for i, a in enumerate(last)])
+    que = [nodes[i][1] for i in range(n)]
+    free_ones = [i for i in range(n) if nodes[i][0] == "c" and nodes[i][6]]
+    ends = [i for i in range(n) if not succ[i] or nodes[i][0] == "d"]
+    needs = [set(k for k, f in preds[i]) for i in range(n)]
+    seed = [SEED]
 
-    def gap(i, full):
-        return 0.0 if full is None else (last[i] + WAKE if full else hold[i])
+    def draw():
+        seed[0] = (seed[0] * 1103515245 + 12345) % 2 ** 31
+        return seed[0] / 2.0 ** 31
 
-    def find(uses, t):
-        lo, hi = 0, len(uses)
-        while lo < hi:
-            mid = (lo + hi) // 2
-            if uses[mid][0] < t:
-                lo = mid + 1
-            else:
-                hi = mid
-        return lo
+    def flip(i):
+        q, c = (nodes[i][6][0], nodes[i][6][2]) if que[i] == nodes[i][1] else (nodes[i][1], nodes[i][5])
+        que[i] = q
+        for case in CASES:
+            times[case][0][i] = times[case][1][i] = c * case[0]
+
+    def back_to(best):
+        for i in free_ones:
+            if que[i] != best[2][i]:
+                flip(i)
 
     def place(rank, back):
         before, after = (succ, preds) if back else (preds, succ)
         left = [len(p) for p in before]
-        est = [last[i] - hold[i] if back else 0.0 for i in range(n)]
+        est = [last[i] - hold[i] for i in range(n)] if back else [0.0] * n
         at = [0.0] * n
         ready = [(rank[i], i) for i in range(n) if not left[i]]
-        busy = {}
+        busy = {k: [] for k in PS + ["v", "s", "t", "g", "y"]}
         while ready:
             e = min(ready)
             ready.remove(e)
             i = e[1]
             q, t, h = que[i], est[i], hold[i]
-            own = busy.setdefault(q, [])
-            shared = [busy.setdefault(b, []) for b in banks[i]]
+            own = busy[q]
+            k = len(own)
+            while k and own[k - 1][1] > t:
+                k -= 1
             t0 = -1.0
             while t != t0:
-                t0 = t
-                k = max(find(own, t) - 1, 0)
                 while k < len(own) and own[k][0] < t + h:
-                    t = max(t, own[k][1])
+                    if own[k][1] > t:
+                        t = own[k][1]
                     k += 1
-                for uses in shared:
-                    k = find(uses, t - 2.0)
-                    while k < len(uses) and uses[k][0] - WAKE < t + h:
-                        if uses[k][2] != q:
-                            t = max(t, uses[k][1] + WAKE)
-                        k += 1
-            for uses in [own] + shared:
-                uses.insert(find(uses, t), (t, t + h, q))
-            at[i] = t + h if back else t
+                t0 = t
+                for b in banks[i]:
+                    uses = busy[b]
+                    m = len(uses)
+                    while m and uses[m - 1][0] > t - 1.5:
+                        m -= 1
+                    for x, y, w in uses[m:]:
+                        if x - WAKE >= t + h:
+                            break
+                        if w != q and y + WAKE > t:
+                            t = y + WAKE
+            while k and own[k - 1][0] > t:
+                k -= 1
+            own.insert(k, (t, t + h))
+            for b in banks[i]:
+                uses = busy[b]
+                m = len(uses)
+                while m and uses[m - 1][0] > t:
+                    m -= 1
+                uses.insert(m, (t, t + h, q))
+            if back:
+                t += h
+            at[i] = t
             for k, f in after[i]:
-                est[k] = max(est[k], at[i] + gap(k, f) - hold[k] if back else t + gap(i, f))
+                if back:
+                    e = t + last[k] + WAKE - hold[k] if f else (t - hold[k] if f is None else t)
+                else:
+                    e = t + last[i] + WAKE if f else (t if f is None else t + h)
+                if e > est[k]:
+                    est[k] = e
                 left[k] -= 1
                 if not left[k]:
                     ready.append((rank[k], k))
@@ -177,103 +199,113 @@ def schedule(nodes):
         at = place(rank, False)
         rank = [-a for a in place([-(at[i] + last[i]) for i in range(n)], True)]
         at = place(rank, False)
-        return max(at[i] + last[i] for i in range(n)), rank, at
-    seed = [1]
+        return max(at[i] + last[i] for i in ends), rank, at
 
-    def draw():
-        seed[0] = (seed[0] * 1103515245 + 12345) % 2 ** 31
-        return seed[0] / 2.0 ** 31
-    rank = [0.0] * n
-    for i in range(n - 1, -1, -1):
-        rank[i] = min([-last[i]] + [rank[k] - gap(i, f) for k, f in succ[i]])
-    span, rank, at = settle(rank)
-    best = (span, at, list(que))
-    for _ in range(ROUNDS):
-        lo, wide, far, part = -span * draw(), 3 + 17 * draw(), 0.5 * 8 ** draw(), 0.1 * 10 ** draw()
-        turned = [i for i in free_ones if lo - wide <= rank[i] < lo and draw() < TURN]
-        for i in turned:
-            flip(i)
-        s2, r2, at = settle([a + far * (draw() + draw() - 1) * 2 if lo - wide <= a < lo and draw() < part else a for a in rank])
-        if s2 < best[0]:
-            best = (s2, at, list(que))
-        if s2 <= span + 0.15:
-            span, rank = s2, r2
-        else:
+    def shift(best):
+        span, rank, at = settle(best[1])
+        for _ in range(ROUNDS):
+            lo, wide, far, part = -span * draw(), 3 + 17 * draw(), 0.5 * 8 ** draw(), 0.1 * 10 ** draw()
+            turned = [i for i in free_ones if lo - wide <= rank[i] < lo and draw() < TURN]
             for i in turned:
                 flip(i)
-    for i in free_ones:
-        if que[i] != best[2][i]:
-            flip(i)
+            s2, r2, at = settle([a + far * (draw() + draw() - 1) * 2 if lo - wide <= a < lo and draw() < part else a for a in rank])
+            if s2 < best[0]:
+                best = (s2, at, list(que))
+            if s2 <= span + 0.15:
+                span, rank = s2, r2
+            else:
+                for i in turned:
+                    flip(i)
+        back_to(best)
+        return best
 
-    def run(order):
-        at, why, free, held = [0.0] * n, [None] * n, {}, {}
-        for i in order:
+    def run(order, start, old, case):
+        first = start // 64
+        wake = case[1]
+        hold, last = times[case]
+        at, why, marks = (list(old[1]), list(old[2]), old[4][:first + 1]) if old else ([0.0] * n, [None] * n, [{}])
+        held = dict(marks[-1])
+        for p in range(64 * first, n):
+            if p % 64 == 0 and p > 64 * first:
+                marks.append(dict(held))
+            i = order[p]
             t, w, q = 0.0, None, que[i]
             for k, f in preds[i]:
-                e = at[k] + last[k] + WAKE if f else at[k] + gap(k, f)
+                e = at[k] + last[k] + wake if f else (at[k] if f is None else at[k] + hold[k])
                 if e > t:
                     t, w = e, (k, False)
-            if q in free and free[q][0] > t:
-                t, w = free[q][0], (free[q][1], True)
+            k = held.get(q)
+            if k is not None and at[k] + hold[k] > t:
+                t, w = at[k] + hold[k], (k, True)
             for b in banks[i]:
-                for other, (e, k) in held.setdefault(b, {}).items():
-                    if other != q and e + WAKE > t:
-                        t, w = e + WAKE, (k, True)
+                for other in "vst":
+                    k = held.get(b + other)
+                    if k is not None and other != q and at[k] + hold[k] + wake > t:
+                        t, w = at[k] + hold[k] + wake, (k, True)
+                held[b + q] = i
             at[i], why[i] = t, w
-            free[q] = (t + hold[i], i)
-            for b in banks[i]:
-                held[b][q] = free[q]
-        j = max(range(n), key=lambda k: at[k] + last[k])
-        return at[j] + last[j], at, why, j
-    needs = [set(k for k, f in preds[i]) for i in range(n)]
-    order = sorted(range(n), key=lambda i: (best[1][i], i))
-    span, at, why, j = run(order)
-    for step in range(SWAPS):
-        pairs, k = [], j
-        while why[k] is not None:
-            if why[k][1]:
-                pairs.append((why[k][0], k))
-            k = why[k][0]
-        a, b = pairs[int(draw() * len(pairs))]
-        bound = span - (0.1 * (1 - step / SWAPS) + 0.01) * math.log(draw() + 1e-9)
-        if nodes[a][0] == "c" and nodes[a][6] and draw() < 0.3:
-            flip(a)
-            s2, at, w2, j2 = run(order)
-            if s2 < best[0]:
-                best = (s2, at, list(que))
-            if s2 <= bound:
-                span, why, j = s2, w2, j2
-            else:
+            held[q] = i
+        j = max(ends, key=lambda k: at[k] + last[k])
+        return at[j] + last[j], at, why, j, marks
+
+    def swap(best, cases, swaps, heat):
+        order = sorted(range(n), key=lambda i: (best[1][i], i))
+        now = [run(order, 0, None, case) for case in cases]
+        base = [case[3] * now[0][0] / e[0] for e, case in zip(now, cases)]
+
+        def mean(runs):
+            return sum(w * e[0] for w, e in zip(base, runs))
+        best = (mean(now), now[0][1], list(que))
+        for step in range(swaps):
+            if step % 200 == 0:
+                order = sorted(range(n), key=lambda i: (now[0][1][i], i))
+                now = [run(order, 0, None, case) for case in cases]
+            why, k = now[int(draw() * len(cases))][2:4]
+            pairs = []
+            while why[k] is not None:
+                if why[k][1]:
+                    pairs.append((why[k][0], k))
+                k = why[k][0]
+            a, b = pairs[int(draw() * len(pairs))]
+            bound = mean(now) - (heat * (1 - step / swaps) + 0.01) * math.log(draw() + 1e-9)
+            pa, pb = order.index(a), order.index(b)
+            turn = nodes[a][0] == "c" and nodes[a][6] and draw() < 0.3
+            if turn:
                 flip(a)
-            continue
-        more = (0, 0, 0, 3, 10)[int(draw() * 5)]
-        pa, pb = order.index(a), order.index(b)
-        if draw() < 0.5:
-            pa = max(0, pa - more)
-            part, first = order[pa:pb + 1], {b}
-            for k in reversed(part):
-                if k in first:
-                    first |= needs[k]
-            if a in first:
-                continue
-        else:
-            pb = min(n - 1, pb + more)
-            part, late = order[pa:pb + 1], {a}
-            for k in part:
-                if needs[k] & late:
-                    late.add(k)
-            if b in late:
-                continue
-            first = set(part) - late
-        other = order[:pa] + [k for k in part if k in first] + [k for k in part if k not in first] + order[pb + 1:]
-        s2, at, w2, j2 = run(other)
-        if s2 <= bound:
-            order, span, why, j = other, s2, w2, j2
-            if s2 < best[0]:
-                best = (s2, at, list(que))
-    for i in free_ones:
-        if que[i] != best[2][i]:
-            flip(i)
+                other = order
+            else:
+                more = (0, 0, 0, 3, 10)[int(draw() * 5)]
+                if draw() < 0.5:
+                    pa = max(0, pa - more)
+                    part, first = order[pa:pb + 1], {b}
+                    for k in reversed(part):
+                        if k in first:
+                            first |= needs[k]
+                    if a in first:
+                        continue
+                else:
+                    pb = min(n - 1, pb + more)
+                    part, late = order[pa:pb + 1], {a}
+                    for k in part:
+                        if needs[k] & late:
+                            late.add(k)
+                    if b in late:
+                        continue
+                    first = set(part) - late
+                other = order[:pa] + [k for k in part if k in first] + [k for k in part if k not in first] + order[pb + 1:]
+            new = [run(other, pa, e, case) for e, case in zip(now, cases)]
+            if mean(new) < best[0]:
+                best = (mean(new), new[0][1], list(que))
+            if mean(new) <= bound:
+                order, now = other, new
+            elif turn:
+                flip(a)
+        back_to(best)
+        return best
+    rank = [0.0] * n
+    for i in range(n - 1, -1, -1):
+        rank[i] = min([-last[i]] + [rank[k] - (0.0 if f is None else last[i] + WAKE if f else hold[i]) for k, f in succ[i]])
+    best = swap(swap(shift((1e9, rank, list(que))), CASES[:1], SWAPS, HEAT), CASES, SWAPS2, HEAT2)
     ORDER["plan"] = (best[:2], preds, hold, last, banks)
     ORDER["queues"] = que
     return sorted(range(n), key=lambda i: (best[1][i], i))
@@ -289,8 +321,8 @@ def rank_program(g, core, T, topo):
     clock = {}
     hist = {}
 
-    def R(name, lo=0, hi=None, step=1, p1=128):
-        return (name, lo, SB[name][0] if hi is None and name in SB else (512 if hi is None else hi), step, p1)
+    def R(name, lo=0, hi=None, step=1):
+        return (name, lo, SB[name][0] if hi is None and name in SB else (512 if hi is None else hi), step)
 
     def P(win, off):
         return ("ind", win, off)
@@ -298,13 +330,11 @@ def rank_program(g, core, T, topo):
     def ap(r):
         if r[0] == "ind":
             return ap(r[1]).indirect(ap(r[2]))
-        name, lo, hi, step, p1 = r
+        name, lo, hi, step = r
         if name == "hq":
             return T.hq[:, lo:hi:step, :]
         if step == -1:
             return T[name][:, hi - 1:(lo - 1 if lo > 0 else None):-1]
-        if p1 != 128:
-            return T[name][0:p1, lo:hi]
         return T[name][:, lo:hi] if step == 1 else T[name][:, lo:hi:step]
 
     def flat(rs):
@@ -345,13 +375,14 @@ def rank_program(g, core, T, topo):
         for rs, w in ((reads, False), (writes, True)):
             for r in rs:
                 old = hist.get(r[0], [])
-                if w and abs(r[3]) == 1 and r[4] == 128:
+                if w and abs(r[3]) == 1:
                     old = [e for e in old if not (r[1] <= e[2] and e[3] <= r[2])]
                 else:
                     old = [e for e in old if not (e[0] == me and e[2:] == (r[1], r[2], w, abs(r[3])))]
                 hist[r[0]] = old + [(me, ev, r[1], r[2], w, abs(r[3]))]
 
     nodes = []
+    spans = {}
 
     def emit(q, fn, reads, writes, cost):
         offs = [r[2] for r in writes if r[0] == "ind"]
@@ -376,12 +407,10 @@ def rank_program(g, core, T, topo):
         nodes.append(("r", "g", fn, [src], [dst], FLIGHT, (lsem, len(engs))))
 
     def finish():
-        order = ORDER.get("order")
-        if order is None or len(order) != len(nodes):
-            order = schedule(nodes)
-            ORDER["order"] = order
+        if "order" not in ORDER:
+            ORDER["order"] = schedule(nodes, spans)
             ORDER["nodes"] = nodes
-        for i in order:
+        for i in ORDER["order"]:
             kind, q, fn, reads, writes, cost, sem = nodes[i]
             if kind == "c":
                 if ORDER["queues"][i] != q:
@@ -407,9 +436,9 @@ def rank_program(g, core, T, topo):
         for sem in sorted(count):
             need("g", (sem, count[sem]))
 
-    for buf, sem in (("zl", "za"), ("yl", "ya")):
-        hist[buf] = [("remote", (sem + str(u), NENG), 128 * u, 128 * u + 128, True, 1) for u in range(UNITS)]
-        for u in range(UNITS):
+    for buf, sem, wide, many in (("zl", "za", 8, UNITS), ("yl", "ya", 128, UNITS), ("wl", "wa", 8, STEPS)):
+        hist[buf] = [("remote", (sem + str(u), NENG), wide * u, wide * u + wide, True, 1) for u in range(many)]
+        for u in range(many):
             count[sem + str(u)] = NENG
 
     def width(r):
@@ -445,8 +474,7 @@ def rank_program(g, core, T, topo):
         if op1 is None:
             emit("v", lambda: V.tensor_scalar(ap(out), ap(a), c1, None, op0), rs, [out], vcost(out, [a], 1))
         else:
-            c2 = s2 if isinstance(s2, (int, float)) else ap(s2)
-            emit("v", lambda: V.tensor_scalar(ap(out), ap(a), c1, c2, op0, op1), rs, [out], vcost(out, [a], 1))
+            emit("v", lambda: V.tensor_scalar(ap(out), ap(a), c1, s2, op0, op1), rs, [out], vcost(out, [a], 1))
 
     def cp(out, a):
         emit("v", lambda: V.tensor_copy(ap(out), ap(a)), [a], [out], vcost(out, [a], 1))
@@ -458,13 +486,7 @@ def rank_program(g, core, T, topo):
         emit("v", lambda: V.tensor_tensor_scan(ap(out), ap(d0), ap(d1), 0.0, op0, op1), [d0, d1], [out], vcost(out, [d0, d1], 1))
 
     def act(out, a, f, bias=0.0, scale=1.0):
-        cols = [c for c in (bias, scale) if not isinstance(c, (int, float))]
-        b = bias if isinstance(bias, (int, float)) else ap(bias)
-        s = scale if isinstance(scale, (int, float)) else ap(scale)
-        emit("s", lambda: S.activation(ap(out), ap(a), f, bias=b, scale=s), [a] + cols, [out], vcost(out, [a], 0))
-
-    def reached(out, a):
-        act(out, a, F.Sigmoid, 500.0, 1000.0)
+        emit("s", lambda: S.activation(ap(out), ap(a), f, bias=bias, scale=scale), [a], [out], vcost(out, [a], 0))
 
     def either(second=False):
         b, a = nodes.pop(), nodes.pop()
@@ -482,6 +504,11 @@ def rank_program(g, core, T, topo):
             cp(out, a)
         either(v)
 
+    def reached(out, a, v=False):
+        act(out, a, F.Sigmoid, 500.0, 1000.0)
+        ts(out, a, 0.0, A.is_ge)
+        either(v)
+
     def mms(calls):
         fns, cost = [], 0.0
         for c in calls:
@@ -490,6 +517,8 @@ def rank_program(g, core, T, topo):
         nodes.append(("c", "t", fns, [c[1] for c in calls] + [c[2] for c in calls], [c[0] for c in calls], cost, None))
 
     def msum(terms, new=True, done=True):
+        if not (new and done):
+            spans[len(nodes)] = "opens" if new else "goes on"
         mms([(o, a, b, new and i == 0, done and i == len(terms) - 1) for i, (o, a, b) in enumerate(terms)])
 
     def mm(out, lhsT, rhs):
@@ -500,11 +529,6 @@ def rank_program(g, core, T, topo):
 
     def iota(out, pat, base, cm):
         emit("g", lambda: g.iota(ap(out), pat, base, cm, allow_small_or_imprecise_dtypes=True), [], [out], 0.13 + 2 * width(out) * CYC)
-
-    def sfill(name, lo, hi, c):
-        for a in range(lo, hi, 1024):
-            b = min(hi, a + 1024)
-            act(R(name, a, b), R("ONE", 0, b - a), F.Copy, 0.0, c)
 
     def gfill(name, lo, hi, c, step=0):
         for a in range(lo, hi, 384):
@@ -522,17 +546,17 @@ def rank_program(g, core, T, topo):
     ID, NID, RM = R("IDb"), R("NIDb"), R("rm", 0, 128)
     N256, P256, NB5 = R("DE", 0, 128), R("D256"), R("DE", 256, 384)
     fill(R("ONE"), 1.0)
-    aff(ID, R("ONE", 0, 128), [[-1, 128]], A.is_equal, 0.0, 0, 1)
+    aff(ID, R("ONE"), [[-1, 128]], A.is_equal, 0.0, 0, 1)
     aff(R("G8t"), R("ONE", 0, 8), [[-16, 8]], A.is_ge, 0.0, 0, 1)
     aff(R("G8"), R("G8t"), [[16, 8]], A.is_ge, 0.0, 15, -1)
-    aff(R("BDt"), R("ONE", 0, 128), [[-16, 8], [0, 16]], A.is_ge, 0.0, 0, 1)
+    aff(R("BDt"), R("ONE"), [[-16, 8], [0, 16]], A.is_ge, 0.0, 0, 1)
     aff(R("BD"), R("BDt"), [[16, 8], [0, 16]], A.is_ge, 0.0, 15, -1)
     iota(R("CRK"), [[0, 8], [-32, 16]], 528, 0)
     iota(R("II"), [[1, 256]], 0, 0)
     iota(R("trash"), [[16, 16]], W, 1)
     gfill("IDX", 0, 2304, -int(VO), 1)
     gfill("XW", 0, M + L, 0)
-    fill(R("XT", M, W + 16), 0.0)
+    fill(R("XT", M, W + 128), 0.0)
     fill(R("CH"), MK / 128)
     fill(R("hq"), 0.0)
     fill(R("BK", 2 * H, 2 * H + 16), -1.0)
@@ -540,32 +564,31 @@ def rank_program(g, core, T, topo):
     cp(R("IDf"), ID)
     for m in range(16):
         cp(R("REP", m, 2048, 16), ID)
-    cp(R("G8f"), R("G8"))
     cp(R("lvu"), R("sp"))
     cp(R("lv0"), R("sp"))
-    for j, w in ((0, "W1"), (1, "W2")):
-        if HASHA:
-            sfill(w, 0, 2048, 0.0)
-            ts(R("GW", 8 * j, 8 * j + 8), R("G8f"), R("wt", j, j + 1), A.mult)
-            for q in range(8):
-                ts(R(w, 16 * q, 16 * q + 129 * 15 + 1, 129), R("ONE", 0, 16), R("GW", 8 * j + q, 8 * j + q + 1), A.mult)
+    for j in range(2):
         ts(R("GWb", 8 * j, 8 * j + 8), R("G8"), R("wt", j, j + 1), A.mult)
         ts(R("BW", 128 * j, 128 * j + 128), R("BD"), R("wt", j, j + 1), A.mult)
+    for t in range(STEPS):
+        send(R("wt"), R("wl", 8 * t, 8 * t + 2), (rank - 1 - t) % 4, "ws%d" % t, "wa%d" % t)
+        for j in range(2):
+            ts(R("BW", 256 * t + 128 * j + 256, 256 * t + 128 * j + 384), R("BD"), R("wl", 8 * t + j, 8 * t + j + 1), A.mult)
     for name, lo, c in (("DK", 0, -2.0 ** -12), ("DK", 128, -2.0 ** -12), ("DE", 0, -256.0), ("DE", 128, 1024.0), ("DE", 256, -B5), ("DE", 384, -256.0),
                         ("D256", 0, 256.0), ("DB5", 0, B5), ("I4K", 0, 4096.0), ("P64K", 0, 65536.0)):
         ts(R(name, lo, lo + 128), ID, c, A.mult)
-    for name, lo, c in (("GS", 0, 1.0), ("GS", 8, 1.0), ("GS", 16, 65536.0), ("GS", 24, 1.0), ("GO", 0, -64.0), ("G8x", 0, 8192.0), ("G8x", 8, 1.0)):
+    for name, lo, c in (("GS", 0, 1.0), ("GS", 8, 1.0), ("GS", 16, 65536.0), ("GS", 24, 1.0), ("GO", 0, -64.0), ("G8x", 0, -8192.0), ("G8x", 8, 1.0)):
         ts(R(name, lo, lo + 8), R("G8"), c, A.mult)
     tt(R("pms", 0, 64), R("IDb", 0, 64), R("IDb", 64, 128), A.add)
     tt(R("pms", 64, 96), R("pms", 0, 32), R("pms", 32, 64), A.add)
     tt(R("pm", 0, 16), R("pms", 64, 80), R("pms", 80, 96), A.add)
     for n in (16, 32, 64):
         cp(R("pm", n, 2 * n), R("pm", 0, n))
-    for name, lo, a, b in (("CT", 0, 2048.0, 192.0), ("CT", 128, 2048.0, -1856.0), ("CT", 256, B5, -B5), ("CT", 384, -256.0, 0.0),
-                           ("N4", 0, -4095.0, 4095.0), ("NM", 0, B5, -B5), ("NM", 128, B5, -B5), ("C8", 0, -8192.0, 16384.0)) + tuple(("PN", 128 * t, M + 256.0 * t + 2 ** 17, -2.0 ** 17) for t in range(STEPS)):
+    for name, lo, a, b in [("CT", 0, 2048.0, 192.0), ("CT", 128, 2048.0, -1856.0), ("CT", 256, B5, -B5), ("CT", 384, -256.0, 0.0),
+                           ("N4", 0, -4095.0, 4095.0), ("NM", 0, B5, -B5), ("NM", 128, B5, -B5), ("C8", 0, -8192.0, 16384.0 + VO)] + [
+                           ("PN", 128 * t, M + 256.0 * t + 2 ** 17, -2.0 ** 17) for t in range(STEPS)]:
         ts(R(name, lo, lo + 128), R("pm"), a, A.mult, b, A.add)
     iota(R("rm"), [[0, 16], [1, 16]], -1, 0)
-    reached(R("rm"), R("rm"))
+    act(R("rm"), R("rm"), F.Sigmoid, 500.0, 1000.0)
     nodes[-1] = nodes[-1][:5] + (nodes[-1][5] + 1.3, None)
     fill(R("RT"), -1.0)
     cp(R("RT", 0, 256, 16), R("trash"))
@@ -591,19 +614,22 @@ def rank_program(g, core, T, topo):
         t, h = u // 2, u % 2
         return t, h, "x%d" % (t % 2), "x%d" % (1 - t % 2), "lv%d" % (t % 2), "lv%d" % (1 - t % 2)
 
+    def early(u):
+        return u > 0 and u % 2 == 0
+
     def book(u):
         return R("BK", 0, 2 * H + 16 if u >= TWICE else H)
 
-    def list_hash(u, src, b, at, ui, p, out):
-        msum([(R(b, at, at + 256), ID, R("NM")), (R(b, at, at + 128), R("BW", 0, 128), src), (R(b, at + 128, at + 256), R("BW", 128, 256), src)])
-        scan(R(ui + "w"), R("rm"), R(b, at, at + 256))
+    def list_hash(u, src, w, b, ui, p, out):
+        msum([(R(b, 256, 512), ID, R("NM")), (R(b, 256, 384), R("BW", w, w + 128), src), (R(b, 384, 512), R("BW", w + 128, w + 256), src)])
+        scan(R(ui + "w"), R("rm"), R(b, 256, 512))
         ts(R(ui), R(ui + "w", 15, 256, 16), 4095, A.bitwise_and)
         tt(R(p), R(ui, 0, 8), R(ui, 8, 16), A.mult)
         ts(R(p), R(p), 5, A.arith_shift_right, 4095, A.bitwise_and)
         tt(R(p), R(p), R(ui, 8, 16), A.add)
         if u < TWICE:
             ts(R(p), R(p), 4095, A.bitwise_and)
-        cp(R(out), R(p))
+        cp(out, R(p))
 
     def slots(u, out):
         t, h = u // 2, u % 2
@@ -617,17 +643,15 @@ def rank_program(g, core, T, topo):
         ts(r("em", h), cl, float(W), A.is_equal)
         ts(r("Cm", h), cl, -2048.0, A.add)
 
-    def early(u):
-        return u in EARLY
-
     def head(u):
         t, h, x, xn, lv, lvn = names(u)
         slots(u, r("CL", h))
         mm(R("m0", 128, 256), r(x, h), ID)
         move(r("xT", h), R("m0", 128, 256), v=h == 1)
         tt(r("d0", h), P(R("XT"), l("lvu", h)), r(x, h), A.subtract)
-        act(r("zo", u), r("d0", h), F.Abs)
-        send(r("zo", u), r("zl", u), (rank + 1 + t) % 4, "zs%d" % u, "za%d" % u)
+        act(r("zz", h), r("d0", h), F.Abs)
+        list_hash(u, r("zz", h), 256 * (t + 1), "m0", "ru", "rp", l("zo", u))
+        send(l("zo", u), l("zl", u), (rank + 1 + t) % 4, "zs%d" % u, "za%d" % u)
         if not early(u):
             marks(u, r("CL", h))
         move(r("vA", h), P(R("IDX"), l("lvu", h)))
@@ -647,36 +671,19 @@ def rank_program(g, core, T, topo):
 
     def bulk(u):
         h = u % 2
-        for a in range(2048 * h, 2048 * h + 2048, GP):
-            children = P(R("XT"), R("CL", a // 16, (a + GP) // 16))
-            move(R("XG", a, a + GP), children, v=(a // 512) % 4 in XGV[u])
-
-        def sub(j):
-            b = R("dp%d" % (j % 2))
-            msum([(b, NID, R("XG", 512 * j, 512 * j + 512)), (b, r("xT", h), R("REP", 512 * (j % 4), 512 * (j % 4) + 512))])
-            return b
-
-        def sign(j, b):
-            reached(R("SG", 512 * j, 512 * j + 512), b)
-            ts(R("SG", 512 * j, 512 * j + 512), b, 0.0, A.is_ge)
-            either(j % 4 < SGN[u])
         for j in range(4 * h, 4 * h + 4):
-            b = sub(j)
+            move(R("XG", 512 * j, 512 * j + 512), P(R("XT"), R("CL", 32 * j, 32 * j + 32)), v=j % 4 in XGV[u])
+        for j in range(4 * h, 4 * h + 4):
+            b = R("BH%d" % h if j % 4 in SUB else "dp%d" % (j % 2))
+            msum([(b, NID, R("XG", 512 * j, 512 * j + 512)), (b, r("xT", h), R("REP", 512 * (j % 4), 512 * (j % 4) + 512))])
             act(R("DD", 512 * j, 512 * j + 512), b, F.Abs)
-            if j % 4 not in AGAIN[u]:
-                sign(j, b)
-        for j in AGAIN[u]:
-            sign(4 * h + j, sub(4 * h + j))
+            reached(R("SG", 512 * j, 512 * j + 512), b, j % 4 < SGN[u])
 
     def verdicts(u):
         h = u % 2
         for e in range(2):
             a, c, o = 2048 * h + 1024 * e, 128 * h + 64 * e, 128 * e
-            if u in HASHA:
-                sums = [(R("HB", o + z, o + z + 64), R(w, 128 * k, 128 * k + 128), R("DD", a + k, a + 1024, 16)) for z, w in ((0, "W1"), (64, "W2")) for k in range(16)]
-            else:
-                sums = [(R("HB", o + k, o + 128, 8), R("DD", a + k, a + 1024, 8), R("GWb")) for k in range(8)]
-            msum([(R("HB", o, o + 128), R("ONE", 0, 128), R("CH"))] + sums)
+            msum([(R("HB", o, o + 128), R("ONE"), R("CH"))] + [(R("HB", o + k, o + 128, 8), R("DD", a + k, a + 1024, 8), R("GWb")) for k in range(8)])
             move(R("hr", 2 * c, 2 * c + 128), R("HB", o, o + 128), -2047.5, v=h == 0)
             u2 = R("HB", 256 + 64 * e, 320 + 64 * e)
             tt(R("u1", c, c + 64), R("HB", o, o + 64), R("hr", 2 * c, 2 * c + 64), A.subtract)
@@ -684,43 +691,32 @@ def rank_program(g, core, T, topo):
             hp = R("hp", c, c + 64)
             tt(hp, R("u1", c, c + 64), u2, A.mult)
             ts(hp, hp, 5, A.arith_shift_right, 4095, A.bitwise_and)
-            if u in HASHA:
-                if early(u):
-                    tt(R("HB", o, o + 64), R("fA", c, c + 64), u2, A.add)
-                    u2 = R("HB", o, o + 64)
+            z = 17 * (2 * h + e)
+            if u < TWICE:
                 tt(hp, hp, u2, A.add)
-                if u < TWICE:
-                    ts(hp, hp, 4095, A.bitwise_and)
-                ts(R("HL", c, c + 64), hp, 2.0 * H, A.min)
+                ts(hp, hp, 4095, A.bitwise_and)
+                cp(R("hq", z + 1, z + 17, 2), hp)
             else:
-                z = 17 * (2 * h + e)
-                if u < TWICE:
-                    tt(hp, hp, u2, A.add)
-                    ts(hp, hp, 4095, A.bitwise_and)
-                    cp(R("hq", z + 1, z + 17, 2), hp)
-                else:
-                    tt(R("hq", z + 1, z + 17, 2), hp, u2, A.add)
-                ht = R("HB", o, o + 64)
-                msum(([(ht, ID, R("fA", c, c + 64))] if early(u) else []) +
-                     [(ht, R("hq", z + 1, z + 17), R("IDf", 0, 128, 2)), (ht, R("hq", z, z + 16), R("IDf", 1, 128, 2))])
-                ts(R("HL", c, c + 64), ht, 2.0 * H, A.min)
+                tt(R("hq", z + 1, z + 17, 2), hp, u2, A.add)
+            ht = R("HB", o, o + 64)
+            msum(([(ht, ID, R("fA", c, c + 64))] if early(u) else []) +
+                 [(ht, R("hq", z + 1, z + 17), R("IDf", 0, 128, 2)), (ht, R("hq", z, z + 16), R("IDf", 1, 128, 2))])
+            ts(R("HL", c, c + 64), ht, 2.0 * H, A.min)
             for z in range(a, a + 1024, 512):
-                column, j = P(book(u), R("HL", z // 16, z // 16 + 32)), z // 512
-                if j % 4 in BKS[u]:
-                    bg, b = R("BG", 512 * (j % 2), 512 * (j % 2) + 512), R("dp%d" % (j % 2))
+                column, j = P(book(u), R("HL", z // 16, z // 16 + 32)), z // 512 % 4
+                if j in BKS[u]:
+                    o = BKS[u].index(j) % 2
+                    bg, b = R("BG", 512 * o, 512 * o + 512), R("dp%d" % o)
                     act(bg, column, F.Copy)
                     msum([(b, NID, R("DD", z, z + 512)), (b, ID, bg)])
                     reached(R("CMP", z, z + 512), b)
-                    ts(R("CMP", z, z + 512), b, 0.0, A.is_ge)
-                    either()
                 else:
                     tt(R("CMP", z, z + 512), column, R("DD", z, z + 512), A.is_ge)
         if h == 1:
             over(u)
 
     def serve(u):
-        list_hash(u, r("zl", u), "m0", 256, "ru", "rp", "rl")
-        move(r("yo", u), P(book(u), R("rl")))
+        move(r("yo", u), P(book(u), l("zl", u)))
         send(r("yo", u), r("yl", u), (rank - 1 - u // 2) % 4, "ys%d" % u, "ya%d" % u)
 
     def answer(u):
@@ -737,7 +733,7 @@ def rank_program(g, core, T, topo):
         tt(R("fd"), P(R("XW", 0, M + L), l("lvu", 0)), r(x, 0), A.subtract)
         act(R("fD"), R("fd"), F.Abs)
         ts(R("fS"), R("fd"), 0.0, A.is_le)
-        list_hash(u, R("fD"), "m2", 256, "fu", "fp", "fl")
+        list_hash(u, R("fD"), 0, "m2", "fu", "fp", R("fl"))
         tt(R("fC"), P(book(u), R("fl")), R("fD"), A.is_ge)
         slots(u, R("CF"))
         ts(R("fA"), R("CF"), M + 128.0 * (u - 1), A.is_ge, 2.0 * H, A.mult)
@@ -752,10 +748,10 @@ def rank_program(g, core, T, topo):
         b = "BH%d" % h
         q, ky = R("m2", 0, 256), R(b, 0, 256)
 
-        def sums(bank, lo, hi, c):
-            return [(R(bank, lo + k, hi, 16), R("CMP", 2048 * h + k, 2048 * h + 2048, 16), R("GS", c, c + (hi - lo) // 16)) for k in range(16)]
+        def sums(bank, c):
+            return [(R(bank, k, 256, 16), R("CMP", 2048 * h + k, 2048 * h + 2048, 16), R("GS", c, c + 16)) for k in range(16)]
         fq = [(q, ID, R("CT", 0, 256)), (q, r("Kb", h), R("DK")), (q, r("em", h), R("DE", 0, 256))]
-        fk = [(ky, ID, R("CT", 256, 512)), (R(b, 0, 128), R("ONE", 0, 128), R("CRK")), (ky, r("em", h), R("DE", 256, 512)), (R(b, 0, 128), r("Cm", h), ID)]
+        fk = [(ky, ID, R("CT", 256, 512)), (R(b, 0, 128), R("ONE"), R("CRK")), (ky, r("em", h), R("DE", 256, 512)), (R(b, 0, 128), r("Cm", h), ID)]
         if early(u):
             mm(R(b, 256, 384), R("fC"), R("NBD"))
             tt(R("fs"), R("fr"), R(b, 256, 384), A.mult)
@@ -763,8 +759,8 @@ def rank_program(g, core, T, topo):
             fk += [(ky, R("fC"), R("BDQ", 256, 512)), (R(b, 0, 128), R("P64K"), R("fs")), (R(b, 128, 256), ID, R("fs"))]
         msum(fq, True, False)
         msum(fk, True, False)
-        msum(sums("m2", 0, 256, 0), False)
-        msum(sums(b, 0, 256, 16), False, False)
+        msum(sums("m2", 0), False)
+        msum(sums(b, 16), False, False)
 
     def decide(u):
         t, h, x, xn, lv, lvn = names(u)
@@ -773,11 +769,11 @@ def rank_program(g, core, T, topo):
         tt(r("wm", h), R("m2", 128, 256), r("tA", h), A.is_gt)
         tt(r("ncn", h), R("m2", 0, 128), r("tA", h), A.is_le)
         mm(R("m2", 384, 400), r("wm", h), R("G8x"))
-        tt(l("lvw", h), l(lv, h), R("m2", 384, 392), A.subtract)
-        tt(l("b1", h), l(lv, h), R("m2", 392, 400), A.mult)
+        tt(l("lvw", h), l(lv, h), R("m2", 384, 392), A.add)
         msum([(R(b, 0, 128), R("DB5"), r("ncn", h)), (R(b, 128, 256), N256, r("ncn", h)), (R(b, 128, 256), P256, r("wm", h))], False)
         for c in range(8 * h, 8 * h + 8):
             ts(R("EQ", 272 * c, 256 * c + 256), R("vA", 16 * c, 256), R("lvw", c, c + 1), A.subtract, 8192.0 - VO, A.is_equal)
+        tt(l("b1", h), l(lv, h), R("m2", 392, 400), A.mult)
         scan(r("k1", h), RM, R(b, 0, 128))
         move(r("sc", h), R(b, 128, 256), 0.0, True)
         scan(r("k2", h, -1), RM, r("k1", h, -1))
@@ -788,18 +784,18 @@ def rank_program(g, core, T, topo):
         def lower(c):
             lo = max(128 * h, 16 * c + 16)
             return (R("m1", lo - 128 * h, 128), R("BD2"), R("EQ", 256 * c + lo, 256 * c + 128 * h + 128))
-        msum([(ta, ID, R("C8"))] + [lower(c) for c in range(8 * h)], True, False)
+        msum([(ta, ID, R("C8")), (ta, ID, r("vA", h))] + [lower(c) for c in range(8 * h)], True, False)
         msum([lower(c) for c in range(8 * h, 8 * h + 4)], False, False)
         msum([lower(c) for c in range(8 * h + 4, 8 * h + 7)], False, False)
         msum([(R("m1", k, 128, 16), R("TRI", 128 * k, 128 * k + 128), R("EQ", 272 * 8 * h + k, 272 * 8 * (h + 1), 272)) for k in range(16)], False)
         scan(r("tw", h), r("RT", h), ta, A.max, A.min)
-        act(r("win", h), ta, F.Relu, 1.0, -2.0 ** -13)
-        ts(r("win", h), ta, 1.0, A.is_lt)
+        act(r("win", h), ta, F.Sigmoid, 4096.0, -1.0)
+        ts(r("win", h), ta, 4096.0, A.is_lt)
         either()
-        tw = ends("tw", h)
-        tt(l("of", h), l(lv, h), tw, A.max)
-        cp(l("ofu", h), l("of", h))
-        if early(u + 1):
+        cp(l("ofu", h), ends("tw", h))
+        tw = l("of", h)
+        ts(tw, ends("tw", h), float(W), A.is_ge, 4096.0, A.mult)
+        if early(u + 1) and u + 1 < UNITS:
             cp(P(R("XW"), l("ofu", h)), r(x, h))
         mm(R(b, 384, 512), r("ncn", h), ID)
         kd = R(b, 256, 384)
@@ -821,37 +817,30 @@ def rank_program(g, core, T, topo):
         msum([(y2, ID, r("rr", h)), (y2, R("BDW", 0, 128), r("win", h))])
         msum([(y1, ID, r(x, h)), (y1, R("BDW", 0, 128), r("win", h))])
         msum([(na, ID, r("Cm", h)), (na, r("sc", h), R("I4K")), (na, R("BDW", 256, 384), r("win", h))])
-        move(r("rw", h), y2, -256.0, True, v=h == 1)
-        move(R("XT", n0, n0 + 128), y1, -256.0, True, v=h == 1)
+        move(R("XT", n0, n0 + 256), R("m1", 256, 512), -256.0, True, v=h == 1)
         ts(R("ET", n0, n0 + 128) if t == 0 else r("EN", u - 2), na, 2048.0 - B5, A.add, 4095.0, A.max)
         msum([(y3, ID, r(x, h)), (y3, R("BDW", 128, 256), r("win", h))])
-        tt(r(xn, h), r("rw", h), y3, A.max)
+        tt(r(xn, h), R("XT", n0 + 128, n0 + 256), y3, A.max)
 
     head(0)
     head(1)
     bulk(0)
-    for a in range(0, M, 448):
-        move(R("ET", a, a + 448), R("KI", a, a + 448))
+    for a in range(0, M, 256):
+        aff(R("ET", a, a + 256), R("KI", a, a + 256), [[0, 256]], A.is_ge, 0.0, 0, 0)
     for u in range(UNITS):
         serve(u)
-        if u + 1 < UNITS and (u % 2 == 0 or early(u + 1)):
+        if u + 1 < UNITS:
             bulk(u + 1)
         if early(u):
             mend(u)
         if u % 2 == 0:
             verdicts(u)
             verdicts(u + 1)
-        if u % 2 == 0:
             over(u)
         counts(u)
         answer(u)
         decide(u)
-        if u + 2 < UNITS and early(u + 2):
-            head(u + 2)
-        if u + 2 < UNITS and u % 2 == 1:
-            if not early(u + 1):
-                head(u + 1)
-                bulk(u + 1)
+        if u + 2 < UNITS:
             head(u + 2)
     xn, lvn = "x%d" % (STEPS % 2), "lv%d" % (STEPS % 2)
     dma("y", T.ykids[:, M + L:W - 128], T.EN[:, 0:384], [R("EN", 0, 384)], [])

@@ -7,48 +7,60 @@ UNITS = 2 * STEPS
 NENG = 8
 MK = 786432.0
 B5 = float(2 ** 22)
-VO = 1280.0
+FAR = float(2 ** 18)
+VO = 2048
+EPS = 2.0 ** -10
+ROWS = ("hq", "hu", "hf")
 
 SB = {
     "XT": (W + 128, "bfloat16"), "BK": (2 * H + 16, "bfloat16"), "ET": (W + 384, "float32"), "EN": (2 * L, "float32"), "KI": (M, "int32"),
-    "IDX": (2304, "float32"), "XW": (W + 384, "bfloat16"),
-    "ONE": (128, "bfloat16"), "IDb": (128, "bfloat16"), "NIDb": (128, "bfloat16"), "IDf": (128, "float32"),
-    "G8t": (8, "bfloat16"), "G8": (8, "bfloat16"), "G8x": (16, "bfloat16"), "GWb": (16, "bfloat16"), "GS": (32, "bfloat16"), "GO": (8, "bfloat16"),
+    "IDX": (VO, "float32"), "XW": (W + 384, "bfloat16"),
+    "ONE": (128, "bfloat16"), "IDb": (128, "bfloat16"), "NIDb": (128, "bfloat16"), "IDf": (128, "float32"), "DB": (4096, "bfloat16"), "BG": (1024, "bfloat16"),
+    "G8t": (8, "bfloat16"), "G8": (8, "bfloat16"), "G8x": (16, "bfloat16"), "GW": (32, "float32"), "GS": (32, "bfloat16"),
     "BW": (256 * (STEPS + 1), "bfloat16"), "NM": (256, "bfloat16"), "REP": (2048, "bfloat16"), "TRI": (2048, "bfloat16"),
-    "BDt": (128, "bfloat16"), "BD": (128, "bfloat16"), "NBD": (128, "bfloat16"), "BD2": (128, "bfloat16"), "BDQ": (512, "bfloat16"), "BDW": (640, "bfloat16"),
+    "BDt": (128, "bfloat16"), "BD": (128, "bfloat16"), "BD2": (128, "bfloat16"), "BDW": (512, "bfloat16"),
     "Ck": (32, "float32"), "pms": (128, "bfloat16"), "pm": (128, "bfloat16"),
-    "CT": (512, "bfloat16"), "CRK": (128, "bfloat16"), "CH": (128, "bfloat16"), "C8": (128, "bfloat16"), "DK": (256, "bfloat16"), "DE": (512, "bfloat16"),
-    "DB5": (128, "bfloat16"), "D256": (128, "bfloat16"), "I4K": (128, "bfloat16"), "P64K": (128, "bfloat16"),
-    "II": (256, "bfloat16"), "PN": (128 * STEPS, "bfloat16"), "N4": (128, "float32"), "rm": (256, "bfloat16"), "trash": (16, "float32"), "RT": (256, "float32"),
-    "wt": (2, "bfloat16"), "sp": (16, "int32"), "x0": (256, "bfloat16"), "x1": (256, "bfloat16"), "lv0": (16, "float32"), "lv1": (16, "float32"),
-    "lvu": (16, "uint16"), "lvw": (16, "float32"),
-    "Ef": (256, "float32"), "Kb": (256, "bfloat16"), "CL": (256, "uint16"), "CF": (128, "uint16"), "em": (256, "bfloat16"), "Cm": (256, "float16"),
-    "vA": (256, "float16"), "xT": (256, "bfloat16"), "d0": (256, "bfloat16"),
-    "XG": (4096, "bfloat16"), "DD": (4096, "bfloat16"), "SG": (4096, "bfloat16"), "CMP": (4096, "bfloat16"), "BG": (1024, "bfloat16"),
-    "EQ": (4352, "bfloat16"), "HL": (256, "uint16"), "hr": (512, "bfloat16"), "u1": (256, "float32"), "hp": (256, "int32"), "hq": (68, "float32"),
+    "CT": (128, "float16"), "CRK": (128, "bfloat16"), "C8": (128, "bfloat16"), "DK": (256, "bfloat16"), "DE": (512, "bfloat16"),
+    "DN": (640, "bfloat16"), "IN": (L * STEPS, "float16"), "km": (256, "float32"), "ne": (128, "bfloat16"), "I4K": (128, "bfloat16"), "I8K": (128, "bfloat16"), "IK32": (128, "bfloat16"), "SI": (512, "bfloat16"),
+    "II": (256, "bfloat16"), "PN": (128, "bfloat16"), "N4": (128, "float32"), "rm": (256, "bfloat16"), "trash": (16, "float32"), "RT": (256, "float32"),
+    "wt": (2, "bfloat16"), "sp": (16, "int32"), "x0": (256, "bfloat16"), "x1": (256, "bfloat16"), "lv0": (80, "float32"), "lv1": (80, "float32"),
+    "lvu": (16, "uint16"), "lvz": (16, "float32"),
+    "Ef": (256, "int32"), "c1": (256, "int32"), "Kb": (256, "bfloat16"), "Kc": (256, "bfloat16"), "CL": (256, "uint16"), "em": (256, "bfloat16"),
+    "Cm": (256, "float16"), "vA": (256, "float16"), "xT": (256, "bfloat16"), "d0": (256, "bfloat16"),
+    "XG": (4096, "bfloat16"), "DD": (4096, "float32"), "CMP": (4096, "bfloat16"),
+    "EQ": (4352, "bfloat16"), "HL": (256, "uint16"), "ui": (768, "int32"), "um": (512, "int32"), "us": (256, "float32"), "hp": (256, "int32"),
+    "hq": (68, "float16"), "hu": (68, "float16"), "hf": (68, "bfloat16"),
     "ruw": (256, "int32"), "ru": (16, "int32"), "rp": (8, "int32"),
     "fuw": (256, "int32"), "fu": (16, "int32"), "fp": (8, "int32"), "fl": (8, "uint16"),
-    "fd": (128, "bfloat16"), "fD": (128, "bfloat16"), "fS": (128, "bfloat16"), "fC": (128, "bfloat16"),
-    "fA": (128, "bfloat16"), "fr": (128, "bfloat16"), "fo": (128, "bfloat16"), "fs": (128, "bfloat16"),
-    "tA": (256, "bfloat16"), "ncn": (256, "bfloat16"), "wm": (256, "bfloat16"), "sc": (256, "bfloat16"), "s1": (256, "bfloat16"), "s2": (256, "bfloat16"),
+    "fd": (128, "bfloat16"), "fD": (128, "bfloat16"), "fN": (128, "bfloat16"), "fC": (128, "bfloat16"),
+    "fA": (128, "bfloat16"), "fo": (128, "bfloat16"), "fb": (128, "bfloat16"), "fr": (128, "bfloat16"), "fs": (128, "bfloat16"),
+    "nw": (512, "bfloat16"), "sc": (256, "bfloat16"), "s1": (256, "bfloat16"), "s2": (256, "bfloat16"),
     "k1": (256, "float32"), "k2": (256, "float32"), "k3": (256, "int32"), "tw": (256, "float32"), "win": (256, "bfloat16"),
     "A1": (256, "float32"), "A2": (256, "float32"), "rr": (256, "bfloat16"), "bw": (256, "int32"),
-    "of": (16, "float32"), "ofu": (16, "uint16"), "dn": (16, "int32"), "b1": (16, "float32"), "b2": (16, "float32"), "bi": (16, "int32"),
+    "ofu": (16, "uint16"), "dn": (16, "int32"), "b1": (16, "float32"), "e0": (80, "bfloat16"), "e1": (80, "int32"),
     "wl": (8 * STEPS, "bfloat16"), "zz": (256, "bfloat16"), "zo": (8 * UNITS, "uint16"), "zl": (8 * UNITS, "uint16"), "yo": (128 * UNITS, "bfloat16"), "yl": (128 * UNITS, "bfloat16"),
 }
 PS = ["dp0", "dp1", "HB", "m0", "BH0", "BH1", "m1", "m2"]
-SCRATCH = {k: ("sbuf", [128, n, 8] if k == "hq" else [128, n], d) for k, (n, d) in SB.items()}
+SCRATCH = {k: ("sbuf", [128, n, 8] if k in ROWS else [128, n], d) for k, (n, d) in SB.items()}
 for _n in PS:
     SCRATCH[_n] = ("psum", [128, 512], "float32")
-NDMA = 14
+NDMA = 15
 SEMAPHORES = ["qv", "qs", "qt", "qg"] + ["D%d" % i for i in range(NDMA)] + [n + str(u) for u in range(UNITS) for n in ("zs", "za", "ys", "ya")] + [
     n + str(t) for t in range(STEPS) for n in ("ws", "wa")]
 
-SGN = (4, 0, 2, 0, 2, 0)
-XGV = ((1, 3), (), (1,), (), (1,), ())
-BKS = ((), (1, 3), (), (1, 3), (), (1, 3))
-SUB = (1, 2)
-TWICE = 1
+XGV = ((1, 3), (1,), (), (), (), ())
+BKS = ((1, 3), (1, 3)) * 3
+BKB = ("HB", "dp1")
+YB = ("HB", "m1")
+FB = "m1"
+CB = ("BH0", "BH1")
+SEEN = True
+WB = ("m2", "m2")
+CW = (512,) * 6
+LOADS = (0, 1, 2)
+SUB = ("dp0", "dp1", "HB", "dp0")
+TWICE = 2
+SX = True
 
 ORDER = {}
 CYC = 0.83e-3
@@ -57,16 +69,23 @@ WAKE = 0.22
 ACT0 = 0.06
 FLIGHT = 4.0
 FIRST = 2.0
-DMA0 = 2.0
-DMARATE = 2.5e5
+DMA0 = 1.7
+DMAROWS = 0.3
+DMARATE = 2.9e5
 TURN = 0.05
-HEAT = 0.1
-ROUNDS = 1300
-SWAPS = 4000
+HEAT = 0.03
+COOL = 0.15
+NEAR = 0.3
+STARTS = 2
+ROUNDS = 1800
+SWAPS = 100000
 SEED = 2
-SWAPS2 = 30000
-HEAT2 = 0.07
-CASES = ((1.0, 0.22, 4.0, 0.55), (1.35, 0.22, 4.5, 0.45))
+SWAPS2 = 200000
+HEAT2 = 0.02
+LISTS = ("lvu", "CL", "HL", "zl", "fl", "ofu")
+SLOW = 1.0
+PAIR = 1.7
+CASES = ((1.0, 0.22, 4.0, 0.5, 1.0, 1.0), (1.35, 0.22, 4.5, 0.5, 1.0, 1.0))
 
 
 def overlap(a, b):
@@ -100,25 +119,44 @@ def schedule(nodes, spans):
     loads = [i for i in range(n) if nodes[i][0] == "d"]
     for a, b in zip(loads, loads[1:]):
         preds[b].append((a, None))
+    above = []
+    for i in range(n):
+        far = 0
+        for k, f in preds[i]:
+            if f:
+                far |= above[k]
+        preds[i] = [(k, f) for k, f in preds[i] if nodes[k][0] != "c" or not far >> k & 1]
+        for k, f in preds[i]:
+            far |= above[k] | (1 << k if f else 0)
+        above.append(far)
     succ = [[] for _ in range(n)]
     for i in range(n):
         for j, full in preds[i]:
             succ[j].append((i, full))
-    banks = [[b for b in PS if any(r[0] == b for r in nodes[i][3] + nodes[i][4])] for i in range(n)]
+    banks = [[b for b in range(8) if any(r[0] == PS[b] for r in nodes[i][3] + nodes[i][4])] for i in range(n)]
     opener = min(i for i in range(n) if nodes[i][0] == "r")
-    hold = [nodes[i][5] if nodes[i][0] == "c" else (0.1 if nodes[i][0] == "d" else 0.8) for i in range(n)]
-    last = [nodes[i][5] + (FIRST if i == opener else 0.0) for i in range(n)]
+    hold = [nodes[i][5] * SLOW if nodes[i][0] == "c" else (0.1 if nodes[i][0] == "d" else 0.8) for i in range(n)]
+    last = [hold[i] if nodes[i][0] == "c" else nodes[i][5] + (FIRST if i == opener else 0.0) for i in range(n)]
     moved = DMA0
     for i in loads:
-        if nodes[i][4]:
+        if not nodes[i][3]:
             moved += last[i] - DMA0
             last[i] = moved
-    times = {CASES[0]: (hold, last)}
-    for case in CASES[1:]:
-        times[case] = ([h * case[0] if nodes[i][0] == "c" else h for i, h in enumerate(hold)],
-                       [a * case[0] if nodes[i][0] == "c" else (a + case[2] - FLIGHT if nodes[i][0] == "r" else a) for i, a in enumerate(last)])
-    que = [nodes[i][1] for i in range(n)]
-    free_ones = [i for i in range(n) if nodes[i][0] == "c" and nodes[i][6]]
+    last[loads[-5]] += sum(last[i] - DMA0 for i in loads[-4:])
+    for i in loads[-4:]:
+        last[i] += 1.5
+    world = []
+    listed = [nodes[i][0] == "c" and nodes[i][5] > 0.2 and any(r[0] in LISTS for r in nodes[i][3]) for i in range(n)]
+    for slow, wake, flight, weight, late, jump in CASES:
+        slow = [slow * jump if listed[i] else slow for i in range(n)]
+        hd = [h * slow[i] if nodes[i][0] == "c" else h for i, h in enumerate(hold)]
+        ls = [a * slow[i] if nodes[i][0] == "c" else (a + flight - FLIGHT if nodes[i][0] == "r" else a * late) for i, a in enumerate(last)]
+        world.append((hd, ls, wake, [x for i in range(n) for x in (ls[i] + wake, 0.0, hd[i])], slow))
+    ahead = [[(k, 3 * k + (0 if f else 1 if f is None else 2)) for k, f in preds[i]] for i in range(n)]
+    behind = [[(k, 3 * i + (0 if f else 1 if f is None else 2)) for k, f in succ[i]] for i in range(n)]
+    que = [8 + "vstgy".index(nodes[i][1]) for i in range(n)]
+    both = [nodes[i][0] == "c" and bool(nodes[i][6]) for i in range(n)]
+    free_ones = [i for i in range(n) if both[i]]
     ends = [i for i in range(n) if not succ[i] or nodes[i][0] == "d"]
     needs = [set(k for k, f in preds[i]) for i in range(n)]
     seed = [SEED]
@@ -128,10 +166,12 @@ def schedule(nodes, spans):
         return seed[0] / 2.0 ** 31
 
     def flip(i):
-        q, c = (nodes[i][6][0], nodes[i][6][2]) if que[i] == nodes[i][1] else (nodes[i][1], nodes[i][5])
-        que[i] = q
-        for case in CASES:
-            times[case][0][i] = times[case][1][i] = c * case[0]
+        que[i] = 17 - que[i]
+        c = SLOW * (nodes[i][5] if "vs"[que[i] - 8] == nodes[i][1] else nodes[i][6][2])
+        hold[i] = last[i] = c
+        for hd, ls, wake, lag, slow in world:
+            hd[i] = ls[i] = lag[3 * i + 2] = c * slow[i]
+            lag[3 * i] = c * slow[i] + wake
 
     def back_to(best):
         for i in free_ones:
@@ -139,16 +179,17 @@ def schedule(nodes, spans):
                 flip(i)
 
     def place(rank, back):
-        before, after = (succ, preds) if back else (preds, succ)
-        left = [len(p) for p in before]
+        after, lag = ahead if back else behind, world[0][3]
         est = [last[i] - hold[i] for i in range(n)] if back else [0.0] * n
         at = [0.0] * n
-        ready = [(rank[i], i) for i in range(n) if not left[i]]
-        busy = {k: [] for k in PS + ["v", "s", "t", "g", "y"]}
-        while ready:
-            e = min(ready)
-            ready.remove(e)
-            i = e[1]
+        rank = list(rank)
+        for i in (range(n - 1, -1, -1) if back else range(n)):
+            e = rank[i] + 1e-6
+            for k, x in after[i]:
+                if rank[k] < e:
+                    rank[k] = e
+        busy = [[] for _ in range(13)]
+        for e, i in sorted(zip(rank, range(n))):
             q, t, h = que[i], est[i], hold[i]
             own = busy[q]
             k = len(own)
@@ -183,16 +224,10 @@ def schedule(nodes, spans):
             if back:
                 t += h
             at[i] = t
-            for k, f in after[i]:
-                if back:
-                    e = t + last[k] + WAKE - hold[k] if f else (t - hold[k] if f is None else t)
-                else:
-                    e = t + last[i] + WAKE if f else (t if f is None else t + h)
+            for k, x in after[i]:
+                e = t + lag[x] - hold[k] if back else t + lag[x]
                 if e > est[k]:
                     est[k] = e
-                left[k] -= 1
-                if not left[k]:
-                    ready.append((rank[k], k))
         return at
 
     def settle(rank):
@@ -219,60 +254,133 @@ def schedule(nodes, spans):
         back_to(best)
         return best
 
-    def run(order, start, old, case):
-        first = start // 64
-        wake = case[1]
-        hold, last = times[case]
-        at, why, marks = (list(old[1]), list(old[2]), old[4][:first + 1]) if old else ([0.0] * n, [None] * n, [{}])
-        held = dict(marks[-1])
-        for p in range(64 * first, n):
-            if p % 64 == 0 and p > 64 * first:
-                marks.append(dict(held))
+    def forward(order, lo, hi, case, at, state):
+        hd, ls, wake, lag, slow = case
+        free, bq, be, bo = state
+        for p in range(lo, hi):
             i = order[p]
-            t, w, q = 0.0, None, que[i]
-            for k, f in preds[i]:
-                e = at[k] + last[k] + wake if f else (at[k] if f is None else at[k] + hold[k])
+            q = que[i]
+            t = free[q]
+            for k, x in ahead[i]:
+                e = at[k] + lag[x]
                 if e > t:
-                    t, w = e, (k, False)
-            k = held.get(q)
-            if k is not None and at[k] + hold[k] > t:
-                t, w = at[k] + hold[k], (k, True)
+                    t = e
             for b in banks[i]:
-                for other in "vst":
-                    k = held.get(b + other)
-                    if k is not None and other != q and at[k] + hold[k] + wake > t:
-                        t, w = at[k] + hold[k] + wake, (k, True)
-                held[b + q] = i
-            at[i], why[i] = t, w
-            held[q] = i
-        j = max(ends, key=lambda k: at[k] + last[k])
-        return at[j] + last[j], at, why, j, marks
+                e = bo[b] if bq[b] == q else be[b]
+                if e > t:
+                    t = e
+            at[i] = t
+            t += hd[i]
+            free[q] = t
+            for b in banks[i]:
+                if bq[b] != q:
+                    bo[b] = be[b]
+                    bq[b] = q
+                be[b] = t + wake
+
+    def backward(order, lo, hi, case, to, state):
+        hd, ls, wake, lag, slow = case
+        free, bq, be, bo = state
+        for p in range(hi - 1, lo - 1, -1):
+            i = order[p]
+            q = que[i]
+            t = free[q]
+            for b in banks[i]:
+                e = bo[b] if bq[b] == q else be[b]
+                if e > t:
+                    t = e
+            t += hd[i]
+            if ls[i] > t:
+                t = ls[i]
+            for k, x in behind[i]:
+                e = to[k] + lag[x]
+                if e > t:
+                    t = e
+            to[i] = t
+            free[q] = t
+            for b in banks[i]:
+                if bq[b] != q:
+                    bo[b] = be[b]
+                    bq[b] = q
+                be[b] = t + wake
+
+    def copy(s):
+        return list(s[0]), list(s[1]), list(s[2]), list(s[3])
+
+    where = [0] * n
+
+    def sweep(order, case, rec, lo, hi):
+        at, to, fs, bs = rec
+        s, far = copy(fs[lo // 16]), hi
+        for c in range(lo // 16, (n - 1) // 16 + 1):
+            part = order[16 * c:16 * c + 16]
+            was = [at[i] for i in part]
+            forward(order, 16 * c, min(n, 16 * c + 16), case, at, s)
+            for i, a in zip(part, was):
+                if at[i] != a or 16 * c <= hi:
+                    for k, x in behind[i]:
+                        if where[k] > far:
+                            far = where[k]
+            if far < 16 * c + 16 and s == fs[c + 1]:
+                break
+            fs[c + 1] = copy(s)
+        s, far = copy(bs[hi // 16 + 1]), lo
+        for c in range(hi // 16, -1, -1):
+            part = order[16 * c:16 * c + 16]
+            was = [to[i] for i in part]
+            backward(order, 16 * c, min(n, 16 * c + 16), case, to, s)
+            for i, a in zip(part, was):
+                if to[i] != a or 16 * c >= lo:
+                    for k, x in ahead[i]:
+                        if where[k] < far:
+                            far = where[k]
+            if far >= 16 * c and s == bs[c]:
+                break
+            bs[c] = copy(s)
 
     def swap(best, cases, swaps, heat):
         order = sorted(range(n), key=lambda i: (best[1][i], i))
-        now = [run(order, 0, None, case) for case in cases]
-        base = [case[3] * now[0][0] / e[0] for e, case in zip(now, cases)]
-
-        def mean(runs):
-            return sum(w * e[0] for w, e in zip(base, runs))
-        best = (mean(now), now[0][1], list(que))
+        recs = []
+        for case in cases:
+            fresh = [([0.0] * 13, [-1] * 8, [-9.0] * 8, [-9.0] * 8) for _ in range(n // 16 + 2)]
+            recs.append(([0.0] * n, [0.0] * n, fresh, list(fresh)))
+            sweep(order, case, recs[-1], 0, n - 1)
+        span = [max(r[1]) for r in recs]
+        base = [CASES[c][3] * span[0] / span[c] / sum(e[3] for e in CASES[:len(cases)]) for c in range(len(cases))]
+        best = (sum(w * s for w, s in zip(base, span)), list(recs[0][0]), list(que))
         for step in range(swaps):
-            if step % 200 == 0:
-                order = sorted(range(n), key=lambda i: (now[0][1][i], i))
-                now = [run(order, 0, None, case) for case in cases]
-            why, k = now[int(draw() * len(cases))][2:4]
-            pairs = []
-            while why[k] is not None:
-                if why[k][1]:
-                    pairs.append((why[k][0], k))
-                k = why[k][0]
-            a, b = pairs[int(draw() * len(pairs))]
-            bound = mean(now) - (heat * (1 - step / swaps) + 0.01) * math.log(draw() + 1e-9)
-            pa, pb = order.index(a), order.index(b)
-            turn = nodes[a][0] == "c" and nodes[a][6] and draw() < 0.3
-            if turn:
-                flip(a)
-                other = order
+            if step % 500 == 0:
+                order.sort(key=lambda i: recs[0][0][i])
+                for p, i in enumerate(order):
+                    where[i] = p
+                for case, rec in zip(cases, recs):
+                    sweep(order, case, rec, 0, n - 1)
+            c = int(draw() * len(cases))
+            at, to, hd, wake = recs[c][0], recs[c][1], cases[c][0], cases[c][2]
+            pb = int(draw() * n)
+            b = order[pb]
+            if at[b] + to[b] < span[c] - NEAR * draw() ** 2 - 1e-6:
+                continue
+            pa, t = pb - 1, at[b] - 1e-6
+            while pa >= 0:
+                a = order[pa]
+                if que[a] == que[b]:
+                    if at[a] + hd[a] < t:
+                        pa = -1
+                    break
+                if banks[b] and at[a] + hd[a] + wake >= t and any(x in banks[a] for x in banks[b]):
+                    break
+                pa -= 1
+            turn, x = None, draw()
+            if both[b] and (pa < 0 or x < 0.2):
+                turn, pa = b, pb
+            elif pa < 0:
+                continue
+            elif both[a] and x < 0.4:
+                turn, pb = a, pa
+            if turn is not None:
+                flip(turn)
+                part = [turn]
             else:
                 more = (0, 0, 0, 3, 10)[int(draw() * 5)]
                 if draw() < 0.5:
@@ -292,22 +400,51 @@ def schedule(nodes, spans):
                     if b in late:
                         continue
                     first = set(part) - late
-                other = order[:pa] + [k for k in part if k in first] + [k for k in part if k not in first] + order[pb + 1:]
-            new = [run(other, pa, e, case) for e, case in zip(now, cases)]
-            if mean(new) < best[0]:
-                best = (mean(new), new[0][1], list(que))
-            if mean(new) <= bound:
-                order, now = other, new
-            elif turn:
-                flip(a)
+                part = [k for k in part if k in first] + [k for k in part if k not in first]
+            old = order[pa:pb + 1]
+            lo, hi = pa // 16 * 16, min(n, pb // 16 * 16 + 16)
+            bound = -heat * COOL ** (step / swaps) * math.log(draw() + 1e-9)
+            order[pa:pb + 1] = part
+            inside, loss = order[lo:hi], 0.0
+            for case, rec, w in zip(cases, recs, base):
+                at, to = rec[0], rec[1]
+                keep = [at[k] for k in inside], [to[k] for k in inside]
+                forward(order, lo, hi, case, at, copy(rec[2][lo // 16]))
+                backward(order, lo, hi, case, to, copy(rec[3][(hi - 1) // 16 + 1]))
+                loss += w * (max([at[k] + to[k] for k in inside]) - max([u + v for u, v in zip(*keep)]))
+                for k, u, v in zip(inside, *keep):
+                    at[k], to[k] = u, v
+                if loss > bound + 1.0:
+                    break
+            if loss <= bound:
+                for p in range(pa, pb + 1):
+                    where[order[p]] = p
+                for case, rec in zip(cases, recs):
+                    sweep(order, case, rec, lo, hi - 1)
+                span = [max(r[1]) for r in recs]
+                now = sum(w * s for w, s in zip(base, span))
+                if now < best[0]:
+                    best = (now, list(recs[0][0]), list(que))
+            else:
+                order[pa:pb + 1] = old
+                if turn is not None:
+                    flip(turn)
         back_to(best)
         return best
     rank = [0.0] * n
     for i in range(n - 1, -1, -1):
         rank[i] = min([-last[i]] + [rank[k] - (0.0 if f is None else last[i] + WAKE if f else hold[i]) for k, f in succ[i]])
-    best = swap(swap(shift((1e9, rank, list(que))), CASES[:1], SWAPS, HEAT), CASES, SWAPS2, HEAT2)
+    start = (1e9, rank, list(que))
+    tries = []
+    for _ in range(STARTS):
+        back_to(start)
+        tries.append(swap(shift(start), world[:1], SWAPS, HEAT))
+    ORDER["placed"] = [round(e[0], 1) for e in tries]
+    best = min(tries)
+    back_to(best)
+    best = swap(best, world, SWAPS2, HEAT2)
     ORDER["plan"] = (best[:2], preds, hold, last, banks)
-    ORDER["queues"] = que
+    ORDER["queues"] = ["vstgy"[q - 8] for q in que]
     return sorted(range(n), key=lambda i: (best[1][i], i))
 
 
@@ -331,8 +468,8 @@ def rank_program(g, core, T, topo):
         if r[0] == "ind":
             return ap(r[1]).indirect(ap(r[2]))
         name, lo, hi, step = r
-        if name == "hq":
-            return T.hq[:, lo:hi:step, :]
+        if name in ROWS:
+            return T[name][:, lo:hi:step, :]
         if step == -1:
             return T[name][:, hi - 1:(lo - 1 if lo > 0 else None):-1]
         return T[name][:, lo:hi] if step == 1 else T[name][:, lo:hi:step]
@@ -395,7 +532,7 @@ def rank_program(g, core, T, topo):
         nd[0] += 1
         r = (writes or reads)[0]
         size = 128 * (r[2] - r[1]) * (4 if SB[r[0]][1] in ("float32", "int32") else 2)
-        nodes.append(("d", q, lambda: queues[q].dma_start(out, in_), reads, writes, DMA0 + size / DMARATE, sem))
+        nodes.append(("d", q, lambda: queues[q].dma_start(out, in_), reads, writes, DMA0 + DMAROWS + size / DMARATE, sem))
 
     def send(src, dst, peer, lsem, rsem):
         to = T.cores[peer]
@@ -442,7 +579,7 @@ def rank_program(g, core, T, topo):
             count[sem + str(u)] = NENG
 
     def width(r):
-        return 16 * width(r[2]) if r[0] == "ind" else -((r[1] - r[2]) // abs(r[3])) * (8 if r[0] == "hq" else 1)
+        return 16 * width(r[2]) if r[0] == "ind" else -((r[1] - r[2]) // abs(r[3])) * (8 if r[0] in ROWS else 1)
 
     def dtype_of(r):
         return "float32" if r[0] in PS else SB[r[0]][1]
@@ -452,7 +589,7 @@ def rank_program(g, core, T, topo):
             return 0.05 + 3.8 * width(out[2]) * 16 * CYC
         n = width(out)
         if any(r[0] == "ind" for r in ins):
-            return 0.05 + 1.56 * n * CYC
+            return 0.05 + (PAIR if kind == 2 else 1.56) * n * CYC
         if kind == 0:
             return ACT0 + n * CYC
         if kind == 2:
@@ -474,7 +611,8 @@ def rank_program(g, core, T, topo):
         if op1 is None:
             emit("v", lambda: V.tensor_scalar(ap(out), ap(a), c1, None, op0), rs, [out], vcost(out, [a], 1))
         else:
-            emit("v", lambda: V.tensor_scalar(ap(out), ap(a), c1, s2, op0, op1), rs, [out], vcost(out, [a], 1))
+            c2 = s2 if isinstance(s2, (int, float)) else ap(s2)
+            emit("v", lambda: V.tensor_scalar(ap(out), ap(a), c1, c2, op0, op1), rs, [out], vcost(out, [a], 1))
 
     def cp(out, a):
         emit("v", lambda: V.tensor_copy(ap(out), ap(a)), [a], [out], vcost(out, [a], 1))
@@ -490,7 +628,7 @@ def rank_program(g, core, T, topo):
 
     def either(second=False):
         b, a = nodes.pop(), nodes.pop()
-        if second:
+        if second and a[4][0][0] in ("XG", "BK"):
             a, b = b, a
         nodes.append(a[:6] + ((b[1], b[2], b[5]),))
 
@@ -503,10 +641,18 @@ def rank_program(g, core, T, topo):
         else:
             cp(out, a)
         either(v)
+        if not SX and dtype_of(out) in ("int32", "uint16"):
+            b = nodes.pop()
+            nodes.append(b[:6] + (None,) if v else ("c", b[6][0], b[6][1], b[3], b[4], b[6][2], None))
 
-    def reached(out, a, v=False):
-        act(out, a, F.Sigmoid, 500.0, 1000.0)
-        ts(out, a, 0.0, A.is_ge)
+    def under(out, a, c, v=True):
+        act(out, a, F.Sigmoid, 256.0 * c - 128.0, -256.0)
+        ts(out, a, float(c), A.is_lt)
+        either(v)
+
+    def reached(out, a, c, v=True):
+        act(out, a, F.Sigmoid, 128.0 - 256.0 * c, 256.0)
+        ts(out, a, float(c), A.is_ge)
         either(v)
 
     def mms(calls):
@@ -537,14 +683,20 @@ def rank_program(g, core, T, topo):
 
     dma("y", T.sp[:], T.spot[:], [], [R("sp")])
     dma("s", T.wt[:], T.wts[:], [], [R("wt")])
-    dma("y", T.KI[:], T.kids[:], [], [R("KI")])
-    dma("y", T.XT[:, 0:M], T.nodes[:], [], [R("XT", 0, M)])
-    dma("y", T.x0[:], T.cand[:], [], [R("x0")])
+    for which in LOADS:
+        if which == 0:
+            dma("y", T.KI[:], T.kids[:], [], [R("KI")])
+        elif which == 1:
+            dma("y", T.XT[:, 0:M], T.nodes[:], [], [R("XT", 0, M)])
+        else:
+            dma("y", T.x0[:], T.cand[:], [], [R("x0")])
     dma("y", T.BK[:, 0:H], T.book[:], [], [R("BK", 0, H)])
-    dma("y", T.BK[:, H:2 * H], T.book[:], [], [R("BK", H, 2 * H)])
+    dma("y", T.XW[:, 0:M], T.nodes[:], [], [R("XW", 0, M)])
+    for a in range(0, H, 1024):
+        move(R("BK", a, a + 1024), R("BK", a, a + 1024), 1.0, v=True)
+    dma("y", T.BK[:, H:2 * H], T.BK[:, 0:H], [R("BK", 0, H)], [R("BK", H, 2 * H)])
 
     ID, NID, RM = R("IDb"), R("NIDb"), R("rm", 0, 128)
-    N256, P256, NB5 = R("DE", 0, 128), R("D256"), R("DE", 256, 384)
     fill(R("ONE"), 1.0)
     aff(ID, R("ONE"), [[-1, 128]], A.is_equal, 0.0, 0, 1)
     aff(R("G8t"), R("ONE", 0, 8), [[-16, 8]], A.is_ge, 0.0, 0, 1)
@@ -554,46 +706,52 @@ def rank_program(g, core, T, topo):
     iota(R("CRK"), [[0, 8], [-32, 16]], 528, 0)
     iota(R("II"), [[1, 256]], 0, 0)
     iota(R("trash"), [[16, 16]], W, 1)
-    gfill("IDX", 0, 2304, -int(VO), 1)
-    gfill("XW", 0, M + L, 0)
-    fill(R("XT", M, W + 128), 0.0)
-    fill(R("CH"), MK / 128)
-    fill(R("hq"), 0.0)
-    fill(R("BK", 2 * H, 2 * H + 16), -1.0)
+    gfill("IDX", 0, VO, -VO, 1)
+    gfill("XW", M, M + L, 0)
+    for name in ROWS:
+        fill(R(name), 0.0)
+    fill(R("BK", 2 * H, 2 * H + 16), 0.0)
+    fill(R("e1"), 0)
+    fill(R("e0"), 1.0)
+    fill(R("e0", 0, 80, 5), 0.0)
     ts(NID, ID, -1.0, A.mult)
-    cp(R("IDf"), ID)
     for m in range(16):
         cp(R("REP", m, 2048, 16), ID)
     cp(R("lvu"), R("sp"))
-    cp(R("lv0"), R("sp"))
+    cp(R("lv0", 4, 80, 5), R("sp"))
+    ts(R("GW", 16, 24), R("G8"), 1 / (1 + EPS), A.mult)
+    ts(R("GW", 24, 32), R("G8"), 1 / EPS, A.mult)
     for j in range(2):
-        ts(R("GWb", 8 * j, 8 * j + 8), R("G8"), R("wt", j, j + 1), A.mult)
+        ts(R("GW", 8 * j, 8 * j + 8), R("GW", 16, 24), R("wt", j, j + 1), A.mult)
         ts(R("BW", 128 * j, 128 * j + 128), R("BD"), R("wt", j, j + 1), A.mult)
     for t in range(STEPS):
         send(R("wt"), R("wl", 8 * t, 8 * t + 2), (rank - 1 - t) % 4, "ws%d" % t, "wa%d" % t)
         for j in range(2):
             ts(R("BW", 256 * t + 128 * j + 256, 256 * t + 128 * j + 384), R("BD"), R("wl", 8 * t + j, 8 * t + j + 1), A.mult)
-    for name, lo, c in (("DK", 0, -2.0 ** -12), ("DK", 128, -2.0 ** -12), ("DE", 0, -256.0), ("DE", 128, 1024.0), ("DE", 256, -B5), ("DE", 384, -256.0),
-                        ("D256", 0, 256.0), ("DB5", 0, B5), ("I4K", 0, 4096.0), ("P64K", 0, 65536.0)):
+    for name, lo, c in (("DK", 0, -2.0 ** -12), ("DK", 128, 2.0 ** -12), ("DE", 0, -256.0), ("DE", 128, -16384.0), ("DE", 256, -1.0), ("DE", 384, -1.0),
+                        ("DN", 0, FAR), ("DN", 128, -FAR), ("DN", 256, -2 * B5), ("DN", 384, 2.0), ("DN", 512, 1 / B5), ("IDf", 0, B5),
+                        ("I4K", 0, 4096.0 * 32), ("I8K", 0, 2.0 * H), ("IK32", 0, MK + 32 * 4096.0),
+                        ("SI", 0, 1.0), ("SI", 128, -1.0), ("SI", 256, 65536 / B5), ("SI", 384, 1 / 32)):
         ts(R(name, lo, lo + 128), ID, c, A.mult)
-    for name, lo, c in (("GS", 0, 1.0), ("GS", 8, 1.0), ("GS", 16, 65536.0), ("GS", 24, 1.0), ("GO", 0, -64.0), ("G8x", 0, -8192.0), ("G8x", 8, 1.0)):
+    ts(R("CRK"), R("CRK"), 1 / B5, A.mult)
+    for t in range(STEPS):
+        ts(R("IN", L * t, L * t + L), R("II"), M + L * t - 2048.0, A.add)
+    for name, lo, c in (("GS", 0, 1.0), ("GS", 8, -1.0), ("GS", 16, 65536 / B5), ("GS", 24, 1 / 32), ("G8x", 0, -float(VO)), ("G8x", 8, 1.0)):
         ts(R(name, lo, lo + 8), R("G8"), c, A.mult)
     tt(R("pms", 0, 64), R("IDb", 0, 64), R("IDb", 64, 128), A.add)
     tt(R("pms", 64, 96), R("pms", 0, 32), R("pms", 32, 64), A.add)
     tt(R("pm", 0, 16), R("pms", 64, 80), R("pms", 80, 96), A.add)
     for n in (16, 32, 64):
         cp(R("pm", n, 2 * n), R("pm", 0, n))
-    for name, lo, a, b in [("CT", 0, 2048.0, 192.0), ("CT", 128, 2048.0, -1856.0), ("CT", 256, B5, -B5), ("CT", 384, -256.0, 0.0),
-                           ("N4", 0, -4095.0, 4095.0), ("NM", 0, B5, -B5), ("NM", 128, B5, -B5), ("C8", 0, -8192.0, 16384.0 + VO)] + [
-                           ("PN", 128 * t, M + 256.0 * t + 2 ** 17, -2.0 ** 17) for t in range(STEPS)]:
+    for name, lo, a, b in (("CT", 0, -32768.0 - 383, 32768.0), ("N4", 0, 4 * FAR, 4095.0), ("NM", 0, B5, -B5), ("NM", 128, B5, -B5),
+                           ("C8", 0, -8192.0, 16384.0 + VO), ("PN", 0, FAR / 2 + 2048, FAR / 2)):
         ts(R(name, lo, lo + 128), R("pm"), a, A.mult, b, A.add)
     iota(R("rm"), [[0, 16], [1, 16]], -1, 0)
     act(R("rm"), R("rm"), F.Sigmoid, 500.0, 1000.0)
     nodes[-1] = nodes[-1][:5] + (nodes[-1][5] + 1.3, None)
     fill(R("RT"), -1.0)
     cp(R("RT", 0, 256, 16), R("trash"))
-    for name, lo, c in (("BD2", 0, 16384.0), ("NBD", 0, -1.0), ("BDQ", 0, 1.0), ("BDQ", 128, 1.0), ("BDQ", 256, 65536.0), ("BDQ", 384, 1.0),
-                        ("BDW", 0, 256.0), ("BDW", 128, -256.0), ("BDW", 256, B5), ("BDW", 384, 64.0), ("BDW", 512, -64.0)):
+    for name, lo, c in (("BD2", 0, 16384.0), ("BDW", 0, 256.0), ("BDW", 128, -256.0), ("BDW", 256, B5), ("BDW", 384, 2.0 ** 21)):
         ts(R(name, lo, lo + 128), R("BD"), c, A.mult)
     scan(R("Ck", 0, 16), R("ONE", 0, 16), R("pm", 0, 16))
     ts(R("Ck", 16, 32), R("pm", 0, 16), -1.5, A.mult)
@@ -606,6 +764,9 @@ def rank_program(g, core, T, topo):
 
     def l(n, h):
         return R(n, 8 * h, 8 * h + 8)
+
+    def col(n, h, j=4):
+        return R(n, 40 * h + j, 40 * h + 40, 5)
 
     def ends(n, h):
         return R(n, 128 * h + 15, 128 * h + 128, 16)
@@ -629,91 +790,96 @@ def rank_program(g, core, T, topo):
         tt(R(p), R(p), R(ui, 8, 16), A.add)
         if u < TWICE:
             ts(R(p), R(p), 4095, A.bitwise_and)
-        cp(out, R(p))
+        move(out, R(p), v=True)
 
-    def slots(u, out):
+    def slots(u):
         t, h = u // 2, u % 2
-        move(r("Ef", h), P(R("KI") if t == 0 else R("ET", 0, M + 256 * (t - 1)), l("lvu", h)), -4095.0)
-        move(r("Kb", h), r("Ef", h), MK + 2047.5, v=True)
-        msum([(R("m0", 0, 128), R("IDf"), r("Ef", h)), (R("m0", 0, 128), NID, r("Kb", h))])
-        ts(out, R("m0", 0, 128), MK + 4095.0, A.add, float(W), A.min)
+        move(r("Ef", h), P(R("KI") if t == 0 else R("ET", 0, M + 256 * (t - 1)), l("lvu", h)))
+        ts(r("c1", h), r("Ef", h), 4095, A.bitwise_and)
 
-    def marks(u, cl):
+    def marks(u):
         h = u % 2
-        ts(r("em", h), cl, float(W), A.is_equal)
-        ts(r("Cm", h), cl, -2048.0, A.add)
+        move(r("Kb", h), r("Ef", h), MK - 2047.5)
+        reached(r("em", h), r("c1", h), 4095)
+        if early(u):
+            move(r("Cm", h), r("c1", h), -2048.0)
+        else:
+            move(r("Cm", h), r("CL", h), -2048.0)
 
     def head(u):
         t, h, x, xn, lv, lvn = names(u)
-        slots(u, r("CL", h))
+        slots(u)
+        ts(r("CL", h), r("c1", h), M + 128.0 * max(u - 1, 0) - 1, A.min)
         mm(R("m0", 128, 256), r(x, h), ID)
-        move(r("xT", h), R("m0", 128, 256), v=h == 1)
-        tt(r("d0", h), P(R("XT"), l("lvu", h)), r(x, h), A.subtract)
+        move(r("xT", h), R("m0", 128, 256))
+        tt(r("d0", h), P(R("XT", 0, M + 256 * max(t - 1, 0)), l("lvu", h)), r(x, h), A.subtract)
         act(r("zz", h), r("d0", h), F.Abs)
         list_hash(u, r("zz", h), 256 * (t + 1), "m0", "ru", "rp", l("zo", u))
         send(l("zo", u), l("zl", u), (rank + 1 + t) % 4, "zs%d" % u, "za%d" % u)
         if not early(u):
-            marks(u, r("CL", h))
+            marks(u)
         move(r("vA", h), P(R("IDX"), l("lvu", h)))
-
-    def over(u):
-        h = u % 2
-        b, o = ("m2", 256) if h == 0 else ("HB", 384)
-        ov = R(b, o, o + 128)
-        sums = [(R(b, o + k, o + 128, 16), R("SG", 2048 * h + k, 2048 * h + 2048, 16), R("GO")) for k in range(16)]
-        if early(u):
-            msum([(ov, R("fS"), R("BDW", 384, 512))] + sums)
-            tt(R("fo"), R("fr"), ov, A.mult)
-            msum([(ov, R("fS"), R("BDW", 512, 640)), (ov, ID, R("fo"))])
-        else:
-            mms([c + (True, True) for c in sums])
-        move(r("tA", h), ov, 736.0, True)
 
     def bulk(u):
         h = u % 2
         for j in range(4 * h, 4 * h + 4):
-            move(R("XG", 512 * j, 512 * j + 512), P(R("XT"), R("CL", 32 * j, 32 * j + 32)), v=j % 4 in XGV[u])
+            move(R("XG", 512 * j, 512 * j + 512), P(R("XT", 0, M + 128 * max(u - 1, 0)), R("CL", 32 * j, 32 * j + 32)), v=j % 4 in XGV[u])
         for j in range(4 * h, 4 * h + 4):
-            b = R("BH%d" % h if j % 4 in SUB else "dp%d" % (j % 2))
+            b = R(SUB[(4 * u + j % 4) % len(SUB)])
             msum([(b, NID, R("XG", 512 * j, 512 * j + 512)), (b, r("xT", h), R("REP", 512 * (j % 4), 512 * (j % 4) + 512))])
-            act(R("DD", 512 * j, 512 * j + 512), b, F.Abs)
-            reached(R("SG", 512 * j, 512 * j + 512), b, j % 4 < SGN[u])
+            act(R("DD", 512 * j, 512 * j + 512), b, F.Abs, EPS, 1 + EPS)
 
     def verdicts(u):
         h = u % 2
         for e in range(2):
-            a, c, o = 2048 * h + 1024 * e, 128 * h + 64 * e, 128 * e
-            msum([(R("HB", o, o + 128), R("ONE"), R("CH"))] + [(R("HB", o + k, o + 128, 8), R("DD", a + k, a + 1024, 8), R("GWb")) for k in range(8)])
-            move(R("hr", 2 * c, 2 * c + 128), R("HB", o, o + 128), -2047.5, v=h == 0)
-            u2 = R("HB", 256 + 64 * e, 320 + 64 * e)
-            tt(R("u1", c, c + 64), R("HB", o, o + 64), R("hr", 2 * c, 2 * c + 64), A.subtract)
-            tt(u2, R("HB", o + 64, o + 128), R("hr", 2 * c + 64, 2 * c + 128), A.subtract)
-            hp = R("hp", c, c + 64)
-            tt(hp, R("u1", c, c + 64), u2, A.mult)
+            a, c, o = 2048 * h + 1024 * e, 128 * h + 64 * e, 256 * e
+            hb = "BH%d" % h
+            mms([(R(hb, o + k, o + 256, 8), R("DD", a + k, a + 1024, 8), R("GW"), True, True) for k in range(8)])
+            move(R("ui", 3 * c, 3 * c + 192), R(hb, o, o + 192))
+            ts(R("um", 2 * c, 2 * c + 128), R("ui", 3 * c, 3 * c + 128), 4095, A.bitwise_and)
+            hp, u2 = R("hp", c, c + 64), R("um", 2 * c + 64, 2 * c + 128)
+            tt(hp, R("um", 2 * c, 2 * c + 64), u2, A.mult)
             ts(hp, hp, 5, A.arith_shift_right, 4095, A.bitwise_and)
             z = 17 * (2 * h + e)
+
+            def turned(out, name, eye):
+                return [(out, R(name, z + 1, z + 17), R(eye, 0, 128, 2)), (out, R(name, z, z + 16), R(eye, 1, 128, 2))]
+            ht = R(hb, o + 64, o + 128)
             if u < TWICE:
                 tt(hp, hp, u2, A.add)
                 ts(hp, hp, 4095, A.bitwise_and)
-                cp(R("hq", z + 1, z + 17, 2), hp)
+                terms = []
             else:
-                tt(R("hq", z + 1, z + 17, 2), hp, u2, A.add)
-            ht = R("HB", o, o + 64)
-            msum(([(ht, ID, R("fA", c, c + 64))] if early(u) else []) +
-                 [(ht, R("hq", z + 1, z + 17), R("IDf", 0, 128, 2)), (ht, R("hq", z, z + 16), R("IDf", 1, 128, 2))])
-            ts(R("HL", c, c + 64), ht, 2.0 * H, A.min)
-            for z in range(a, a + 1024, 512):
-                column, j = P(book(u), R("HL", z // 16, z // 16 + 32)), z // 512 % 4
+                move(R("hu", z + 1, z + 17, 2), u2, -2048.0)
+                terms = turned(ht, "hu", "IDb") + ([(ht, R("I8K"), R("fA", c, c + 64))] if early(u) else [])
+            move(R("hq", z + 1, z + 17, 2), hp, -2048.0, v=True)
+            msum(terms + turned(ht, "hq", "IDb"))
+            if early(u):
+                ts(R("HL", c, c + 64), ht, 4096.0, A.add, 2.0 * H, A.min)
+            else:
+                move(R("HL", c, c + 64), ht, 2048.0 if u < TWICE else 4096.0, v=True)
+            for y in range(a, a + 1024, 512):
+                column, j = P(book(u), R("HL", y // 16, y // 16 + 32)), y // 512 % 4
                 if j in BKS[u]:
-                    o = BKS[u].index(j) % 2
-                    bg, b = R("BG", 512 * o, 512 * o + 512), R("dp%d" % o)
+                    m = BKS[u].index(j) % 2
+                    bg, b = R("BG", 512 * m, 512 * m + 512), R(BKB[m])
+                    for y1 in range(y, y + 512, 256):
+                        aff(R("DB", y1, y1 + 256), R("DD", y1, y1 + 256), [[0, 256]], A.is_ge, 0.0, 0, 0)
                     act(bg, column, F.Copy)
-                    msum([(b, NID, R("DD", z, z + 512)), (b, ID, bg)])
-                    reached(R("CMP", z, z + 512), b)
+                    msum([(b, NID, R("DB", y, y + 512)), (b, ID, bg)])
+                    act(R("CMP", y, y + 512), b, F.Sigmoid, -512.0, 1024.0)
+                    ts(R("CMP", y, y + 512), b, 0.5, A.is_gt)
+                    either()
                 else:
-                    tt(R("CMP", z, z + 512), column, R("DD", z, z + 512), A.is_ge)
-        if h == 1:
-            over(u)
+                    for y1 in range(y, y + 512, CW[u]):
+                        tt(R("CMP", y1, y1 + CW[u]), P(book(u), R("HL", y1 // 16, (y1 + CW[u]) // 16)), R("DD", y1, y1 + CW[u]), A.is_gt)
+            act(R("us", c, c + 64), R("ui", 3 * c + 128, 3 * c + 192), F.Identity, 7.0, 1 / EPS + 1)
+            ts(R("us", c, c + 64), R("ui", 3 * c + 128, 3 * c + 192), 1 / EPS + 1, A.mult, 7.0, A.add)
+            either()
+            tt(R("hf", z + 1, z + 17, 2), R(hb, o + 192, o + 256), R("us", c, c + 64), A.is_lt)
+            hi = R(hb, 192 + 64 * e, 256 + 64 * e)
+            msum(turned(hi, "hf", "IK32") + ([(hi, ID, R("fo", c, c + 64))] if early(u) else []))
+        tt(r("Kc", h), r("Kb", h), R(hb, 192, 320), A.max)
 
     def serve(u):
         move(r("yo", u), P(book(u), l("zl", u)))
@@ -721,61 +887,53 @@ def rank_program(g, core, T, topo):
 
     def answer(u):
         t, h, x, xn, lv, lvn = names(u)
-        a = R("m0", 128, 256)
+        a = R("m0", 0, 128)
         msum([(a, ID, r("yl", u)), (a, NID, r(x, h))])
-        act(r("rr", h), a, F.Abs)
+        act(r("rr", h), a, F.Abs, -1.0)
         msum([(a, ID, R("NM", 0, 128)), (a, R("BW", 0, 128), r("rr", h))])
         scan(r("bw", h), RM, a)
-        ts(l("bi", h), ends("bw", h), 1023, A.bitwise_and)
+        for j in (1, 4):
+            ts(col("e1", h, j), ends("bw", h), 1023, A.bitwise_and)
 
     def mend(u):
         t, h, x, xn, lv, lvn = names(u)
         tt(R("fd"), P(R("XW", 0, M + L), l("lvu", 0)), r(x, 0), A.subtract)
         act(R("fD"), R("fd"), F.Abs)
-        ts(R("fS"), R("fd"), 0.0, A.is_le)
+        ts(R("fN"), R("fd"), 0.0, A.is_gt, -4.5 / 16, A.add)
         list_hash(u, R("fD"), 0, "m2", "fu", "fp", R("fl"))
-        tt(R("fC"), P(book(u), R("fl")), R("fD"), A.is_ge)
-        slots(u, R("CF"))
-        ts(R("fA"), R("CF"), M + 128.0 * (u - 1), A.is_ge, 2.0 * H, A.mult)
-        marks(u, R("CF"))
-        mm(R("m0", 0, 128), R("fA"), ID)
-        act(R("fr"), R("m0", 0, 128), F.Relu, 1.0, -1.0)
-        ts(R("fr"), R("m0", 0, 128), 1.0, A.is_lt)
-        either()
+        tt(R("fC"), P(book(u), R("fl")), R("fD"), A.is_gt)
+        slots(u)
+        reached(R("fA"), r("c1", 0), M + 128 * (u - 1))
+        marks(u)
+        mm(R("m2", 128, 256), R("BDW", 384, 512), R("fN"))
+        tt(R("fo"), R("fA"), R("m2", 128, 256), A.mult)
 
     def counts(u):
         h = u % 2
         b = "BH%d" % h
-        q, ky = R("m2", 0, 256), R(b, 0, 256)
-
-        def sums(bank, c):
-            return [(R(bank, k, 256, 16), R("CMP", 2048 * h + k, 2048 * h + 2048, 16), R("GS", c, c + 16)) for k in range(16)]
-        fq = [(q, ID, R("CT", 0, 256)), (q, r("Kb", h), R("DK")), (q, r("em", h), R("DE", 0, 256))]
-        fk = [(ky, ID, R("CT", 256, 512)), (R(b, 0, 128), R("ONE"), R("CRK")), (ky, r("em", h), R("DE", 256, 512)), (R(b, 0, 128), r("Cm", h), ID)]
+        msum([(R(b), r("em", h), R("DE")), (r(b, 1), ID, R("CT")), (r(b, 2), R("ONE"), R("CRK")), (r(b, 2), r("Cm", h), r("DN", 4))], True, False)
+        msum([(R(b, 0, 256), r("Kc", h), R("DK"))], False, False)
         if early(u):
-            mm(R(b, 256, 384), R("fC"), R("NBD"))
-            tt(R("fs"), R("fr"), R(b, 256, 384), A.mult)
-            fq += [(q, R("fC"), R("BDQ", 0, 256)), (R("m2", 0, 128), ID, R("fs")), (R("m2", 128, 256), ID, R("fs"))]
-            fk += [(ky, R("fC"), R("BDQ", 256, 512)), (R(b, 0, 128), R("P64K"), R("fs")), (R(b, 128, 256), ID, R("fs"))]
-        msum(fq, True, False)
-        msum(fk, True, False)
-        msum(sums("m2", 0), False)
-        msum(sums(b, 16), False, False)
+            mm(R(FB, 256, 384), R("BD"), R("fC"))
+            tt(R("fs"), R("fA"), R(FB, 256, 384), A.mult)
+        msum([(R(b, k, 512, 16), R("CMP", 2048 * h + k, 2048 * h + 2048, 16), R("GS")) for k in range(16)], False, not early(u))
+        if early(u):
+            msum([(R(b), R("fs"), R("SI"))], False)
 
     def decide(u):
         t, h, x, xn, lv, lvn = names(u)
         b = "BH%d" % h
         n0 = M + 128 * u
-        tt(r("wm", h), R("m2", 128, 256), r("tA", h), A.is_gt)
-        tt(r("ncn", h), R("m2", 0, 128), r("tA", h), A.is_le)
-        mm(R("m2", 384, 400), r("wm", h), R("G8x"))
-        tt(l("lvw", h), l(lv, h), R("m2", 384, 392), A.add)
-        msum([(R(b, 0, 128), R("DB5"), r("ncn", h)), (R(b, 128, 256), N256, r("ncn", h)), (R(b, 128, 256), P256, r("wm", h))], False)
+        nc, wm = r("nw", 2 * h), r("nw", 2 * h + 1)
+        under(R("nw", 256 * h, 256 * h + 256), R(b, 0, 256), -191)
+        mm(R(WB[h], 256, 272), wm, R("G8x"))
+        top = 128 * h + 128 if SEEN else 256
         for c in range(8 * h, 8 * h + 8):
-            ts(R("EQ", 272 * c, 256 * c + 256), R("vA", 16 * c, 256), R("lvw", c, c + 1), A.subtract, 8192.0 - VO, A.is_equal)
-        tt(l("b1", h), l(lv, h), R("m2", 392, 400), A.mult)
-        scan(r("k1", h), RM, R(b, 0, 128))
-        move(r("sc", h), R(b, 128, 256), 0.0, True)
+            ts(R("EQ", 272 * c, 256 * c + top), R("vA", 16 * c, top), R(lv, 5 * c + 4, 5 * c + 5), A.subtract, R(WB[h], 256 + c % 8, 257 + c % 8), A.is_equal)
+        tt(l("b1", h), col(lv, h), R(WB[h], 264, 272), A.mult)
+        tt(r("km", h), r(b, 2), nc, A.add)
+        tt(r("sc", h), r(b, 3), nc, A.subtract)
+        scan(r("k1", h), RM, r("km", h))
         scan(r("k2", h, -1), RM, r("k1", h, -1))
         scan(r("s1", h), RM, r("sc", h))
         scan(r("s2", h, -1), RM, r("s1", h, -1))
@@ -784,7 +942,13 @@ def rank_program(g, core, T, topo):
         def lower(c):
             lo = max(128 * h, 16 * c + 16)
             return (R("m1", lo - 128 * h, 128), R("BD2"), R("EQ", 256 * c + lo, 256 * c + 128 * h + 128))
-        msum([(ta, ID, R("C8")), (ta, ID, r("vA", h))] + [lower(c) for c in range(8 * h)], True, False)
+        if SEEN:
+            msum([(ta, ID, R("C8")), (ta, ID, r("vA", h))], True, False)
+            if h == 1:
+                tt(R("ne"), P(R("ET", 0, M + 256 * max(t - 1, 0)), l("lvu", 1)), r("Ef", 1), A.not_equal)
+                msum([(ta, R("BD2"), R("ne"))], False, False)
+        else:
+            msum([(ta, ID, R("C8")), (ta, ID, r("vA", h))] + [lower(c) for c in range(8 * h)], True, False)
         msum([lower(c) for c in range(8 * h, 8 * h + 4)], False, False)
         msum([lower(c) for c in range(8 * h + 4, 8 * h + 7)], False, False)
         msum([(R("m1", k, 128, 16), R("TRI", 128 * k, 128 * k + 128), R("EQ", 272 * 8 * h + k, 272 * 8 * (h + 1), 272)) for k in range(16)], False)
@@ -792,32 +956,29 @@ def rank_program(g, core, T, topo):
         act(r("win", h), ta, F.Sigmoid, 4096.0, -1.0)
         ts(r("win", h), ta, 4096.0, A.is_lt)
         either()
-        cp(l("ofu", h), ends("tw", h))
-        tw = l("of", h)
-        ts(tw, ends("tw", h), float(W), A.is_ge, 4096.0, A.mult)
+        move(l("ofu", h), ends("tw", h), v=True)
+        reached(col("e0", h, 2), ends("tw", h), W)
         if early(u + 1) and u + 1 < UNITS:
             cp(P(R("XW"), l("ofu", h)), r(x, h))
-        mm(R(b, 384, 512), r("ncn", h), ID)
-        kd = R(b, 256, 384)
-        msum([(kd, ID, R("NM", 0, 128)), (kd, r("wm", h), NB5), (kd, r("k2", h), R("IDf"))])
-        tt(r("A2", h), r("Ef", h), R(b, 384, 512), A.mult)
+        st, kd, ra = R(CB[h], 0, 128), R(b, 256, 384), R(CB[h], 128, 256)
+        msum([(st, nc, r("DN", 0)), (st, wm, r("DN", 1))])
+        msum([(kd, r("DN", 3), R("NM", 0, 128)), (kd, wm, r("DN", 2)), (kd, r("k2", h), R("IDf"))])
+        tt(r("A2", h), r("Ef", h), st, A.min)
         scan(r("k3", h), RM, kd)
-        ra = R(b, 128, 256)
-        msum([(ra, ID, r("II", h)), (ra, ID, r("PN", t)), (ra, r("s2", h), R("I4K"))])
-        tt(r("A1", h), R("N4"), ra, A.max)
-        tt(P(R("ET"), l("ofu", h)), r("A1", h), r("A2", h), A.add)
+        msum([(ra, ID, r("IN", u)), (ra, ID, R("PN")), (ra, r("DN", 0), r("em", h)), (ra, nc, r("DN", 1)), (ra, wm, r("DN", 1)),
+              (ra, r("s2", h), R("I4K"))])
+        tt(r("A1", h), R("N4"), ra, A.min)
+        tt(P(R("ET"), l("ofu", h)), r("A1", h), r("A2", h), A.max)
         ts(l("dn", h), ends("k3", h), 4095, A.bitwise_and)
-        tt(l("b1", h), l("b1", h), l("dn", h), A.add)
-        tt(l("b2", h), l("bi", h), tw, A.subtract)
-        tt(l("b1", h), l("b1", h), tw, A.min)
-        tt(l(lvn, h), l("b1", h), l("b2", h), A.max)
-        if t < STEPS - 1:
-            cp(l("lvu", h), l(lvn, h))
-        na, y1, y2, y3 = R("m1", 128, 256), R("m1", 256, 384), R("m1", 384, 512), R(b, 0, 128)
+        tt(col("e1", h, 2), l("b1", h), l("dn", h), A.add)
+        scan(R(lvn, 40 * h, 40 * h + 40), R("e1", 40 * h, 40 * h + 40), R("e0", 40 * h, 40 * h + 40), A.subtract, A.mult)
+        move(l("lvu" if t < STEPS - 1 else "lvz", h), col(lvn, h), v=True)
+        yb = YB[h]
+        na, y1, y2, y3 = R(yb, 128, 256), R(yb, 256, 384), R(yb, 384, 512), R(b, 384, 512)
         msum([(y2, ID, r("rr", h)), (y2, R("BDW", 0, 128), r("win", h))])
         msum([(y1, ID, r(x, h)), (y1, R("BDW", 0, 128), r("win", h))])
         msum([(na, ID, r("Cm", h)), (na, r("sc", h), R("I4K")), (na, R("BDW", 256, 384), r("win", h))])
-        move(R("XT", n0, n0 + 256), R("m1", 256, 512), -256.0, True, v=h == 1)
+        move(R("XT", n0, n0 + 256), R(yb, 256, 512), -256.0, True, v=h == 1)
         ts(R("ET", n0, n0 + 128) if t == 0 else r("EN", u - 2), na, 2048.0 - B5, A.add, 4095.0, A.max)
         msum([(y3, ID, r(x, h)), (y3, R("BDW", 128, 256), r("win", h))])
         tt(r(xn, h), R("XT", n0 + 128, n0 + 256), y3, A.max)
@@ -836,7 +997,6 @@ def rank_program(g, core, T, topo):
         if u % 2 == 0:
             verdicts(u)
             verdicts(u + 1)
-            over(u)
         counts(u)
         answer(u)
         decide(u)
@@ -848,7 +1008,7 @@ def rank_program(g, core, T, topo):
     dma("y", T.ykids[:, 0:M + L], T.ET[:, 0:M + L], [R("ET", 0, M + L)], [])
     dma("s", T.ykids[:, W - 128:W], T.EN[:, 384:512], [R("EN", 384, 512)], [])
     dma("s", T.ynodes[:, 640:768], T.XT[:, W - 128:W], [R("XT", W - 128, W)], [])
-    dma("s", T.yspot[:], T[lvn][:], [R(lvn)], [])
+    dma("s", T.yspot[:], T.lvz[:], [R("lvz")], [])
     dma("s", T.ycand[:], T[xn][:], [R(xn)], [])
 
     finish()

@@ -11,53 +11,57 @@ FAR = float(2 ** 18)
 VO = 2048
 EPS = 2.0 ** -10
 ROWS = ("hq", "hu", "hf")
+FEW = ("sp", "sh", "c16", "SEL", "o16")
 
 SB = {
     "XT": (W + 128, "bfloat16"), "BK": (2 * H + 16, "bfloat16"), "ET": (W + 384, "float32"), "EN": (2 * L, "float32"), "KI": (M, "int32"),
     "IDX": (VO, "float32"), "XW": (W + 384, "bfloat16"),
     "ONE": (128, "bfloat16"), "IDb": (128, "bfloat16"), "NIDb": (128, "bfloat16"), "IDf": (128, "float32"), "DB": (4096, "bfloat16"), "BG": (1024, "bfloat16"),
     "G8t": (8, "bfloat16"), "G8": (8, "bfloat16"), "G8x": (16, "bfloat16"), "GW": (32, "float32"), "GS": (32, "bfloat16"),
-    "BW": (256 * (STEPS + 1), "bfloat16"), "NM": (256, "bfloat16"), "REP": (2048, "bfloat16"), "TRI": (2048, "bfloat16"),
+    "BW": (256 * (STEPS + 1), "bfloat16"), "NM": (512, "bfloat16"), "REP": (2048, "bfloat16"), "TRI": (128, "bfloat16"),
     "BDt": (128, "bfloat16"), "BD": (128, "bfloat16"), "BD2": (128, "bfloat16"), "BDW": (512, "bfloat16"),
-    "Ck": (32, "float32"), "pms": (128, "bfloat16"), "pm": (128, "bfloat16"),
+    "Ck": (256, "bfloat16"), "pms": (128, "bfloat16"), "pm": (128, "bfloat16"),
     "CT": (128, "float16"), "CRK": (128, "bfloat16"), "C8": (128, "bfloat16"), "DK": (256, "bfloat16"), "DE": (512, "bfloat16"),
     "DN": (640, "bfloat16"), "IN": (L * STEPS, "float16"), "km": (256, "float32"), "ne": (128, "bfloat16"), "I4K": (128, "bfloat16"), "I8K": (128, "bfloat16"), "IK32": (128, "bfloat16"), "SI": (512, "bfloat16"),
-    "II": (256, "bfloat16"), "PN": (128, "bfloat16"), "N4": (128, "float32"), "rm": (256, "bfloat16"), "trash": (16, "float32"), "RT": (256, "float32"),
-    "wt": (2, "bfloat16"), "sp": (16, "int32"), "x0": (256, "bfloat16"), "x1": (256, "bfloat16"), "lv0": (80, "float32"), "lv1": (80, "float32"),
+    "II": (256, "bfloat16"), "PN": (128, "bfloat16"), "N4": (128, "float32"), "rm": (512, "bfloat16"), "trash": (16, "float32"), "RT": (256, "float32"),
+    "wt": (2, "bfloat16"), "sp": (128, "int32"), "sh": (128, "float16"), "c16": (2048, "bfloat16"), "SEL": (136, "bfloat16"), "o16": (136, "bfloat16"),
+    "x0": (256, "bfloat16"), "x1": (256, "bfloat16"), "lv0": (80, "float32"), "lv1": (80, "float32"),
     "lvu": (16, "uint16"), "lvz": (16, "float32"),
     "Ef": (256, "int32"), "c1": (256, "int32"), "Kb": (256, "bfloat16"), "Kc": (256, "bfloat16"), "CL": (256, "uint16"), "em": (256, "bfloat16"),
     "Cm": (256, "float16"), "vA": (256, "float16"), "xT": (256, "bfloat16"), "d0": (256, "bfloat16"),
     "XG": (4096, "bfloat16"), "DD": (4096, "float32"), "CMP": (4096, "bfloat16"),
-    "EQ": (4352, "bfloat16"), "HL": (256, "uint16"), "ui": (768, "int32"), "um": (512, "int32"), "us": (256, "float32"), "hp": (256, "int32"),
+    "EQ": (4096, "bfloat16"), "HL": (256, "uint16"), "ui": (768, "int32"), "um": (512, "int32"), "us": (256, "float32"), "hp": (256, "int32"),
     "hq": (68, "float16"), "hu": (68, "float16"), "hf": (68, "bfloat16"),
-    "ruw": (256, "int32"), "ru": (16, "int32"), "rp": (8, "int32"),
+    "ruw": (512, "int32"), "ru": (32, "int32"), "rp": (16, "int32"),
     "fuw": (256, "int32"), "fu": (16, "int32"), "fp": (8, "int32"), "fl": (8, "uint16"),
     "fd": (128, "bfloat16"), "fD": (128, "bfloat16"), "fN": (128, "bfloat16"), "fC": (128, "bfloat16"),
-    "fA": (128, "bfloat16"), "fo": (128, "bfloat16"), "fb": (128, "bfloat16"), "fr": (128, "bfloat16"), "fs": (128, "bfloat16"),
+    "fA": (128, "bfloat16"), "fo": (128, "bfloat16"), "fs": (128, "bfloat16"),
     "nw": (512, "bfloat16"), "sc": (256, "bfloat16"), "s1": (256, "bfloat16"), "s2": (256, "bfloat16"),
     "k1": (256, "float32"), "k2": (256, "float32"), "k3": (256, "int32"), "tw": (256, "float32"), "win": (256, "bfloat16"),
     "A1": (256, "float32"), "A2": (256, "float32"), "rr": (256, "bfloat16"), "bw": (256, "int32"),
-    "ofu": (16, "uint16"), "dn": (16, "int32"), "b1": (16, "float32"), "e0": (80, "bfloat16"), "e1": (80, "int32"),
+    "ofu": (16, "uint16"), "e0": (80, "bfloat16"), "e1": (80, "int32"),
     "wl": (8 * STEPS, "bfloat16"), "zz": (256, "bfloat16"), "zo": (8 * UNITS, "uint16"), "zl": (8 * UNITS, "uint16"), "yo": (128 * UNITS, "bfloat16"), "yl": (128 * UNITS, "bfloat16"),
 }
 PS = ["dp0", "dp1", "HB", "m0", "BH0", "BH1", "m1", "m2"]
 SCRATCH = {k: ("sbuf", [128, n, 8] if k in ROWS else [128, n], d) for k, (n, d) in SB.items()}
+SCRATCH["EQ"] = ("sbuf", [128, 16, 256], "bfloat16")
 for _n in PS:
     SCRATCH[_n] = ("psum", [128, 512], "float32")
-NDMA = 15
+NDMA = 14
 SEMAPHORES = ["qv", "qs", "qt", "qg"] + ["D%d" % i for i in range(NDMA)] + [n + str(u) for u in range(UNITS) for n in ("zs", "za", "ys", "ya")] + [
     n + str(t) for t in range(STEPS) for n in ("ws", "wa")]
 
 XGV = ((1, 3), (1,), (), (), (), ())
-BKS = ((1, 3), (1, 3)) * 3
-BKB = ("HB", "dp1")
+BKS = ((1,), (0, 1), (1,), (0, 1), (1,), (0,))
+BKB = ("HB", "dp1", "HB", "dp1")
 YB = ("HB", "m1")
 FB = "m1"
-CB = ("BH0", "BH1")
-SEEN = True
 WB = ("m2", "m2")
+WO = 256
+EARLY = True
+SEEN = (0, 1)
+ASKS = (1, 1, 1, 1, 1, 1)
 CW = (512,) * 6
-LOADS = (0, 1, 2)
 SUB = ("dp0", "dp1", "HB", "dp0")
 TWICE = 2
 SX = True
@@ -68,7 +72,8 @@ PECYC = 0.42e-3
 WAKE = 0.22
 ACT0 = 0.06
 FLIGHT = 4.0
-FIRST = 2.0
+NEARBY = 3.9
+FIRST = 2.4
 DMA0 = 1.7
 DMAROWS = 0.3
 DMARATE = 2.9e5
@@ -76,16 +81,16 @@ TURN = 0.05
 HEAT = 0.03
 COOL = 0.15
 NEAR = 0.3
-STARTS = 2
-ROUNDS = 1800
-SWAPS = 100000
+STARTS = 5
+ROUNDS = 1400
+SWAPS = 70000
 SEED = 2
-SWAPS2 = 200000
+SWAPS2 = 220000
 HEAT2 = 0.02
 LISTS = ("lvu", "CL", "HL", "zl", "fl", "ofu")
 SLOW = 1.0
 PAIR = 1.7
-CASES = ((1.0, 0.22, 4.0, 0.5, 1.0, 1.0), (1.35, 0.22, 4.5, 0.5, 1.0, 1.0))
+CASES = ((1.0, 0.22, 4.0, 0.35, 1.0, 1.0), (1.35, 0.22, 4.5, 0.35, 1.0, 1.05), (1.1, 0.16, 3.6, 0.3, 0.9, 0.88))
 
 
 def overlap(a, b):
@@ -145,12 +150,16 @@ def schedule(nodes, spans):
     last[loads[-5]] += sum(last[i] - DMA0 for i in loads[-4:])
     for i in loads[-4:]:
         last[i] += 1.5
+    for i in loads[-7:-5]:
+        last[i] += 16.5
+    second = [i for i in range(n) if nodes[i][0] == "r"][1]
+    last[second] += 17.0
     world = []
     listed = [nodes[i][0] == "c" and nodes[i][5] > 0.2 and any(r[0] in LISTS for r in nodes[i][3]) for i in range(n)]
     for slow, wake, flight, weight, late, jump in CASES:
         slow = [slow * jump if listed[i] else slow for i in range(n)]
         hd = [h * slow[i] if nodes[i][0] == "c" else h for i, h in enumerate(hold)]
-        ls = [a * slow[i] if nodes[i][0] == "c" else (a + flight - FLIGHT if nodes[i][0] == "r" else a * late) for i, a in enumerate(last)]
+        ls = [a * slow[i] if nodes[i][0] == "c" else (a * late if nodes[i][0] == "d" else a + (flight - FLIGHT) * (nodes[i][5] == FLIGHT)) for i, a in enumerate(last)]
         world.append((hd, ls, wake, [x for i in range(n) for x in (ls[i] + wake, 0.0, hd[i])], slow))
     ahead = [[(k, 3 * k + (0 if f else 1 if f is None else 2)) for k, f in preds[i]] for i in range(n)]
     behind = [[(k, 3 * i + (0 if f else 1 if f is None else 2)) for k, f in succ[i]] for i in range(n)]
@@ -425,6 +434,7 @@ def schedule(nodes, spans):
                 now = sum(w * s for w, s in zip(base, span))
                 if now < best[0]:
                     best = (now, list(recs[0][0]), list(que))
+                    ORDER["spans"] = span
             else:
                 order[pa:pb + 1] = old
                 if turn is not None:
@@ -468,6 +478,10 @@ def rank_program(g, core, T, topo):
         if r[0] == "ind":
             return ap(r[1]).indirect(ap(r[2]))
         name, lo, hi, step = r
+        if name == "EQ":
+            return T.EQ[:, lo // 256:hi // 256, 0:16] if hi - lo > 256 else T.EQ[:, lo // 256, lo % 256:hi - lo // 256 * 256]
+        if name in FEW:
+            return T[name][0:16, lo:hi:step]
         if name in ROWS:
             return T[name][:, lo:hi:step, :]
         if step == -1:
@@ -527,21 +541,25 @@ def rank_program(g, core, T, topo):
 
     nd = [0]
 
-    def dma(q, out, in_, reads, writes):
+    def dma(q, out, in_, reads, writes, rows=128):
         sem = "D%d" % nd[0]
         nd[0] += 1
         r = (writes or reads)[0]
-        size = 128 * (r[2] - r[1]) * (4 if SB[r[0]][1] in ("float32", "int32") else 2)
-        nodes.append(("d", q, lambda: queues[q].dma_start(out, in_), reads, writes, DMA0 + DMAROWS + size / DMARATE, sem))
+        size = rows * (r[2] - r[1]) * (4 if SB[r[0]][1] in ("float32", "int32") else 2)
+        nodes.append(("d", q, lambda: queues[q].dma_start(out, in_), reads, writes, DMA0 + DMAROWS * rows / 128 + size / DMARATE, sem))
 
-    def send(src, dst, peer, lsem, rsem):
-        to = T.cores[peer]
-        rid, pid = topo.addr(to)[:2]
-        engs = topo.engines(core, to)[:NENG]
+    def engines(a, b, what):
+        e = topo.engines(T.cores[a], T.cores[b])
+        return e[-NENG:] if what == "wl" else e
+
+    def send(src, dst, peer, lsem, rsem, after=()):
+        rid, pid = topo.addr(T.cores[peer])[:2]
+        engs = engines(rank, peer, dst[0])
 
         def fn():
             g.remote_dma(ap(dst), ap(src), T.sem[rsem], T.sem[lsem], pid, rid, sum(1 << e for e in engs))
-        nodes.append(("r", "g", fn, [src], [dst], FLIGHT, (lsem, len(engs))))
+        nodes.append(("r", "g", fn, [src] + list(after), [dst],
+                      NEARBY if topo.chip(core) == topo.chip(T.cores[peer]) else FLIGHT, (lsem, len(engs))))
 
     def finish():
         if "order" not in ORDER:
@@ -573,12 +591,17 @@ def rank_program(g, core, T, topo):
         for sem in sorted(count):
             need("g", (sem, count[sem]))
 
-    for buf, sem, wide, many in (("zl", "za", 8, UNITS), ("yl", "ya", 128, UNITS), ("wl", "wa", 8, STEPS)):
-        hist[buf] = [("remote", (sem + str(u), NENG), wide * u, wide * u + wide, True, 1) for u in range(many)]
+    for buf, sem, wide, many, way in (("zl", "za", 8, UNITS, -1), ("yl", "ya", 128, UNITS, 1), ("wl", "wa", 8, STEPS, 1)):
+        hist[buf] = []
         for u in range(many):
-            count[sem + str(u)] = NENG
+            k = ASKS[u] if many == UNITS else 1
+            if k:
+                count[sem + str(u)] = len(engines((rank + way * (1 + u * STEPS // many)) % 4, rank, buf))
+                hist[buf].append(("remote", (sem + str(u), count[sem + str(u)]), wide * u, wide * (u + k), True, 1))
 
     def width(r):
+        if r[0] == "EQ" and r[2] - r[1] > 256:
+            return 128
         return 16 * width(r[2]) if r[0] == "ind" else -((r[1] - r[2]) // abs(r[3])) * (8 if r[0] in ROWS else 1)
 
     def dtype_of(r):
@@ -681,20 +704,14 @@ def rank_program(g, core, T, topo):
             b = min(hi, a + 384)
             iota(R(name, a, b), [[step, b - a]], c + step * (a - lo), 0)
 
-    dma("y", T.sp[:], T.spot[:], [], [R("sp")])
     dma("s", T.wt[:], T.wts[:], [], [R("wt")])
-    for which in LOADS:
-        if which == 0:
-            dma("y", T.KI[:], T.kids[:], [], [R("KI")])
-        elif which == 1:
-            dma("y", T.XT[:, 0:M], T.nodes[:], [], [R("XT", 0, M)])
-        else:
-            dma("y", T.x0[:], T.cand[:], [], [R("x0")])
+    dma("y", T.sp[0:16, :], T.spot[:], [], [R("sp")], 16)
+    dma("y", T.KI[:], T.kids[:], [], [R("KI")])
+    dma("s", T.c16[0:16, :], T.cand[:], [], [R("c16")], 16)
+    dma("y", T.XT[:, 0:M], T.nodes[:], [], [R("XT", 0, M)])
     dma("y", T.BK[:, 0:H], T.book[:], [], [R("BK", 0, H)])
-    dma("y", T.XW[:, 0:M], T.nodes[:], [], [R("XW", 0, M)])
     for a in range(0, H, 1024):
         move(R("BK", a, a + 1024), R("BK", a, a + 1024), 1.0, v=True)
-    dma("y", T.BK[:, H:2 * H], T.BK[:, 0:H], [R("BK", 0, H)], [R("BK", H, 2 * H)])
 
     ID, NID, RM = R("IDb"), R("NIDb"), R("rm", 0, 128)
     fill(R("ONE"), 1.0)
@@ -707,7 +724,8 @@ def rank_program(g, core, T, topo):
     iota(R("II"), [[1, 256]], 0, 0)
     iota(R("trash"), [[16, 16]], W, 1)
     gfill("IDX", 0, VO, -VO, 1)
-    gfill("XW", M, M + L, 0)
+    if EARLY:
+        gfill("XW", 0, M + L, 0)
     for name in ROWS:
         fill(R(name), 0.0)
     fill(R("BK", 2 * H, 2 * H + 16), 0.0)
@@ -717,17 +735,26 @@ def rank_program(g, core, T, topo):
     ts(NID, ID, -1.0, A.mult)
     for m in range(16):
         cp(R("REP", m, 2048, 16), ID)
-    cp(R("lvu"), R("sp"))
-    cp(R("lv0", 4, 80, 5), R("sp"))
+    fill(R("o16"), 1.0)
+    aff(R("SEL"), R("o16"), [[-1, 136]], A.is_equal, 0.0, 7, 8)
+    cp(R("sh"), R("sp"))
+    msum([(R("m1", 0, 16), R("SEL", 7 - j, 135 - j), R("sh", 16 * j, 16 * j + 16)) for j in range(8)])
+    cp(R("lvu"), R("m1", 0, 16))
+    cp(R("lv0", 4, 80, 5), R("m1", 0, 16))
+    msum([(R("HB", 0, L), R("SEL", 7 - j, 135 - j), R("c16", L * j, L * j + L)) for j in range(8)])
+    move(R("x0"), R("HB", 0, L))
     ts(R("GW", 16, 24), R("G8"), 1 / (1 + EPS), A.mult)
     ts(R("GW", 24, 32), R("G8"), 1 / EPS, A.mult)
     for j in range(2):
         ts(R("GW", 8 * j, 8 * j + 8), R("GW", 16, 24), R("wt", j, j + 1), A.mult)
         ts(R("BW", 128 * j, 128 * j + 128), R("BD"), R("wt", j, j + 1), A.mult)
-    for t in range(STEPS):
-        send(R("wt"), R("wl", 8 * t, 8 * t + 2), (rank - 1 - t) % 4, "ws%d" % t, "wa%d" % t)
+
+    def weights(t, after):
+        send(R("wt"), R("wl", 8 * t, 8 * t + 2), (rank - 1 - t) % 4, "ws%d" % t, "wa%d" % t, after)
         for j in range(2):
             ts(R("BW", 256 * t + 128 * j + 256, 256 * t + 128 * j + 384), R("BD"), R("wl", 8 * t + j, 8 * t + j + 1), A.mult)
+    weights(0, [])
+    weights(1, [])
     for name, lo, c in (("DK", 0, -2.0 ** -12), ("DK", 128, 2.0 ** -12), ("DE", 0, -256.0), ("DE", 128, -16384.0), ("DE", 256, -1.0), ("DE", 384, -1.0),
                         ("DN", 0, FAR), ("DN", 128, -FAR), ("DN", 256, -2 * B5), ("DN", 384, 2.0), ("DN", 512, 1 / B5), ("IDf", 0, B5),
                         ("I4K", 0, 4096.0 * 32), ("I8K", 0, 2.0 * H), ("IK32", 0, MK + 32 * 4096.0),
@@ -736,28 +763,27 @@ def rank_program(g, core, T, topo):
     ts(R("CRK"), R("CRK"), 1 / B5, A.mult)
     for t in range(STEPS):
         ts(R("IN", L * t, L * t + L), R("II"), M + L * t - 2048.0, A.add)
-    for name, lo, c in (("GS", 0, 1.0), ("GS", 8, -1.0), ("GS", 16, 65536 / B5), ("GS", 24, 1 / 32), ("G8x", 0, -float(VO)), ("G8x", 8, 1.0)):
+    for name, lo, c in (("GS", 0, 1.0), ("GS", 8, -1.0), ("GS", 16, 65536 / B5), ("GS", 24, 1 / 32), ("G8x", 0, -float(VO)), ("G8x", 8, -1.0)):
         ts(R(name, lo, lo + 8), R("G8"), c, A.mult)
     tt(R("pms", 0, 64), R("IDb", 0, 64), R("IDb", 64, 128), A.add)
     tt(R("pms", 64, 96), R("pms", 0, 32), R("pms", 32, 64), A.add)
     tt(R("pm", 0, 16), R("pms", 64, 80), R("pms", 80, 96), A.add)
     for n in (16, 32, 64):
         cp(R("pm", n, 2 * n), R("pm", 0, n))
-    for name, lo, a, b in (("CT", 0, -32768.0 - 383, 32768.0), ("N4", 0, 4 * FAR, 4095.0), ("NM", 0, B5, -B5), ("NM", 128, B5, -B5),
+    for name, lo, a, b in (("CT", 0, -32768.0 - 383, 32768.0), ("N4", 0, 4 * FAR, 4095.0), ("NM", 0, B5, -B5), ("NM", 128, B5, -B5), ("NM", 256, B5, -B5), ("NM", 384, B5, -B5),
                            ("C8", 0, -8192.0, 16384.0 + VO), ("PN", 0, FAR / 2 + 2048, FAR / 2)):
         ts(R(name, lo, lo + 128), R("pm"), a, A.mult, b, A.add)
-    iota(R("rm"), [[0, 16], [1, 16]], -1, 0)
+    iota(R("rm"), [[0, 32], [1, 16]], -1, 0)
     act(R("rm"), R("rm"), F.Sigmoid, 500.0, 1000.0)
     nodes[-1] = nodes[-1][:5] + (nodes[-1][5] + 1.3, None)
     fill(R("RT"), -1.0)
     cp(R("RT", 0, 256, 16), R("trash"))
     for name, lo, c in (("BD2", 0, 16384.0), ("BDW", 0, 256.0), ("BDW", 128, -256.0), ("BDW", 256, B5), ("BDW", 384, 2.0 ** 21)):
         ts(R(name, lo, lo + 128), R("BD"), c, A.mult)
-    scan(R("Ck", 0, 16), R("ONE", 0, 16), R("pm", 0, 16))
-    ts(R("Ck", 16, 32), R("pm", 0, 16), -1.5, A.mult)
-    tt(R("Ck", 0, 16), R("Ck", 0, 16), R("Ck", 16, 32), A.add)
-    for k in range(16):
-        ts(R("TRI", 128 * k, 128 * k + 128), R("BD2"), R("Ck", k, k + 1), A.mult)
+    scan(R("Ck", 0, 128), RM, R("pm"), A.mult, A.add)
+    ts(R("Ck", 128, 256), R("pm"), -1.5, A.mult)
+    tt(R("Ck", 0, 128), R("Ck", 0, 128), R("Ck", 128, 256), A.add)
+    tt(R("TRI"), R("BD2"), R("Ck", 0, 128), A.mult)
 
     def r(n, h, step=1):
         return R(n, 128 * h, 128 * h + 128, step)
@@ -776,21 +802,37 @@ def rank_program(g, core, T, topo):
         return t, h, "x%d" % (t % 2), "x%d" % (1 - t % 2), "lv%d" % (t % 2), "lv%d" % (1 - t % 2)
 
     def early(u):
-        return u > 0 and u % 2 == 0
+        return EARLY and u > 0 and u % 2 == 0
+
+    def known_nodes(u):
+        return M + (128 * max(u - 1, 0) if EARLY else L * (u // 2))
 
     def book(u):
         return R("BK", 0, 2 * H + 16 if u >= TWICE else H)
 
     def list_hash(u, src, w, b, ui, p, out):
-        msum([(R(b, 256, 512), ID, R("NM")), (R(b, 256, 384), R("BW", w, w + 128), src), (R(b, 384, 512), R("BW", w + 128, w + 256), src)])
-        scan(R(ui + "w"), R("rm"), R(b, 256, 512))
-        ts(R(ui), R(ui + "w", 15, 256, 16), 4095, A.bitwise_and)
-        tt(R(p), R(ui, 0, 8), R(ui, 8, 16), A.mult)
-        ts(R(p), R(p), 5, A.arith_shift_right, 4095, A.bitwise_and)
-        tt(R(p), R(p), R(ui, 8, 16), A.add)
+        n = width(src)
+        a, k, p = 512 - 2 * n, n // 16, R(p, 0, n // 16)
+        msum([(R(b, a, 512), ID, R("NM", 0, 2 * n)), (R(b, a, a + n), R("BW", w, w + 128), src), (R(b, a + n, 512), R("BW", w + 128, w + 256), src)])
+        scan(R(ui + "w", 0, 2 * n), R("rm", 0, 2 * n), R(b, a, 512))
+        ts(R(ui, 0, 2 * k), R(ui + "w", 15, 2 * n, 16), 4095, A.bitwise_and)
+        tt(p, R(ui, 0, k), R(ui, k, 2 * k), A.mult)
+        ts(p, p, 5, A.arith_shift_right, 4095, A.bitwise_and)
+        tt(p, p, R(ui, k, 2 * k), A.add)
         if u < TWICE:
-            ts(R(p), R(p), 4095, A.bitwise_and)
-        move(out, R(p), v=True)
+            ts(p, p, 4095, A.bitwise_and)
+        move(out, p, v=True)
+
+    def part(n, u, wide=128, step=False):
+        a = wide * (u % 2 if step else u)
+        return R(n, a, a + wide * ASKS[u])
+
+    def ask(u):
+        t, h, x, xn, lv, lvn = names(u)
+        tt(part("d0", u, 128, True), P(R("XT", 0, M + 256 * max(t - 1, 0)), part("lvu", u, 8, True)), part(x, u, 128, True), A.subtract)
+        act(part("zz", u, 128, True), part("d0", u, 128, True), F.Abs)
+        list_hash(u, part("zz", u, 128, True), 256 * (t + 1), "m0", "ru", "rp", part("zo", u, 8))
+        send(part("zo", u, 8), part("zl", u, 8), (rank + 1 + t) % 4, "zs%d" % u, "za%d" % u)
 
     def slots(u):
         t, h = u // 2, u % 2
@@ -809,13 +851,11 @@ def rank_program(g, core, T, topo):
     def head(u):
         t, h, x, xn, lv, lvn = names(u)
         slots(u)
-        ts(r("CL", h), r("c1", h), M + 128.0 * max(u - 1, 0) - 1, A.min)
+        ts(r("CL", h), r("c1", h), known_nodes(u) - 1.0, A.min)
         mm(R("m0", 128, 256), r(x, h), ID)
         move(r("xT", h), R("m0", 128, 256))
-        tt(r("d0", h), P(R("XT", 0, M + 256 * max(t - 1, 0)), l("lvu", h)), r(x, h), A.subtract)
-        act(r("zz", h), r("d0", h), F.Abs)
-        list_hash(u, r("zz", h), 256 * (t + 1), "m0", "ru", "rp", l("zo", u))
-        send(l("zo", u), l("zl", u), (rank + 1 + t) % 4, "zs%d" % u, "za%d" % u)
+        if ASKS[u] != 2:
+            ask(u if ASKS[u] else u - 1)
         if not early(u):
             marks(u)
         move(r("vA", h), P(R("IDX"), l("lvu", h)))
@@ -823,7 +863,7 @@ def rank_program(g, core, T, topo):
     def bulk(u):
         h = u % 2
         for j in range(4 * h, 4 * h + 4):
-            move(R("XG", 512 * j, 512 * j + 512), P(R("XT", 0, M + 128 * max(u - 1, 0)), R("CL", 32 * j, 32 * j + 32)), v=j % 4 in XGV[u])
+            move(R("XG", 512 * j, 512 * j + 512), P(R("XT", 0, known_nodes(u)), R("CL", 32 * j, 32 * j + 32)), v=j % 4 in XGV[u])
         for j in range(4 * h, 4 * h + 4):
             b = R(SUB[(4 * u + j % 4) % len(SUB)])
             msum([(b, NID, R("XG", 512 * j, 512 * j + 512)), (b, r("xT", h), R("REP", 512 * (j % 4), 512 * (j % 4) + 512))])
@@ -862,10 +902,10 @@ def rank_program(g, core, T, topo):
                 column, j = P(book(u), R("HL", y // 16, y // 16 + 32)), y // 512 % 4
                 if j in BKS[u]:
                     m = BKS[u].index(j) % 2
-                    bg, b = R("BG", 512 * m, 512 * m + 512), R(BKB[m])
+                    bg, b = R("BG", 512 * m, 512 * m + 512), R(BKB[2 * h + m])
                     for y1 in range(y, y + 512, 256):
                         aff(R("DB", y1, y1 + 256), R("DD", y1, y1 + 256), [[0, 256]], A.is_ge, 0.0, 0, 0)
-                    act(bg, column, F.Copy)
+                    move(bg, column)
                     msum([(b, NID, R("DB", y, y + 512)), (b, ID, bg)])
                     act(R("CMP", y, y + 512), b, F.Sigmoid, -512.0, 1024.0)
                     ts(R("CMP", y, y + 512), b, 0.5, A.is_gt)
@@ -882,18 +922,19 @@ def rank_program(g, core, T, topo):
         tt(r("Kc", h), r("Kb", h), R(hb, 192, 320), A.max)
 
     def serve(u):
-        move(r("yo", u), P(book(u), l("zl", u)))
-        send(r("yo", u), r("yl", u), (rank - 1 - u // 2) % 4, "ys%d" % u, "ya%d" % u)
+        move(part("yo", u), P(book(u), part("zl", u, 8)))
+        send(part("yo", u), part("yl", u), (rank - 1 - u // 2) % 4, "ys%d" % u, "ya%d" % u)
 
     def answer(u):
         t, h, x, xn, lv, lvn = names(u)
-        a = R("m0", 0, 128)
-        msum([(a, ID, r("yl", u)), (a, NID, r(x, h))])
-        act(r("rr", h), a, F.Abs, -1.0)
-        msum([(a, ID, R("NM", 0, 128)), (a, R("BW", 0, 128), r("rr", h))])
-        scan(r("bw", h), RM, a)
-        for j in (1, 4):
-            ts(col("e1", h, j), ends("bw", h), 1023, A.bitwise_and)
+        n = 128 * ASKS[u]
+        a = R("m0", 0, 128) if n == 128 else R("m0", 256, 512)
+        msum([(a, ID, part("yl", u)), (a, NID, part(x, u, 128, True))])
+        act(part("rr", u, 128, True), a, F.Abs, -1.0)
+        msum([(a, ID, R("NM", 0, n)), (a, R("BW", 0, 128), part("rr", u, 128, True))])
+        scan(part("bw", u, 128, True), R("rm", 0, n), a)
+        for j in (3, 4):
+            ts(R("e1", 40 * h + j, 40 * (h + ASKS[u]), 5), R("bw", 128 * h + 15, 128 * h + n, 16), 1023, A.bitwise_and)
 
     def mend(u):
         t, h, x, xn, lv, lvn = names(u)
@@ -926,41 +967,40 @@ def rank_program(g, core, T, topo):
         n0 = M + 128 * u
         nc, wm = r("nw", 2 * h), r("nw", 2 * h + 1)
         under(R("nw", 256 * h, 256 * h + 256), R(b, 0, 256), -191)
-        mm(R(WB[h], 256, 272), wm, R("G8x"))
-        top = 128 * h + 128 if SEEN else 256
+        mm(R(WB[h], WO, WO + 16), wm, R("G8x"))
+        top = 128 * h + 128 if t in SEEN else 256
         for c in range(8 * h, 8 * h + 8):
-            ts(R("EQ", 272 * c, 256 * c + top), R("vA", 16 * c, top), R(lv, 5 * c + 4, 5 * c + 5), A.subtract, R(WB[h], 256 + c % 8, 257 + c % 8), A.is_equal)
-        tt(l("b1", h), col(lv, h), R(WB[h], 264, 272), A.mult)
+            ts(R("EQ", 256 * c, 240 * c + top), R("vA", 16 * c, top), R(lv, 5 * c + 4, 5 * c + 5), A.subtract, R(WB[h], WO + c % 8, WO + 1 + c % 8), A.is_equal)
+        move(col("e0", h, 1), R(WB[h], WO + 8, WO + 16))
+        move(col("e1", h, 1), col(lv, h))
         tt(r("km", h), r(b, 2), nc, A.add)
         tt(r("sc", h), r(b, 3), nc, A.subtract)
         scan(r("k1", h), RM, r("km", h))
         scan(r("k2", h, -1), RM, r("k1", h, -1))
         scan(r("s1", h), RM, r("sc", h))
         scan(r("s2", h, -1), RM, r("s1", h, -1))
-        ta = R("m1", 0, 128)
+        ta = R("m1" if h == 0 or (EARLY and u + 1 < UNITS) else "dp0", 0, 128)
 
         def lower(c):
             lo = max(128 * h, 16 * c + 16)
-            return (R("m1", lo - 128 * h, 128), R("BD2"), R("EQ", 256 * c + lo, 256 * c + 128 * h + 128))
-        if SEEN:
-            msum([(ta, ID, R("C8")), (ta, ID, r("vA", h))], True, False)
-            if h == 1:
-                tt(R("ne"), P(R("ET", 0, M + 256 * max(t - 1, 0)), l("lvu", 1)), r("Ef", 1), A.not_equal)
-                msum([(ta, R("BD2"), R("ne"))], False, False)
-        else:
-            msum([(ta, ID, R("C8")), (ta, ID, r("vA", h))] + [lower(c) for c in range(8 * h)], True, False)
+            return (R(ta[0], lo - 128 * h, 128), R("BD2"), R("EQ", 240 * c + lo, 240 * c + 128 * h + 128))
+        msum([(ta, ID, R("C8")), (ta, ID, r("vA", h))], True, False)
+        if h == 1 and t in SEEN:
+            tt(R("ne"), P(R("ET", 0, M + 256 * max(t - 1, 0)), l("lvu", 1)), r("Ef", 1), A.not_equal)
+            msum([(ta, R("BD2"), R("ne"))], False, False)
+        elif h == 1:
+            msum([lower(c) for c in range(8)], False, False)
         msum([lower(c) for c in range(8 * h, 8 * h + 4)], False, False)
-        msum([lower(c) for c in range(8 * h + 4, 8 * h + 7)], False, False)
-        msum([(R("m1", k, 128, 16), R("TRI", 128 * k, 128 * k + 128), R("EQ", 272 * 8 * h + k, 272 * 8 * (h + 1), 272)) for k in range(16)], False)
+        msum([lower(c) for c in range(8 * h + 4, 8 * h + 7)] + [(ta, R("TRI"), R("EQ", 2048 * h, 2048 * h + 2048))], False)
         scan(r("tw", h), r("RT", h), ta, A.max, A.min)
         act(r("win", h), ta, F.Sigmoid, 4096.0, -1.0)
         ts(r("win", h), ta, 4096.0, A.is_lt)
         either()
         move(l("ofu", h), ends("tw", h), v=True)
-        reached(col("e0", h, 2), ends("tw", h), W)
+        reached(col("e0", h, 3), ends("tw", h), W)
         if early(u + 1) and u + 1 < UNITS:
             cp(P(R("XW"), l("ofu", h)), r(x, h))
-        st, kd, ra = R(CB[h], 0, 128), R(b, 256, 384), R(CB[h], 128, 256)
+        st, kd, ra = r(b, 1), r(b, 2), r(b, 3)
         msum([(st, nc, r("DN", 0)), (st, wm, r("DN", 1))])
         msum([(kd, r("DN", 3), R("NM", 0, 128)), (kd, wm, r("DN", 2)), (kd, r("k2", h), R("IDf"))])
         tt(r("A2", h), r("Ef", h), st, A.min)
@@ -969,12 +1009,11 @@ def rank_program(g, core, T, topo):
               (ra, r("s2", h), R("I4K"))])
         tt(r("A1", h), R("N4"), ra, A.min)
         tt(P(R("ET"), l("ofu", h)), r("A1", h), r("A2", h), A.max)
-        ts(l("dn", h), ends("k3", h), 4095, A.bitwise_and)
-        tt(col("e1", h, 2), l("b1", h), l("dn", h), A.add)
+        ts(col("e1", h, 2), ends("k3", h), 4095, A.bitwise_and)
         scan(R(lvn, 40 * h, 40 * h + 40), R("e1", 40 * h, 40 * h + 40), R("e0", 40 * h, 40 * h + 40), A.subtract, A.mult)
         move(l("lvu" if t < STEPS - 1 else "lvz", h), col(lvn, h), v=True)
         yb = YB[h]
-        na, y1, y2, y3 = R(yb, 128, 256), R(yb, 256, 384), R(yb, 384, 512), R(b, 384, 512)
+        na, y1, y2, y3 = R(yb, 128, 256), R(yb, 256, 384), R(yb, 384, 512), r(b, 0)
         msum([(y2, ID, r("rr", h)), (y2, R("BDW", 0, 128), r("win", h))])
         msum([(y1, ID, r(x, h)), (y1, R("BDW", 0, 128), r("win", h))])
         msum([(na, ID, r("Cm", h)), (na, r("sc", h), R("I4K")), (na, R("BDW", 256, 384), r("win", h))])
@@ -989,8 +1028,13 @@ def rank_program(g, core, T, topo):
     for a in range(0, M, 256):
         aff(R("ET", a, a + 256), R("KI", a, a + 256), [[0, 256]], A.is_ge, 0.0, 0, 0)
     for u in range(UNITS):
-        serve(u)
-        if u + 1 < UNITS:
+        if ASKS[u]:
+            serve(u)
+        if u == 0:
+            dma("y", T.BK[:, H:2 * H], T.BK[:, 0:H], [R("BK", 0, H), r("yl", 0)], [R("BK", H, 2 * H)])
+        if u == 1:
+            weights(2, [r("yl", 1)])
+        if u + 1 < UNITS and (EARLY or u % 2 == 0):
             bulk(u + 1)
         if early(u):
             mend(u)
@@ -998,16 +1042,21 @@ def rank_program(g, core, T, topo):
             verdicts(u)
             verdicts(u + 1)
         counts(u)
-        answer(u)
+        if ASKS[u]:
+            answer(u)
         decide(u)
-        if u + 2 < UNITS:
+        if u + 2 < UNITS and EARLY:
             head(u + 2)
+        elif u + 2 < UNITS and u % 2:
+            head(u + 1)
+            head(u + 2)
+            bulk(u + 1)
     xn, lvn = "x%d" % (STEPS % 2), "lv%d" % (STEPS % 2)
-    dma("y", T.ykids[:, M + L:W - 128], T.EN[:, 0:384], [R("EN", 0, 384)], [])
-    dma("y", T.ynodes[:, 0:640], T.XT[:, M:W - 128], [R("XT", M, W - 128)], [])
+    dma("y", T.ykids[:, M + L:W - L], T.EN[:, 0:L], [R("EN", 0, L)], [])
+    dma("y", T.ynodes[:, 0:2 * L], T.XT[:, M:W - L], [R("XT", M, W - L)], [])
     dma("y", T.ykids[:, 0:M + L], T.ET[:, 0:M + L], [R("ET", 0, M + L)], [])
-    dma("s", T.ykids[:, W - 128:W], T.EN[:, 384:512], [R("EN", 384, 512)], [])
-    dma("s", T.ynodes[:, 640:768], T.XT[:, W - 128:W], [R("XT", W - 128, W)], [])
+    dma("s", T.ykids[:, W - L:W], T.EN[:, L:2 * L], [R("EN", L, 2 * L)], [])
+    dma("s", T.ynodes[:, 2 * L:3 * L], T.XT[:, W - L:W], [R("XT", W - L, W)], [])
     dma("s", T.yspot[:], T.lvz[:], [R("lvz")], [])
     dma("s", T.ycand[:], T[xn][:], [R(xn)], [])
 

import math
from concourse.mybir import dt, AluOpType as A, ActivationFunctionType as F

M, L, STEPS, H = 1792, 256, 3, 4096
W = M + L * STEPS
UNITS = 2 * STEPS
NENG = 8
MK = 786432.0
B5 = float(2 ** 22)
FAR = float(2 ** 18)
VO = 2048
EPS = 2.0 ** -10
ROWS = ("hq", "hu", "hf")
FEW = ("sp", "sh", "c16", "SEL", "o16")

SB = {
    "XT": (W + 128, "bfloat16"), "BK": (2 * H + 16, "bfloat16"), "ET": (W + 384, "float32"), "EN": (2 * L, "float32"), "KI": (M, "int32"),
    "IDX": (VO, "float32"), "XW": (W + 384, "bfloat16"),
    "ONE": (128, "bfloat16"), "IDb": (128, "bfloat16"), "NIDb": (128, "bfloat16"), "IDf": (128, "float32"), "DB": (4096, "bfloat16"), "BG": (1024, "bfloat16"),
    "G8t": (8, "bfloat16"), "G8": (8, "bfloat16"), "G8x": (16, "bfloat16"), "GW": (32, "float32"), "GS": (32, "bfloat16"),
    "BW": (256 * (STEPS + 1), "bfloat16"), "NM": (512, "bfloat16"), "REP": (2048, "bfloat16"), "TRI": (128, "bfloat16"),
    "BDt": (128, "bfloat16"), "BD": (128, "bfloat16"), "BD2": (128, "bfloat16"), "BDW": (512, "bfloat16"),
    "Ck": (256, "bfloat16"), "pms": (128, "bfloat16"), "pm": (128, "bfloat16"),
    "CT": (128, "float16"), "CRK": (128, "bfloat16"), "C8": (128, "bfloat16"), "DK": (256, "bfloat16"), "DE": (512, "bfloat16"),
    "DN": (640, "bfloat16"), "IN": (L * STEPS, "float16"), "km": (256, "float32"), "ne": (128, "bfloat16"), "I4K": (128, "bfloat16"), "I8K": (128, "bfloat16"), "IK32": (128, "bfloat16"), "SI": (512, "bfloat16"),
    "II": (256, "bfloat16"), "PN": (128, "bfloat16"), "N4": (128, "float32"), "rm": (512, "bfloat16"), "trash": (16, "float32"), "RT": (256, "float32"),
    "wt": (2, "bfloat16"), "sp": (128, "int32"), "sh": (128, "float16"), "c16": (2048, "bfloat16"), "SEL": (136, "bfloat16"), "o16": (136, "bfloat16"),
    "x0": (256, "bfloat16"), "x1": (256, "bfloat16"), "lv0": (80, "float32"), "lv1": (80, "float32"),
    "lvu": (16, "uint16"), "lvz": (16, "float32"),
    "Ef": (256, "int32"), "c1": (256, "int32"), "Kb": (256, "bfloat16"), "Kc": (256, "bfloat16"), "CL": (256, "uint16"), "em": (256, "bfloat16"),
    "Cm": (256, "float16"), "vA": (256, "float16"), "xT": (256, "bfloat16"), "d0": (256, "bfloat16"),
    "XG": (4096, "bfloat16"), "DD": (4096, "float32"), "CMP": (4096, "bfloat16"),
    "EQ": (4096, "bfloat16"), "HL": (256, "uint16"), "ui": (768, "int32"), "um": (512, "int32"), "us": (256, "float32"), "hp": (256, "int32"),
    "hq": (68, "float16"), "hu": (68, "float16"), "hf": (68, "bfloat16"),
    "ruw": (512, "int32"), "ru": (32, "int32"), "rp": (16, "int32"),
    "fuw": (256, "int32"), "fu": (16, "int32"), "fp": (8, "int32"), "fl": (8, "uint16"),
    "fd": (128, "bfloat16"), "fD": (128, "bfloat16"), "fN": (128, "bfloat16"), "fC": (128, "bfloat16"),
    "fA": (128, "bfloat16"), "fo": (128, "bfloat16"), "fs": (128, "bfloat16"),
    "nw": (512, "bfloat16"), "sc": (256, "bfloat16"), "s1": (256, "bfloat16"), "s2": (256, "bfloat16"),
    "k1": (256, "float32"), "k2": (256, "float32"), "k3": (256, "int32"), "tw": (256, "float32"), "win": (256, "bfloat16"),
    "A1": (256, "float32"), "A2": (256, "float32"), "rr": (256, "bfloat16"), "bw": (256, "int32"),
    "ofu": (16, "uint16"), "e0": (80, "bfloat16"), "e1": (80, "int32"),
    "wl": (8 * STEPS, "bfloat16"), "zz": (256, "bfloat16"), "zo": (8 * UNITS, "uint16"), "zl": (8 * UNITS, "uint16"), "yo": (128 * UNITS, "bfloat16"), "yl": (128 * UNITS, "bfloat16"),
}
PS = ["dp0", "dp1", "HB", "m0", "BH0", "BH1", "m1", "m2"]
SCRATCH = {k: ("sbuf", [128, n, 8] if k in ROWS else [128, n], d) for k, (n, d) in SB.items()}
SCRATCH["EQ"] = ("sbuf", [128, 16, 256], "bfloat16")
for _n in PS:
    SCRATCH[_n] = ("psum", [128, 512], "float32")
NDMA = 14
SEMAPHORES = ["qv", "qs", "qt", "qg"] + ["D%d" % i for i in range(NDMA)] + [n + str(u) for u in range(UNITS) for n in ("zs", "za", "ys", "ya")] + [
    n + str(t) for t in range(STEPS) for n in ("ws", "wa")]

XGV = ((1, 3), (1,), (), (), (), ())
BKS = ((1,), (0, 1), (1,), (0, 1), (1,), (0,))
BKB = ("HB", "dp1", "HB", "dp1")
YB = ("HB", "m1")
FB = "m1"
WB = ("m2", "m2")
WO = 256
EARLY = True
SEEN = (0, 1)
ASKS = (1, 1, 1, 1, 1, 1)
CW = (512,) * 6
SUB = ("dp0", "dp1", "HB", "dp0")
TWICE = 2
SX = True

ORDER = {}
CYC = 0.83e-3
PECYC = 0.42e-3
WAKE = 0.22
ACT0 = 0.06
FLIGHT = 4.0
NEARBY = 3.9
FIRST = 2.4
DMA0 = 1.7
DMAROWS = 0.3
DMARATE = 2.9e5
TURN = 0.05
HEAT = 0.03
COOL = 0.15
NEAR = 0.3
STARTS = 5
ROUNDS = 1400
SWAPS = 70000
SEED = 2
SWAPS2 = 220000
HEAT2 = 0.02
LISTS = ("lvu", "CL", "HL", "zl", "fl", "ofu")
SLOW = 1.0
PAIR = 1.7
CASES = ((1.0, 0.22, 4.0, 0.35, 1.0, 1.0), (1.35, 0.22, 4.5, 0.35, 1.0, 1.05), (1.1, 0.16, 3.6, 0.3, 0.9, 0.88))


def overlap(a, b):
    return a[1] < b[2] and b[1] < a[2] and not (a[3] == b[3] and a[3] > 1 and (a[1] - b[1]) % a[3])


def schedule(nodes, spans):
    n = len(nodes)
    preds = [[] for _ in range(n)]
    hist, users = {}, {}
    for i in range(n):
        kind, q, fn, reads, writes, cost, sem = nodes[i]
        seen = {}
        for rs, w in ((reads, False), (writes, True)):
            for r in rs:
                for (j, rj, wj) in hist.get(r[0], ()):
                    if overlap(r, rj) and (w or wj):
                        seen[j] = seen.get(j, False) or q != "t" or nodes[j][1] != "t"
        for b in sorted(set(r[0] for r in reads + writes if r[0] in PS)):
            since = users.setdefault(b, [])
            for j in (since if spans.get(i) == "opens" else since[:1]):
                seen[j] = seen.get(j, False) or q != "t" or nodes[j][1] != "t"
            users[b] = [i] if i in spans else since + [i]
        preds[i] = list(seen.items())
        for rs, w in ((reads, False), (writes, True)):
            for r in rs:
                h = hist.get(r[0], [])
                if w and abs(r[3]) == 1:
                    h = [e for e in h if not (r[1] <= e[1][1] and e[1][2] <= r[2])]
                hist[r[0]] = h + [(i, r, w)]
    loads = [i for i in range(n) if nodes[i][0] == "d"]
    for a, b in zip(loads, loads[1:]):
        preds[b].append((a, None))
    above = []
    for i in range(n):
        far = 0
        for k, f in preds[i]:
            if f:
                far |= above[k]
        preds[i] = [(k, f) for k, f in preds[i] if nodes[k][0] != "c" or not far >> k & 1]
        for k, f in preds[i]:
            far |= above[k] | (1 << k if f else 0)
        above.append(far)
    succ = [[] for _ in range(n)]
    for i in range(n):
        for j, full in preds[i]:
            succ[j].append((i, full))
    banks = [[b for b in range(8) if any(r[0] == PS[b] for r in nodes[i][3] + nodes[i][4])] for i in range(n)]
    opener = min(i for i in range(n) if nodes[i][0] == "r")
    hold = [nodes[i][5] * SLOW if nodes[i][0] == "c" else (0.1 if nodes[i][0] == "d" else 0.8) for i in range(n)]
    last = [hold[i] if nodes[i][0] == "c" else nodes[i][5] + (FIRST if i == opener else 0.0) for i in range(n)]
    moved = DMA0
    for i in loads:
        if not nodes[i][3]:
            moved += last[i] - DMA0
            last[i] = moved
    last[loads[-5]] += sum(last[i] - DMA0 for i in loads[-4:])
    for i in loads[-4:]:
        last[i] += 1.5
    for i in loads[-7:-5]:
        last[i] += 16.5
    second = [i for i in range(n) if nodes[i][0] == "r"][1]
    last[second] += 17.0
    world = []
    listed = [nodes[i][0] == "c" and nodes[i][5] > 0.2 and any(r[0] in LISTS for r in nodes[i][3]) for i in range(n)]
    for slow, wake, flight, weight, late, jump in CASES:
        slow = [slow * jump if listed[i] else slow for i in range(n)]
        hd = [h * slow[i] if nodes[i][0] == "c" else h for i, h in enumerate(hold)]
        ls = [a * slow[i] if nodes[i][0] == "c" else (a * late if nodes[i][0] == "d" else a + (flight - FLIGHT) * (nodes[i][5] == FLIGHT)) for i, a in enumerate(last)]
        world.append((hd, ls, wake, [x for i in range(n) for x in (ls[i] + wake, 0.0, hd[i])], slow))
    ahead = [[(k, 3 * k + (0 if f else 1 if f is None else 2)) for k, f in preds[i]] for i in range(n)]
    behind = [[(k, 3 * i + (0 if f else 1 if f is None else 2)) for k, f in succ[i]] for i in range(n)]
    que = [8 + "vstgy".index(nodes[i][1]) for i in range(n)]
    both = [nodes[i][0] == "c" and bool(nodes[i][6]) for i in range(n)]
    free_ones = [i for i in range(n) if both[i]]
    ends = [i for i in range(n) if not succ[i] or nodes[i][0] == "d"]
    needs = [set(k for k, f in preds[i]) for i in range(n)]
    seed = [SEED]

    def draw():
        seed[0] = (seed[0] * 1103515245 + 12345) % 2 ** 31
        return seed[0] / 2.0 ** 31

    def flip(i):
        que[i] = 17 - que[i]
        c = SLOW * (nodes[i][5] if "vs"[que[i] - 8] == nodes[i][1] else nodes[i][6][2])
        hold[i] = last[i] = c
        for hd, ls, wake, lag, slow in world:
            hd[i] = ls[i] = lag[3 * i + 2] = c * slow[i]
            lag[3 * i] = c * slow[i] + wake

    def back_to(best):
        for i in free_ones:
            if que[i] != best[2][i]:
                flip(i)

    def place(rank, back):
        after, lag = ahead if back else behind, world[0][3]
        est = [last[i] - hold[i] for i in range(n)] if back else [0.0] * n
        at = [0.0] * n
        rank = list(rank)
        for i in (range(n - 1, -1, -1) if back else range(n)):
            e = rank[i] + 1e-6
            for k, x in after[i]:
                if rank[k] < e:
                    rank[k] = e
        busy = [[] for _ in range(13)]
        for e, i in sorted(zip(rank, range(n))):
            q, t, h = que[i], est[i], hold[i]
            own = busy[q]
            k = len(own)
            while k and own[k - 1][1] > t:
                k -= 1
            t0 = -1.0
            while t != t0:
                while k < len(own) and own[k][0] < t + h:
                    if own[k][1] > t:
                        t = own[k][1]
                    k += 1
                t0 = t
                for b in banks[i]:
                    uses = busy[b]
                    m = len(uses)
                    while m and uses[m - 1][0] > t - 1.5:
                        m -= 1
                    for x, y, w in uses[m:]:
                        if x - WAKE >= t + h:
                            break
                        if w != q and y + WAKE > t:
                            t = y + WAKE
            while k and own[k - 1][0] > t:
                k -= 1
            own.insert(k, (t, t + h))
            for b in banks[i]:
                uses = busy[b]
                m = len(uses)
                while m and uses[m - 1][0] > t:
                    m -= 1
                uses.insert(m, (t, t + h, q))
            if back:
                t += h
            at[i] = t
            for k, x in after[i]:
                e = t + lag[x] - hold[k] if back else t + lag[x]
                if e > est[k]:
                    est[k] = e
        return at

    def settle(rank):
        at = place(rank, False)
        rank = [-a for a in place([-(at[i] + last[i]) for i in range(n)], True)]
        at = place(rank, False)
        return max(at[i] + last[i] for i in ends), rank, at

    def shift(best):
        span, rank, at = settle(best[1])
        for _ in range(ROUNDS):
            lo, wide, far, part = -span * draw(), 3 + 17 * draw(), 0.5 * 8 ** draw(), 0.1 * 10 ** draw()
            turned = [i for i in free_ones if lo - wide <= rank[i] < lo and draw() < TURN]
            for i in turned:
                flip(i)
            s2, r2, at = settle([a + far * (draw() + draw() - 1) * 2 if lo - wide <= a < lo and draw() < part else a for a in rank])
            if s2 < best[0]:
                best = (s2, at, list(que))
            if s2 <= span + 0.15:
                span, rank = s2, r2
            else:
                for i in turned:
                    flip(i)
        back_to(best)
        return best

    def forward(order, lo, hi, case, at, state):
        hd, ls, wake, lag, slow = case
        free, bq, be, bo = state
        for p in range(lo, hi):
            i = order[p]
            q = que[i]
            t = free[q]
            for k, x in ahead[i]:
                e = at[k] + lag[x]
                if e > t:
                    t = e
            for b in banks[i]:
                e = bo[b] if bq[b] == q else be[b]
                if e > t:
                    t = e
            at[i] = t
            t += hd[i]
            free[q] = t
            for b in banks[i]:
                if bq[b] != q:
                    bo[b] = be[b]
                    bq[b] = q
                be[b] = t + wake

    def backward(order, lo, hi, case, to, state):
        hd, ls, wake, lag, slow = case
        free, bq, be, bo = state
        for p in range(hi - 1, lo - 1, -1):
            i = order[p]
            q = que[i]
            t = free[q]
            for b in banks[i]:
                e = bo[b] if bq[b] == q else be[b]
                if e > t:
                    t = e
            t += hd[i]
            if ls[i] > t:
                t = ls[i]
            for k, x in behind[i]:
                e = to[k] + lag[x]
                if e > t:
                    t = e
            to[i] = t
            free[q] = t
            for b in banks[i]:
                if bq[b] != q:
                    bo[b] = be[b]
                    bq[b] = q
                be[b] = t + wake

    def copy(s):
        return list(s[0]), list(s[1]), list(s[2]), list(s[3])

    where = [0] * n

    def sweep(order, case, rec, lo, hi):
        at, to, fs, bs = rec
        s, far = copy(fs[lo // 16]), hi
        for c in range(lo // 16, (n - 1) // 16 + 1):
            part = order[16 * c:16 * c + 16]
            was = [at[i] for i in part]
            forward(order, 16 * c, min(n, 16 * c + 16), case, at, s)
            for i, a in zip(part, was):
                if at[i] != a or 16 * c <= hi:
                    for k, x in behind[i]:
                        if where[k] > far:
                            far = where[k]
            if far < 16 * c + 16 and s == fs[c + 1]:
                break
            fs[c + 1] = copy(s)
        s, far = copy(bs[hi // 16 + 1]), lo
        for c in range(hi // 16, -1, -1):
            part = order[16 * c:16 * c + 16]
            was = [to[i] for i in part]
            backward(order, 16 * c, min(n, 16 * c + 16), case, to, s)
            for i, a in zip(part, was):
                if to[i] != a or 16 * c >= lo:
                    for k, x in ahead[i]:
                        if where[k] < far:
                            far = where[k]
            if far >= 16 * c and s == bs[c]:
                break
            bs[c] = copy(s)

    def swap(best, cases, swaps, heat):
        order = sorted(range(n), key=lambda i: (best[1][i], i))
        recs = []
        for case in cases:
            fresh = [([0.0] * 13, [-1] * 8, [-9.0] * 8, [-9.0] * 8) for _ in range(n // 16 + 2)]
            recs.append(([0.0] * n, [0.0] * n, fresh, list(fresh)))
            sweep(order, case, recs[-1], 0, n - 1)
        span = [max(r[1]) for r in recs]
        base = [CASES[c][3] * span[0] / span[c] / sum(e[3] for e in CASES[:len(cases)]) for c in range(len(cases))]
        best = (sum(w * s for w, s in zip(base, span)), list(recs[0][0]), list(que))
        for step in range(swaps):
            if step % 500 == 0:
                order.sort(key=lambda i: recs[0][0][i])
                for p, i in enumerate(order):
                    where[i] = p
                for case, rec in zip(cases, recs):
                    sweep(order, case, rec, 0, n - 1)
            c = int(draw() * len(cases))
            at, to, hd, wake = recs[c][0], recs[c][1], cases[c][0], cases[c][2]
            pb = int(draw() * n)
            b = order[pb]
            if at[b] + to[b] < span[c] - NEAR * draw() ** 2 - 1e-6:
                continue
            pa, t = pb - 1, at[b] - 1e-6
            while pa >= 0:
                a = order[pa]
                if que[a] == que[b]:
                    if at[a] + hd[a] < t:
                        pa = -1
                    break
                if banks[b] and at[a] + hd[a] + wake >= t and any(x in banks[a] for x in banks[b]):
                    break
                pa -= 1
            turn, x = None, draw()
            if both[b] and (pa < 0 or x < 0.2):
                turn, pa = b, pb
            elif pa < 0:
                continue
            elif both[a] and x < 0.4:
                turn, pb = a, pa
            if turn is not None:
                flip(turn)
                part = [turn]
            else:
                more = (0, 0, 0, 3, 10)[int(draw() * 5)]
                if draw() < 0.5:
                    pa = max(0, pa - more)
                    part, first = order[pa:pb + 1], {b}
                    for k in reversed(part):
                        if k in first:
                            first |= needs[k]
                    if a in first:
                        continue
                else:
                    pb = min(n - 1, pb + more)
                    part, late = order[pa:pb + 1], {a}
                    for k in part:
                        if needs[k] & late:
                            late.add(k)
                    if b in late:
                        continue
                    first = set(part) - late
                part = [k for k in part if k in first] + [k for k in part if k not in first]
            old = order[pa:pb + 1]
            lo, hi = pa // 16 * 16, min(n, pb // 16 * 16 + 16)
            bound = -heat * COOL ** (step / swaps) * math.log(draw() + 1e-9)
            order[pa:pb + 1] = part
            inside, loss = order[lo:hi], 0.0
            for case, rec, w in zip(cases, recs, base):
                at, to = rec[0], rec[1]
                keep = [at[k] for k in inside], [to[k] for k in inside]
                forward(order, lo, hi, case, at, copy(rec[2][lo // 16]))
                backward(order, lo, hi, case, to, copy(rec[3][(hi - 1) // 16 + 1]))
                loss += w * (max([at[k] + to[k] for k in inside]) - max([u + v for u, v in zip(*keep)]))
                for k, u, v in zip(inside, *keep):
                    at[k], to[k] = u, v
                if loss > bound + 1.0:
                    break
            if loss <= bound:
                for p in range(pa, pb + 1):
                    where[order[p]] = p
                for case, rec in zip(cases, recs):
                    sweep(order, case, rec, lo, hi - 1)
                span = [max(r[1]) for r in recs]
                now = sum(w * s for w, s in zip(base, span))
                if now < best[0]:
                    best = (now, list(recs[0][0]), list(que))
                    ORDER["spans"] = span
            else:
                order[pa:pb + 1] = old
                if turn is not None:
                    flip(turn)
        back_to(best)
        return best
    rank = [0.0] * n
    for i in range(n - 1, -1, -1):
        rank[i] = min([-last[i]] + [rank[k] - (0.0 if f is None else last[i] + WAKE if f else hold[i]) for k, f in succ[i]])
    start = (1e9, rank, list(que))
    tries = []
    for _ in range(STARTS):
        back_to(start)
        tries.append(swap(shift(start), world[:1], SWAPS, HEAT))
    ORDER["placed"] = [round(e[0], 1) for e in tries]
    best = min(tries)
    back_to(best)
    best = swap(best, world, SWAPS2, HEAT2)
    ORDER["plan"] = (best[:2], preds, hold, last, banks)
    ORDER["queues"] = ["vstgy"[q - 8] for q in que]
    return sorted(range(n), key=lambda i: (best[1][i], i))


def rank_program(g, core, T, topo):
    rank = T.rank_of(core)
    if rank is None:
        return
    queues = {"v": g.vector, "s": g.scalar, "t": g.tensor, "g": g, "y": g.sync}
    known = {q: {} for q in queues}
    count = {}
    clock = {}
    hist = {}

    def R(name, lo=0, hi=None, step=1):
        return (name, lo, SB[name][0] if hi is None and name in SB else (512 if hi is None else hi), step)

    def P(win, off):
        return ("ind", win, off)

    def ap(r):
        if r[0] == "ind":
            return ap(r[1]).indirect(ap(r[2]))
        name, lo, hi, step = r
        if name == "EQ":
            return T.EQ[:, lo // 256:hi // 256, 0:16] if hi - lo > 256 else T.EQ[:, lo // 256, lo % 256:hi - lo // 256 * 256]
        if name in FEW:
            return T[name][0:16, lo:hi:step]
        if name in ROWS:
            return T[name][:, lo:hi:step, :]
        if step == -1:
            return T[name][:, hi - 1:(lo - 1 if lo > 0 else None):-1]
        return T[name][:, lo:hi] if step == 1 else T[name][:, lo:hi:step]

    def flat(rs):
        out = []
        for r in rs:
            out += [r[1], r[2]] if r[0] == "ind" else [r]
        return out

    def need(q, ev):
        sem, val = ev
        k = known[q]
        if k.get(sem, 0) >= val:
            return
        queues[q].wait_ge(T.sem[sem], val)
        k[sem] = val
        for s2, v2 in clock.get(ev, {}).items():
            if k.get(s2, 0) < v2:
                k[s2] = v2

    def deps(q, me, reads, writes):
        evs = {}
        for rs, w in ((reads, False), (writes, True)):
            for r in rs:
                bank = r[0] in PS
                for (who, ev, lo, hi, wasw, step) in hist.get(r[0], ()):
                    over = lo < r[2] and r[1] < hi and not (step == r[3] and step > 1 and (lo - r[1]) % step)
                    if who == me:
                        if not (w or wasw) or not over or me == "t":
                            continue
                    elif not (bank or (over and (w or wasw))):
                        continue
                    if evs.get(ev[0], 0) < ev[1]:
                        evs[ev[0]] = ev[1]
        for sem in sorted(evs):
            need(q, (sem, evs[sem]))

    def note(me, ev, reads, writes):
        for rs, w in ((reads, False), (writes, True)):
            for r in rs:
                old = hist.get(r[0], [])
                if w and abs(r[3]) == 1:
                    old = [e for e in old if not (r[1] <= e[2] and e[3] <= r[2])]
                else:
                    old = [e for e in old if not (e[0] == me and e[2:] == (r[1], r[2], w, abs(r[3])))]
                hist[r[0]] = old + [(me, ev, r[1], r[2], w, abs(r[3]))]

    nodes = []
    spans = {}

    def emit(q, fn, reads, writes, cost):
        offs = [r[2] for r in writes if r[0] == "ind"]
        nodes.append(("c", q, [fn], flat(reads) + offs, [r[1] if r[0] == "ind" else r for r in writes], cost, None))

    nd = [0]

    def dma(q, out, in_, reads, writes, rows=128):
        sem = "D%d" % nd[0]
        nd[0] += 1
        r = (writes or reads)[0]
        size = rows * (r[2] - r[1]) * (4 if SB[r[0]][1] in ("float32", "int32") else 2)
        nodes.append(("d", q, lambda: queues[q].dma_start(out, in_), reads, writes, DMA0 + DMAROWS * rows / 128 + size / DMARATE, sem))

    def engines(a, b, what):
        e = topo.engines(T.cores[a], T.cores[b])
        return e[-NENG:] if what == "wl" else e

    def send(src, dst, peer, lsem, rsem, after=()):
        rid, pid = topo.addr(T.cores[peer])[:2]
        engs = engines(rank, peer, dst[0])

        def fn():
            g.remote_dma(ap(dst), ap(src), T.sem[rsem], T.sem[lsem], pid, rid, sum(1 << e for e in engs))
        nodes.append(("r", "g", fn, [src] + list(after), [dst],
                      NEARBY if topo.chip(core) == topo.chip(T.cores[peer]) else FLIGHT, (lsem, len(engs))))

    def finish():
        if "order" not in ORDER:
            ORDER["order"] = schedule(nodes, spans)
            ORDER["nodes"] = nodes
        for i in ORDER["order"]:
            kind, q, fn, reads, writes, cost, sem = nodes[i]
            if kind == "c":
                if ORDER["queues"][i] != q:
                    q, fn = sem[:2]
                deps(q, q, reads, writes)
                name = "q" + q
                for f in fn:
                    count[name] = count.get(name, 0) + 1
                    f().then_inc(T.sem[name], 1)
                ev, me = (name, count[name]), q
            elif kind == "d":
                deps(q, sem, reads, writes)
                fn().then_inc(T.sem[sem], 16)
                count[sem] = 16
                ev, me = (sem, 16), sem
            else:
                deps("g", sem[0], reads, [])
                fn()
                count[sem[0]] = sem[1]
                ev, me, writes = sem, sem[0], []
            clock[ev] = dict(known[q])
            note(me, ev, reads, writes)
        for sem in sorted(count):
            need("g", (sem, count[sem]))

    for buf, sem, wide, many, way in (("zl", "za", 8, UNITS, -1), ("yl", "ya", 128, UNITS, 1), ("wl", "wa", 8, STEPS, 1)):
        hist[buf] = []
        for u in range(many):
            k = ASKS[u] if many == UNITS else 1
            if k:
                count[sem + str(u)] = len(engines((rank + way * (1 + u * STEPS // many)) % 4, rank, buf))
                hist[buf].append(("remote", (sem + str(u), count[sem + str(u)]), wide * u, wide * (u + k), True, 1))

    def width(r):
        if r[0] == "EQ" and r[2] - r[1] > 256:
            return 128
        return 16 * width(r[2]) if r[0] == "ind" else -((r[1] - r[2]) // abs(r[3])) * (8 if r[0] in ROWS else 1)

    def dtype_of(r):
        return "float32" if r[0] in PS else SB[r[0]][1]

    def vcost(out, ins, kind):
        if out[0] == "ind":
            return 0.05 + 3.8 * width(out[2]) * 16 * CYC
        n = width(out)
        if any(r[0] == "ind" for r in ins):
            return 0.05 + (PAIR if kind == 2 else 1.56) * n * CYC
        if kind == 0:
            return ACT0 + n * CYC
        if kind == 2:
            c = n if any(r[0] in PS for r in ins) else 2 * n
        else:
            c = n
            if all(dtype_of(r) not in ("float32", "int32") for r in [out] + ins):
                c = n / 2
        return max(64, c) * CYC

    V, S, TE = g.vector, g.scalar, g.tensor

    def tt(out, a, b, op):
        emit("v", lambda: V.tensor_tensor(ap(out), ap(a), ap(b), op), [a, b], [out], vcost(out, [a, b], 2))

    def ts(out, a, s1, op0, s2=None, op1=None):
        rs = [a] + [s for s in (s1, s2) if not isinstance(s, (int, float)) and s is not None]
        c1 = s1 if isinstance(s1, (int, float)) else ap(s1)
        if op1 is None:
            emit("v", lambda: V.tensor_scalar(ap(out), ap(a), c1, None, op0), rs, [out], vcost(out, [a], 1))
        else:
            c2 = s2 if isinstance(s2, (int, float)) else ap(s2)
            emit("v", lambda: V.tensor_scalar(ap(out), ap(a), c1, c2, op0, op1), rs, [out], vcost(out, [a], 1))

    def cp(out, a):
        emit("v", lambda: V.tensor_copy(ap(out), ap(a)), [a], [out], vcost(out, [a], 1))

    def fill(out, c):
        emit("v", lambda: V.memset(ap(out), c), [], [out], vcost(out, [], 1))

    def scan(out, d0, d1, op0=A.mult, op1=A.max):
        emit("v", lambda: V.tensor_tensor_scan(ap(out), ap(d0), ap(d1), 0.0, op0, op1), [d0, d1], [out], vcost(out, [d0, d1], 1))

    def act(out, a, f, bias=0.0, scale=1.0):
        emit("s", lambda: S.activation(ap(out), ap(a), f, bias=bias, scale=scale), [a], [out], vcost(out, [a], 0))

    def either(second=False):
        b, a = nodes.pop(), nodes.pop()
        if second and a[4][0][0] in ("XG", "BK"):
            a, b = b, a
        nodes.append(a[:6] + ((b[1], b[2], b[5]),))

    def move(out, a, bias=0.0, relu=False, v=False):
        act(out, a, F.Relu if relu else (F.Identity if bias else F.Copy), bias)
        if relu:
            ts(out, a, bias, A.add, 0.0, A.max)
        elif bias:
            ts(out, a, bias, A.add)
        else:
            cp(out, a)
        either(v)
        if not SX and dtype_of(out) in ("int32", "uint16"):
            b = nodes.pop()
            nodes.append(b[:6] + (None,) if v else ("c", b[6][0], b[6][1], b[3], b[4], b[6][2], None))

    def under(out, a, c, v=True):
        act(out, a, F.Sigmoid, 256.0 * c - 128.0, -256.0)
        ts(out, a, float(c), A.is_lt)
        either(v)

    def reached(out, a, c, v=True):
        act(out, a, F.Sigmoid, 128.0 - 256.0 * c, 256.0)
        ts(out, a, float(c), A.is_ge)
        either(v)

    def mms(calls):
        fns, cost = [], 0.0
        for c in calls:
            fns.append(lambda c=c: TE.matmul(ap(c[0]), ap(c[1]), ap(c[2]), c[3], c[4]))
            cost += max(64, width(c[2])) * (4 if dtype_of(c[1]) == "float32" else 1) * PECYC
        nodes.append(("c", "t", fns, [c[1] for c in calls] + [c[2] for c in calls], [c[0] for c in calls], cost, None))

    def msum(terms, new=True, done=True):
        if not (new and done):
            spans[len(nodes)] = "opens" if new else "goes on"
        mms([(o, a, b, new and i == 0, done and i == len(terms) - 1) for i, (o, a, b) in enumerate(terms)])

    def mm(out, lhsT, rhs):
        msum([(out, lhsT, rhs)])

    def aff(out, a, pat, op, fl, base, cm):
        emit("g", lambda: g.affine_select(ap(out), ap(a), pat, op, fl, base, cm), [a], [out], 0.17 + 2 * width(out) * CYC)

    def iota(out, pat, base, cm):
        emit("g", lambda: g.iota(ap(out), pat, base, cm, allow_small_or_imprecise_dtypes=True), [], [out], 0.13 + 2 * width(out) * CYC)

    def gfill(name, lo, hi, c, step=0):
        for a in range(lo, hi, 384):
            b = min(hi, a + 384)
            iota(R(name, a, b), [[step, b - a]], c + step * (a - lo), 0)

    dma("s", T.wt[:], T.wts[:], [], [R("wt")])
    dma("y", T.sp[0:16, :], T.spot[:], [], [R("sp")], 16)
    dma("y", T.KI[:], T.kids[:], [], [R("KI")])
    dma("s", T.c16[0:16, :], T.cand[:], [], [R("c16")], 16)
    dma("y", T.XT[:, 0:M], T.nodes[:], [], [R("XT", 0, M)])
    dma("y", T.BK[:, 0:H], T.book[:], [], [R("BK", 0, H)])
    for a in range(0, H, 1024):
        move(R("BK", a, a + 1024), R("BK", a, a + 1024), 1.0, v=True)

    ID, NID, RM = R("IDb"), R("NIDb"), R("rm", 0, 128)
    fill(R("ONE"), 1.0)
    aff(ID, R("ONE"), [[-1, 128]], A.is_equal, 0.0, 0, 1)
    aff(R("G8t"), R("ONE", 0, 8), [[-16, 8]], A.is_ge, 0.0, 0, 1)
    aff(R("G8"), R("G8t"), [[16, 8]], A.is_ge, 0.0, 15, -1)
    aff(R("BDt"), R("ONE"), [[-16, 8], [0, 16]], A.is_ge, 0.0, 0, 1)
    aff(R("BD"), R("BDt"), [[16, 8], [0, 16]], A.is_ge, 0.0, 15, -1)
    iota(R("CRK"), [[0, 8], [-32, 16]], 528, 0)
    iota(R("II"), [[1, 256]], 0, 0)
    iota(R("trash"), [[16, 16]], W, 1)
    gfill("IDX", 0, VO, -VO, 1)
    if EARLY:
        gfill("XW", 0, M + L, 0)
    for name in ROWS:
        fill(R(name), 0.0)
    fill(R("BK", 2 * H, 2 * H + 16), 0.0)
    fill(R("e1"), 0)
    fill(R("e0"), 1.0)
    fill(R("e0", 0, 80, 5), 0.0)
    ts(NID, ID, -1.0, A.mult)
    for m in range(16):
        cp(R("REP", m, 2048, 16), ID)
    fill(R("o16"), 1.0)
    aff(R("SEL"), R("o16"), [[-1, 136]], A.is_equal, 0.0, 7, 8)
    cp(R("sh"), R("sp"))
    msum([(R("m1", 0, 16), R("SEL", 7 - j, 135 - j), R("sh", 16 * j, 16 * j + 16)) for j in range(8)])
    cp(R("lvu"), R("m1", 0, 16))
    cp(R("lv0", 4, 80, 5), R("m1", 0, 16))
    msum([(R("HB", 0, L), R("SEL", 7 - j, 135 - j), R("c16", L * j, L * j + L)) for j in range(8)])
    move(R("x0"), R("HB", 0, L))
    ts(R("GW", 16, 24), R("G8"), 1 / (1 + EPS), A.mult)
    ts(R("GW", 24, 32), R("G8"), 1 / EPS, A.mult)
    for j in range(2):
        ts(R("GW", 8 * j, 8 * j + 8), R("GW", 16, 24), R("wt", j, j + 1), A.mult)
        ts(R("BW", 128 * j, 128 * j + 128), R("BD"), R("wt", j, j + 1), A.mult)

    def weights(t, after):
        send(R("wt"), R("wl", 8 * t, 8 * t + 2), (rank - 1 - t) % 4, "ws%d" % t, "wa%d" % t, after)
        for j in range(2):
            ts(R("BW", 256 * t + 128 * j + 256, 256 * t + 128 * j + 384), R("BD"), R("wl", 8 * t + j, 8 * t + j + 1), A.mult)
    weights(0, [])
    weights(1, [])
    for name, lo, c in (("DK", 0, -2.0 ** -12), ("DK", 128, 2.0 ** -12), ("DE", 0, -256.0), ("DE", 128, -16384.0), ("DE", 256, -1.0), ("DE", 384, -1.0),
                        ("DN", 0, FAR), ("DN", 128, -FAR), ("DN", 256, -2 * B5), ("DN", 384, 2.0), ("DN", 512, 1 / B5), ("IDf", 0, B5),
                        ("I4K", 0, 4096.0 * 32), ("I8K", 0, 2.0 * H), ("IK32", 0, MK + 32 * 4096.0),
                        ("SI", 0, 1.0), ("SI", 128, -1.0), ("SI", 256, 65536 / B5), ("SI", 384, 1 / 32)):
        ts(R(name, lo, lo + 128), ID, c, A.mult)
    ts(R("CRK"), R("CRK"), 1 / B5, A.mult)
    for t in range(STEPS):
        ts(R("IN", L * t, L * t + L), R("II"), M + L * t - 2048.0, A.add)
    for name, lo, c in (("GS", 0, 1.0), ("GS", 8, -1.0), ("GS", 16, 65536 / B5), ("GS", 24, 1 / 32), ("G8x", 0, -float(VO)), ("G8x", 8, -1.0)):
        ts(R(name, lo, lo + 8), R("G8"), c, A.mult)
    tt(R("pms", 0, 64), R("IDb", 0, 64), R("IDb", 64, 128), A.add)
    tt(R("pms", 64, 96), R("pms", 0, 32), R("pms", 32, 64), A.add)
    tt(R("pm", 0, 16), R("pms", 64, 80), R("pms", 80, 96), A.add)
    for n in (16, 32, 64):
        cp(R("pm", n, 2 * n), R("pm", 0, n))
    for name, lo, a, b in (("CT", 0, -32768.0 - 383, 32768.0), ("N4", 0, 4 * FAR, 4095.0), ("NM", 0, B5, -B5), ("NM", 128, B5, -B5), ("NM", 256, B5, -B5), ("NM", 384, B5, -B5),
                           ("C8", 0, -8192.0, 16384.0 + VO), ("PN", 0, FAR / 2 + 2048, FAR / 2)):
        ts(R(name, lo, lo + 128), R("pm"), a, A.mult, b, A.add)
    iota(R("rm"), [[0, 32], [1, 16]], -1, 0)
    act(R("rm"), R("rm"), F.Sigmoid, 500.0, 1000.0)
    nodes[-1] = nodes[-1][:5] + (nodes[-1][5] + 1.3, None)
    fill(R("RT"), -1.0)
    cp(R("RT", 0, 256, 16), R("trash"))
    for name, lo, c in (("BD2", 0, 16384.0), ("BDW", 0, 256.0), ("BDW", 128, -256.0), ("BDW", 256, B5), ("BDW", 384, 2.0 ** 21)):
        ts(R(name, lo, lo + 128), R("BD"), c, A.mult)
    scan(R("Ck", 0, 128), RM, R("pm"), A.mult, A.add)
    ts(R("Ck", 128, 256), R("pm"), -1.5, A.mult)
    tt(R("Ck", 0, 128), R("Ck", 0, 128), R("Ck", 128, 256), A.add)
    tt(R("TRI"), R("BD2"), R("Ck", 0, 128), A.mult)

    def r(n, h, step=1):
        return R(n, 128 * h, 128 * h + 128, step)

    def l(n, h):
        return R(n, 8 * h, 8 * h + 8)

    def col(n, h, j=4):
        return R(n, 40 * h + j, 40 * h + 40, 5)

    def ends(n, h):
        return R(n, 128 * h + 15, 128 * h + 128, 16)

    def names(u):
        t, h = u // 2, u % 2
        return t, h, "x%d" % (t % 2), "x%d" % (1 - t % 2), "lv%d" % (t % 2), "lv%d" % (1 - t % 2)

    def early(u):
        return EARLY and u > 0 and u % 2 == 0

    def known_nodes(u):
        return M + (128 * max(u - 1, 0) if EARLY else L * (u // 2))

    def book(u):
        return R("BK", 0, 2 * H + 16 if u >= TWICE else H)

    def list_hash(u, src, w, b, ui, p, out):
        n = width(src)
        a, k, p = 512 - 2 * n, n // 16, R(p, 0, n // 16)
        msum([(R(b, a, 512), ID, R("NM", 0, 2 * n)), (R(b, a, a + n), R("BW", w, w + 128), src), (R(b, a + n, 512), R("BW", w + 128, w + 256), src)])
        scan(R(ui + "w", 0, 2 * n), R("rm", 0, 2 * n), R(b, a, 512))
        ts(R(ui, 0, 2 * k), R(ui + "w", 15, 2 * n, 16), 4095, A.bitwise_and)
        tt(p, R(ui, 0, k), R(ui, k, 2 * k), A.mult)
        ts(p, p, 5, A.arith_shift_right, 4095, A.bitwise_and)
        tt(p, p, R(ui, k, 2 * k), A.add)
        if u < TWICE:
            ts(p, p, 4095, A.bitwise_and)
        move(out, p, v=True)

    def part(n, u, wide=128, step=False):
        a = wide * (u % 2 if step else u)
        return R(n, a, a + wide * ASKS[u])

    def ask(u):
        t, h, x, xn, lv, lvn = names(u)
        tt(part("d0", u, 128, True), P(R("XT", 0, M + 256 * max(t - 1, 0)), part("lvu", u, 8, True)), part(x, u, 128, True), A.subtract)
        act(part("zz", u, 128, True), part("d0", u, 128, True), F.Abs)
        list_hash(u, part("zz", u, 128, True), 256 * (t + 1), "m0", "ru", "rp", part("zo", u, 8))
        send(part("zo", u, 8), part("zl", u, 8), (rank + 1 + t) % 4, "zs%d" % u, "za%d" % u)

    def slots(u):
        t, h = u // 2, u % 2
        move(r("Ef", h), P(R("KI") if t == 0 else R("ET", 0, M + 256 * (t - 1)), l("lvu", h)))
        ts(r("c1", h), r("Ef", h), 4095, A.bitwise_and)

    def marks(u):
        h = u % 2
        move(r("Kb", h), r("Ef", h), MK - 2047.5)
        reached(r("em", h), r("c1", h), 4095)
        if early(u):
            move(r("Cm", h), r("c1", h), -2048.0)
        else:
            move(r("Cm", h), r("CL", h), -2048.0)

    def head(u):
        t, h, x, xn, lv, lvn = names(u)
        slots(u)
        ts(r("CL", h), r("c1", h), known_nodes(u) - 1.0, A.min)
        mm(R("m0", 128, 256), r(x, h), ID)
        move(r("xT", h), R("m0", 128, 256))
        if ASKS[u] != 2:
            ask(u if ASKS[u] else u - 1)
        if not early(u):
            marks(u)
        move(r("vA", h), P(R("IDX"), l("lvu", h)))

    def bulk(u):
        h = u % 2
        for j in range(4 * h, 4 * h + 4):
            move(R("XG", 512 * j, 512 * j + 512), P(R("XT", 0, known_nodes(u)), R("CL", 32 * j, 32 * j + 32)), v=j % 4 in XGV[u])
        for j in range(4 * h, 4 * h + 4):
            b = R(SUB[(4 * u + j % 4) % len(SUB)])
            msum([(b, NID, R("XG", 512 * j, 512 * j + 512)), (b, r("xT", h), R("REP", 512 * (j % 4), 512 * (j % 4) + 512))])
            act(R("DD", 512 * j, 512 * j + 512), b, F.Abs, EPS, 1 + EPS)

    def verdicts(u):
        h = u % 2
        for e in range(2):
            a, c, o = 2048 * h + 1024 * e, 128 * h + 64 * e, 256 * e
            hb = "BH%d" % h
            mms([(R(hb, o + k, o + 256, 8), R("DD", a + k, a + 1024, 8), R("GW"), True, True) for k in range(8)])
            move(R("ui", 3 * c, 3 * c + 192), R(hb, o, o + 192))
            ts(R("um", 2 * c, 2 * c + 128), R("ui", 3 * c, 3 * c + 128), 4095, A.bitwise_and)
            hp, u2 = R("hp", c, c + 64), R("um", 2 * c + 64, 2 * c + 128)
            tt(hp, R("um", 2 * c, 2 * c + 64), u2, A.mult)
            ts(hp, hp, 5, A.arith_shift_right, 4095, A.bitwise_and)
            z = 17 * (2 * h + e)

            def turned(out, name, eye):
                return [(out, R(name, z + 1, z + 17), R(eye, 0, 128, 2)), (out, R(name, z, z + 16), R(eye, 1, 128, 2))]
            ht = R(hb, o + 64, o + 128)
            if u < TWICE:
                tt(hp, hp, u2, A.add)
                ts(hp, hp, 4095, A.bitwise_and)
                terms = []
            else:
                move(R("hu", z + 1, z + 17, 2), u2, -2048.0)
                terms = turned(ht, "hu", "IDb") + ([(ht, R("I8K"), R("fA", c, c + 64))] if early(u) else [])
            move(R("hq", z + 1, z + 17, 2), hp, -2048.0, v=True)
            msum(terms + turned(ht, "hq", "IDb"))
            if early(u):
                ts(R("HL", c, c + 64), ht, 4096.0, A.add, 2.0 * H, A.min)
            else:
                move(R("HL", c, c + 64), ht, 2048.0 if u < TWICE else 4096.0, v=True)
            for y in range(a, a + 1024, 512):
                column, j = P(book(u), R("HL", y // 16, y // 16 + 32)), y // 512 % 4
                if j in BKS[u]:
                    m = BKS[u].index(j) % 2
                    bg, b = R("BG", 512 * m, 512 * m + 512), R(BKB[2 * h + m])
                    for y1 in range(y, y + 512, 256):
                        aff(R("DB", y1, y1 + 256), R("DD", y1, y1 + 256), [[0, 256]], A.is_ge, 0.0, 0, 0)
                    move(bg, column)
                    msum([(b, NID, R("DB", y, y + 512)), (b, ID, bg)])
                    act(R("CMP", y, y + 512), b, F.Sigmoid, -512.0, 1024.0)
                    ts(R("CMP", y, y + 512), b, 0.5, A.is_gt)
                    either()
                else:
                    for y1 in range(y, y + 512, CW[u]):
                        tt(R("CMP", y1, y1 + CW[u]), P(book(u), R("HL", y1 // 16, (y1 + CW[u]) // 16)), R("DD", y1, y1 + CW[u]), A.is_gt)
            act(R("us", c, c + 64), R("ui", 3 * c + 128, 3 * c + 192), F.Identity, 7.0, 1 / EPS + 1)
            ts(R("us", c, c + 64), R("ui", 3 * c + 128, 3 * c + 192), 1 / EPS + 1, A.mult, 7.0, A.add)
            either()
            tt(R("hf", z + 1, z + 17, 2), R(hb, o + 192, o + 256), R("us", c, c + 64), A.is_lt)
            hi = R(hb, 192 + 64 * e, 256 + 64 * e)
            msum(turned(hi, "hf", "IK32") + ([(hi, ID, R("fo", c, c + 64))] if early(u) else []))
        tt(r("Kc", h), r("Kb", h), R(hb, 192, 320), A.max)

    def serve(u):
        move(part("yo", u), P(book(u), part("zl", u, 8)))
        send(part("yo", u), part("yl", u), (rank - 1 - u // 2) % 4, "ys%d" % u, "ya%d" % u)

    def answer(u):
        t, h, x, xn, lv, lvn = names(u)
        n = 128 * ASKS[u]
        a = R("m0", 0, 128) if n == 128 else R("m0", 256, 512)
        msum([(a, ID, part("yl", u)), (a, NID, part(x, u, 128, True))])
        act(part("rr", u, 128, True), a, F.Abs, -1.0)
        msum([(a, ID, R("NM", 0, n)), (a, R("BW", 0, 128), part("rr", u, 128, True))])
        scan(part("bw", u, 128, True), R("rm", 0, n), a)
        for j in (3, 4):
            ts(R("e1", 40 * h + j, 40 * (h + ASKS[u]), 5), R("bw", 128 * h + 15, 128 * h + n, 16), 1023, A.bitwise_and)

    def mend(u):
        t, h, x, xn, lv, lvn = names(u)
        tt(R("fd"), P(R("XW", 0, M + L), l("lvu", 0)), r(x, 0), A.subtract)
        act(R("fD"), R("fd"), F.Abs)
        ts(R("fN"), R("fd"), 0.0, A.is_gt, -4.5 / 16, A.add)
        list_hash(u, R("fD"), 0, "m2", "fu", "fp", R("fl"))
        tt(R("fC"), P(book(u), R("fl")), R("fD"), A.is_gt)
        slots(u)
        reached(R("fA"), r("c1", 0), M + 128 * (u - 1))
        marks(u)
        mm(R("m2", 128, 256), R("BDW", 384, 512), R("fN"))
        tt(R("fo"), R("fA"), R("m2", 128, 256), A.mult)

    def counts(u):
        h = u % 2
        b = "BH%d" % h
        msum([(R(b), r("em", h), R("DE")), (r(b, 1), ID, R("CT")), (r(b, 2), R("ONE"), R("CRK")), (r(b, 2), r("Cm", h), r("DN", 4))], True, False)
        msum([(R(b, 0, 256), r("Kc", h), R("DK"))], False, False)
        if early(u):
            mm(R(FB, 256, 384), R("BD"), R("fC"))
            tt(R("fs"), R("fA"), R(FB, 256, 384), A.mult)
        msum([(R(b, k, 512, 16), R("CMP", 2048 * h + k, 2048 * h + 2048, 16), R("GS")) for k in range(16)], False, not early(u))
        if early(u):
            msum([(R(b), R("fs"), R("SI"))], False)

    def decide(u):
        t, h, x, xn, lv, lvn = names(u)
        b = "BH%d" % h
        n0 = M + 128 * u
        nc, wm = r("nw", 2 * h), r("nw", 2 * h + 1)
        under(R("nw", 256 * h, 256 * h + 256), R(b, 0, 256), -191)
        mm(R(WB[h], WO, WO + 16), wm, R("G8x"))
        top = 128 * h + 128 if t in SEEN else 256
        for c in range(8 * h, 8 * h + 8):
            ts(R("EQ", 256 * c, 240 * c + top), R("vA", 16 * c, top), R(lv, 5 * c + 4, 5 * c + 5), A.subtract, R(WB[h], WO + c % 8, WO + 1 + c % 8), A.is_equal)
        move(col("e0", h, 1), R(WB[h], WO + 8, WO + 16))
        move(col("e1", h, 1), col(lv, h))
        tt(r("km", h), r(b, 2), nc, A.add)
        tt(r("sc", h), r(b, 3), nc, A.subtract)
        scan(r("k1", h), RM, r("km", h))
        scan(r("k2", h, -1), RM, r("k1", h, -1))
        scan(r("s1", h), RM, r("sc", h))
        scan(r("s2", h, -1), RM, r("s1", h, -1))
        ta = R("m1" if h == 0 or (EARLY and u + 1 < UNITS) else "dp0", 0, 128)

        def lower(c):
            lo = max(128 * h, 16 * c + 16)
            return (R(ta[0], lo - 128 * h, 128), R("BD2"), R("EQ", 240 * c + lo, 240 * c + 128 * h + 128))
        msum([(ta, ID, R("C8")), (ta, ID, r("vA", h))], True, False)
        if h == 1 and t in SEEN:
            tt(R("ne"), P(R("ET", 0, M + 256 * max(t - 1, 0)), l("lvu", 1)), r("Ef", 1), A.not_equal)
            msum([(ta, R("BD2"), R("ne"))], False, False)
        elif h == 1:
            msum([lower(c) for c in range(8)], False, False)
        msum([lower(c) for c in range(8 * h, 8 * h + 4)], False, False)
        msum([lower(c) for c in range(8 * h + 4, 8 * h + 7)] + [(ta, R("TRI"), R("EQ", 2048 * h, 2048 * h + 2048))], False)
        scan(r("tw", h), r("RT", h), ta, A.max, A.min)
        act(r("win", h), ta, F.Sigmoid, 4096.0, -1.0)
        ts(r("win", h), ta, 4096.0, A.is_lt)
        either()
        move(l("ofu", h), ends("tw", h), v=True)
        reached(col("e0", h, 3), ends("tw", h), W)
        if early(u + 1) and u + 1 < UNITS:
            cp(P(R("XW"), l("ofu", h)), r(x, h))
        st, kd, ra = r(b, 1), r(b, 2), r(b, 3)
        msum([(st, nc, r("DN", 0)), (st, wm, r("DN", 1))])
        msum([(kd, r("DN", 3), R("NM", 0, 128)), (kd, wm, r("DN", 2)), (kd, r("k2", h), R("IDf"))])
        tt(r("A2", h), r("Ef", h), st, A.min)
        scan(r("k3", h), RM, kd)
        msum([(ra, ID, r("IN", u)), (ra, ID, R("PN")), (ra, r("DN", 0), r("em", h)), (ra, nc, r("DN", 1)), (ra, wm, r("DN", 1)),
              (ra, r("s2", h), R("I4K"))])
        tt(r("A1", h), R("N4"), ra, A.min)
        tt(P(R("ET"), l("ofu", h)), r("A1", h), r("A2", h), A.max)
        ts(col("e1", h, 2), ends("k3", h), 4095, A.bitwise_and)
        scan(R(lvn, 40 * h, 40 * h + 40), R("e1", 40 * h, 40 * h + 40), R("e0", 40 * h, 40 * h + 40), A.subtract, A.mult)
        move(l("lvu" if t < STEPS - 1 else "lvz", h), col(lvn, h), v=True)
        yb = YB[h]
        na, y1, y2, y3 = R(yb, 128, 256), R(yb, 256, 384), R(yb, 384, 512), r(b, 0)
        msum([(y2, ID, r("rr", h)), (y2, R("BDW", 0, 128), r("win", h))])
        msum([(y1, ID, r(x, h)), (y1, R("BDW", 0, 128), r("win", h))])
        msum([(na, ID, r("Cm", h)), (na, r("sc", h), R("I4K")), (na, R("BDW", 256, 384), r("win", h))])
        move(R("XT", n0, n0 + 256), R(yb, 256, 512), -256.0, True, v=h == 1)
        ts(R("ET", n0, n0 + 128) if t == 0 else r("EN", u - 2), na, 2048.0 - B5, A.add, 4095.0, A.max)
        msum([(y3, ID, r(x, h)), (y3, R("BDW", 128, 256), r("win", h))])
        tt(r(xn, h), R("XT", n0 + 128, n0 + 256), y3, A.max)

    head(0)
    head(1)
    bulk(0)
    for a in range(0, M, 256):
        aff(R("ET", a, a + 256), R("KI", a, a + 256), [[0, 256]], A.is_ge, 0.0, 0, 0)
    for u in range(UNITS):
        if ASKS[u]:
            serve(u)
        if u == 0:
            dma("y", T.BK[:, H:2 * H], T.BK[:, 0:H], [R("BK", 0, H), r("yl", 0)], [R("BK", H, 2 * H)])
        if u == 1:
            weights(2, [r("yl", 1)])
        if u + 1 < UNITS and (EARLY or u % 2 == 0):
            bulk(u + 1)
        if early(u):
            mend(u)
        if u % 2 == 0:
            verdicts(u)
            verdicts(u + 1)
        counts(u)
        if ASKS[u]:
            answer(u)
        decide(u)
        if u + 2 < UNITS and EARLY:
            head(u + 2)
        elif u + 2 < UNITS and u % 2:
            head(u + 1)
            head(u + 2)
            bulk(u + 1)
    xn, lvn = "x%d" % (STEPS % 2), "lv%d" % (STEPS % 2)
    dma("y", T.ykids[:, M + L:W - L], T.EN[:, 0:L], [R("EN", 0, L)], [])
    dma("y", T.ynodes[:, 0:2 * L], T.XT[:, M:W - L], [R("XT", M, W - L)], [])
    dma("y", T.ykids[:, 0:M + L], T.ET[:, 0:M + L], [R("ET", 0, M + L)], [])
    dma("s", T.ykids[:, W - L:W], T.EN[:, L:2 * L], [R("EN", L, 2 * L)], [])
    dma("s", T.ynodes[:, 2 * L:3 * L], T.XT[:, W - L:W], [R("XT", W - L, W)], [])
    dma("s", T.yspot[:], T.lvz[:], [R("lvz")], [])
    dma("s", T.ycand[:], T[xn][:], [R(xn)], [])

    finish()
